import numpy as np
import ml_dtypes


def mxq(x, axis, fmt="e4m3"):
    dtype, down = {"e4m3": (ml_dtypes.float8_e4m3fn, 7), "e5m2": (ml_dtypes.float8_e5m2, 14)}[fmt]
    v = np.moveaxis(np.asarray(x, np.float32).astype(ml_dtypes.bfloat16).astype(np.float64), axis, -1)
    blocks = v.reshape(v.shape[:-1] + (-1, 32))
    amax = np.abs(blocks).max(-1, keepdims=True)
    byte = np.maximum(np.where(amax > 0, np.frexp(amax)[1] - 1 + 127, 0) - down, 1)
    scale = np.exp2(byte - 127.0)
    codes = (blocks / scale).astype(np.float32).astype(dtype).astype(np.float64)
    return np.moveaxis((codes * scale).reshape(v.shape), -1, axis)


WIDE = False


def mx_kscale(k):
    if not WIDE:
        return np.ones(k)
    levels = np.array([10, -10, 5, -5, 0])
    if k % 512:
        return np.exp2(np.random.permutation(np.resize(levels, k // 32))).repeat(32)
    a = np.empty((k // 512, 16))
    for p in range(k // 512):
        a[p, :8] = np.random.permutation(np.resize(levels, 8))
        for g in range(8):
            far = levels[np.abs(levels - a[p, g]) >= 10]
            a[p, g + 8] = far[np.random.randint(len(far))]
    return np.exp2(a.ravel()).repeat(32)


def f64(x):
    return np.asarray(x).astype(np.float64)


def striped(idx):
    return np.tile(idx.reshape(-1, 16).T, (8, 1)).astype(np.uint16)


def unstriped(offs):
    return offs[:16].T.reshape(-1).astype(np.int64)


E2M1 = np.array([0.0, 0.5, 1.0, 1.5, 2.0, 3.0, 4.0, 6.0, -0.0, -0.5, -1.0, -1.5, -2.0, -3.0, -4.0, -6.0])


def pack_weight(w, fmt):
    k, n = w.shape
    w = f64(np.asarray(w, np.float32).astype(ml_dtypes.bfloat16)).reshape(k // 32, 32, n)
    amax = np.abs(w).max(1)
    if fmt == "e4m3":
        byte = np.frexp(amax)[1] - 1 + 127 - 7
    else:
        mant, ex = np.frexp(amax / 6.0)
        byte = np.where(mant > 0.5, ex, ex - 1) + 127
    byte = np.clip(np.where(amax > 0, byte, 1), 1, 254)
    scaled = (w * np.exp2(127.0 - byte)[:, None, :]).reshape(k, n).astype(np.float32)
    by_word = np.ascontiguousarray(scaled.reshape(k // 512, 128, 4, n).transpose(0, 1, 3, 2))
    if fmt == "e4m3":
        words = by_word.astype(ml_dtypes.float8_e4m3fn).view(np.uint8)
    else:
        c = by_word.astype(ml_dtypes.float4_e2m1fn).view(np.uint8) & 0xF
        words = (c[..., 0::2] | (c[..., 1::2] << 4)).reshape(k // 512, 128, 2 * n)
    return np.ascontiguousarray(words), np.ascontiguousarray(byte.astype(np.uint8).reshape(k // 512, 16, n))


def unpack_weight(words, scales, fmt):
    g, _, n = scales.shape
    words = np.ascontiguousarray(words).reshape(g, 128, n, -1)
    if fmt == "e4m3":
        vals = words.view(ml_dtypes.float8_e4m3fn).astype(np.float64)
    else:
        nib = np.empty((g, 128, n, 4), np.uint8)
        nib[..., 0::2] = words & 0xF
        nib[..., 1::2] = words >> 4
        vals = E2M1[nib]
    vals = vals * np.repeat(np.exp2(scales.astype(np.float64) - 127.0), 8, axis=1)[..., None]
    return vals.transpose(0, 1, 3, 2).reshape(g * 512, n)


def gelu(v):
    return 0.5 * v * (1.0 + np.tanh(np.sqrt(2.0 / np.pi) * (v + 0.044715 * v**3)))


K, H, N, T, T2, S = 512, 1024, 768, 2048, 2048, 1024

def setup_inputs():
    n = np.random.standard_normal
    s = mx_kscale(K)[:, None]
    u = mx_kscale(H)[:, None]
    tab_words, tab_scales = pack_weight(n((K, T)) * s, "e4m3")
    wc_words, wc_scales = pack_weight(n((K, H)) / np.sqrt(K) / s, "e2m1")
    wf_words, wf_scales = pack_weight(n((H, N)) / np.sqrt(H) / u, "e4m3")
    xT = (np.round(16 * n((K, T2))) / 16 * s).astype(np.float32)
    ws = (n((K, H)) / np.sqrt(2 * K) / s).astype(np.float32)
    gain = (np.exp(0.3 * n(H)) * u[:, 0]).astype(np.float32)
    drag = (0.5 * n((N, S))).astype(np.float32)
    perm = np.random.permutation(T2)
    return {"tab_words": tab_words, "tab_scales": tab_scales, "xT": xT,
            "offs": striped(np.random.permutation(T)[:S]),
            "offs2": striped(perm[:S]), "offs3": striped(perm[T2 - S:]),
            "wc_words": wc_words, "wc_scales": wc_scales, "ws": ws,
            "gain": gain, "wf_words": wf_words, "wf_scales": wf_scales,
            "drag": drag}

def reference(tab_words, tab_scales, xT, offs, offs2, offs3, wc_words, wc_scales,
              ws, gain, wf_words, wf_scales, drag):
    v = unpack_weight(tab_words, tab_scales, "e4m3")[:, unstriped(offs)]
    x = f64(xT)[:, unstriped(offs2)] - f64(xT)[:, unstriped(offs3)]
    wc = unpack_weight(wc_words, wc_scales, "e2m1")
    wf = unpack_weight(wf_words, wf_scales, "e4m3")
    c = wc.T @ v
    d = mxq(f64(ws), 0, "e4m3").T @ mxq(x, 0, "e4m3")
    soft = np.sqrt(1.0 + (np.square(c) + np.square(d)))
    h = f64(gain)[:, None] * c / soft
    y = wf.T @ mxq(h, 0, "e4m3")
    return y + f64(drag)

@@ -1,0 +1,298 @@
+from contextlib import ExitStack
+
+import concourse.mybir as mybir
+
+K, H, N, T, S = 512, 1024, 768, 2048, 1024
+FLOPS = 2 * S * (2 * K * H + H * N)
+
+F32 = mybir.dt.float32
+BF16 = mybir.dt.bfloat16
+I32 = mybir.dt.int32
+U32 = mybir.dt.uint32
+U16 = mybir.dt.uint16
+U8 = mybir.dt.uint8
+FP8X4 = mybir.dt.float8_e4m3fn_x4
+FP4X4 = mybir.dt.float4_e2m1fn_x4
+ACT = mybir.ActivationFunctionType
+ALU = mybir.AluOpType
+
+P = 128
+PACK = 4
+PASS = P * PACK
+H_PASSES = H // PASS
+CHUNK = 256
+CHUNKS = S // CHUNK
+LIST_COLS = CHUNK // 16
+BANK = 512
+PER_BANK = BANK // CHUNK
+N_TILES = N // P
+RUN = 4
+WIDE_PLANES = 2
+LAG = 2
+
+
+def tile_list_grain_sheath_forces_kernel(
+    tc, tab_words, tab_scales, xT, offs, offs2, offs3, wc_words, wc_scales,
+    ws, gain, wf_words, wf_scales, drag, out,
+):
+    nc = tc.nc
+    with ExitStack() as ctx:
+        keep = ctx.enter_context(tc.tile_pool(name="keep", bufs=1))
+        ring = ctx.enter_context(tc.tile_pool(name="ring", bufs=2))
+        psum = ctx.enter_context(tc.psum_pool(name="psum", bufs=1))
+
+        def held(name, shape, dtype):
+            return keep.tile(shape, dtype, name=name, align_bytes=64)
+
+        idx_tab = keep.tile([P, S // 16], U16, name="idx_tab")
+        idx_a = keep.tile([P, S // 16], U16, name="idx_a")
+        idx_b = keep.tile([P, S // 16], U16, name="idx_b")
+        tab_w = held("tab_w", [P, T], U32)
+        tab_s = held("tab_s", [P, T], U8)
+        wc_w_raw = held("wc_w_raw", [P, 2 * H], U8)
+        wc_s_raw = held("wc_s_raw", [P, H], U8)
+        wc_w = held("wc_w", [P, 2 * H], U8)
+        wc_s = held("wc_s", [P, H], U8)
+        wf_w = held("wf_w", [P, H_PASSES, N], U32)
+        wf_s = held("wf_s", [P, H_PASSES, N], U8)
+        planes = [held("plane%d" % t, [P, T], F32) for t in range(PACK)]
+        ws_raw = [held("ws_raw%d" % a, [P, PACK, PASS], F32) for a in range(H_PASSES)]
+        ws_w = [held("ws_w%d" % a, [P, PASS], U32) for a in range(H_PASSES)]
+        ws_s = [held("ws_s%d" % a, [P, PASS], U8) for a in range(H_PASSES)]
+        gains = held("gains", [P, H_PASSES, PACK], F32)
+        forces = [held("forces%d" % k, [P, N_TILES, CHUNK], F32)[:] for k in range(CHUNKS - H_PASSES)]
+        for a in range(H_PASSES):
+            flat = ws_raw[a][:].rearrange("p t c -> p (t c)")
+            forces.append(flat[:, 0 : N_TILES * CHUNK].rearrange("p (m j) -> p m j", j=CHUNK))
+        sep = held("sep", [P, PACK, S], F32)
+        sep_grouped = [held("sep_grouped%d" % k, [P, CHUNK * PACK], BF16) for k in range(CHUNKS)]
+
+        for plane in (tab_s, wc_s_raw):
+            nc.vector.memset(plane[:].bitcast(I32), 0)
+        nc.vector.memset(wf_s[:].rearrange("p a n -> p (a n)").bitcast(I32), 0)
+
+        def load_scale_rows(plane, rows):
+            for q in range(4):
+                nc.scalar.dma_start(plane[32 * q : 32 * q + 4, :].bitcast(I32), rows[4 * q : 4 * q + 4, :].bitcast(I32))
+
+        x_rows = xT.rearrange("(p t) c -> p t c", t=PACK)
+        ws_rows = ws.rearrange("(p t) c -> p t c", t=PACK)
+        drag_rows = drag.rearrange("(m p) j -> p m j", p=P)
+        out_rows = out.rearrange("(m p) j -> p m j", p=P)
+
+        nc.sync.dma_start(idx_tab[:], offs)
+        nc.sync.dma_start(wc_w_raw[:], wc_words[0])
+        nc.sync.dma_start(tab_w[:].bitcast(I32), tab_words[0].rearrange("p n t -> p (n t)").bitcast(I32))
+        load_scale_rows(tab_s, tab_scales[0])
+        load_scale_rows(wc_s_raw, wc_scales[0])
+        nc.scalar.dma_start(gains[:], gain.rearrange("(a p t) -> p a t", p=P, t=PACK))
+        nc.sync.dma_start(ws_raw[0][:], ws_rows[:, :, 0:PASS])
+        nc.sync.dma_start(idx_b[:], offs3)
+        nc.sync.dma_start(planes[0][:], x_rows[:, 0, :])
+        nc.sync.dma_start(idx_a[:], offs2)
+        nc.sync.dma_start(ws_raw[1][:], ws_rows[:, :, PASS : 2 * PASS])
+        for t in range(1, PACK):
+            nc.sync.dma_start(planes[t][:], x_rows[:, t, :])
+        nc.sync.dma_start(
+            wf_w[:].bitcast(I32), wf_words.rearrange("a p n t -> p a (n t)").bitcast(I32)
+        )
+        for q in range(4):
+            nc.sync.dma_start(
+                wf_s[32 * q : 32 * q + 4, :, :].bitcast(I32),
+                wf_scales[:, 4 * q : 4 * q + 4, :].rearrange("a r n -> r a n").bitcast(I32),
+            )
+        def load_drag(k):
+            nc.sync.dma_start(forces[k], drag_rows[:, :, k * CHUNK : (k + 1) * CHUNK])
+
+        for k in range(CHUNKS - H_PASSES):
+            load_drag(k)
+
+        nc.vector.tensor_copy(
+            wc_w[:].bitcast(U16).rearrange("p (a t m) -> p a t m", a=H_PASSES, t=PACK),
+            wc_w_raw[:].bitcast(U16).rearrange("p (a m t) -> p a t m", a=H_PASSES, t=PACK),
+        )
+        nc.vector.tensor_copy(
+            wc_s[:].rearrange("p (a t m) -> p a t m", a=H_PASSES, t=PACK),
+            wc_s_raw[:].rearrange("p (a m t) -> p a t m", a=H_PASSES, t=PACK),
+        )
+
+        def quantise_ws(a):
+            grouped = ring.tile([P, PACK, P, PACK], BF16, name="ws_grouped", align_bytes=64)
+            nc.scalar.copy(
+                grouped[:].rearrange("p t (g i) j -> p g j i t", i=2),
+                ws_raw[a][:].rearrange("p j (g i t) -> p g j i t", i=2, t=PACK),
+            )
+            nc.vector.quantize_mx(
+                out=ws_w[a][:].bitcast(FP8X4), scales=ws_s[a][:],
+                in_=grouped[:].rearrange("p t m j -> p (t m j)"),
+            )
+            load_drag(CHUNKS - H_PASSES + a)
+
+        soft = {}
+        gained = {}
+
+        species = {}
+
+        def gather_species(k):
+            cols = slice(k * LIST_COLS, (k + 1) * LIST_COLS)
+            v_w = held("v_w%d" % k, [P, CHUNK], U32)
+            v_s = held("v_s%d" % k, [P, CHUNK], U8)
+            nc.vector.tensor_copy(v_w[:], tab_w[:].indirect(idx_tab[:, cols]))
+            nc.vector.tensor_copy(v_s[:], tab_s[:].indirect(idx_tab[:, cols]))
+            species[k] = (v_w, v_s)
+
+        def species_response(k):
+            v_w, v_s = species[k]
+            for a in range(H_PASSES):
+                soft[k, a] = held("soft%d_%d" % (k, a), [P, PACK, CHUNK], F32)
+                gained[k, a] = held("gained%d_%d" % (k, a), [P, PACK, CHUNK], F32)
+                for t0 in range(0, PACK, PER_BANK):
+                    c = psum.tile([P, PER_BANK, CHUNK], F32, name="c_or_y", bufs=5)
+                    for u in range(PER_BANK):
+                        col = a * PASS + (t0 + u) * P
+                        nc.tensor.matmul_mx(
+                            out=c[:, u, :],
+                            lhsT=wc_w[:, 2 * col : 2 * (col + P)].bitcast(FP4X4),
+                            lhsT_scale=wc_s[:, col : col + P],
+                            rhs=v_w[:].bitcast(FP8X4), rhs_scale=v_s[:],
+                            start=True, stop=True,
+                        )
+                    nc.scalar.activation(soft[k, a][:, t0 : t0 + PER_BANK, :], c[:], ACT.Square)
+                    for u in range(PER_BANK):
+                        t = t0 + u
+                        nc.scalar.activation(
+                            gained[k, a][:, t, :], c[:, u, :], ACT.Copy, scale=gains[:, a, t : t + 1]
+                        )
+
+        def gather_separation(t, first, count, second):
+            cols = slice(first // 16, (first + count) // 16)
+            nc.vector.tensor_copy(second, planes[t][:].indirect(idx_b[:, cols]))
+            nc.vector.tensor_tensor(
+                sep[:, t, first : first + count], planes[t][:].indirect(idx_a[:, cols]), second, ALU.subtract
+            )
+
+        def gather_plane(t):
+            for first in range(0, S, 2 * CHUNK):
+                second = ring.tile([P, 2 * CHUNK], F32, name="second", bufs=3)
+                gather_separation(t, first, 2 * CHUNK, second[:])
+
+        def gather_last_planes(k):
+            for t in range(WIDE_PLANES, PACK):
+                if k < LAG:
+                    second = ring.tile([P, CHUNK], F32, name="second", bufs=3)[:]
+                else:
+                    u = t - WIDE_PLANES
+                    second = sep_grouped[k - LAG][:].bitcast(F32)[:, u * CHUNK : (u + 1) * CHUNK]
+                gather_separation(t, k * CHUNK, CHUNK, second)
+
+        separations = {}
+        d_squares = {}
+        interactions = {}
+
+        def quantise_separation(k):
+            nc.scalar.copy(
+                sep_grouped[k][:].rearrange("p (g i t) -> p g t i", i=RUN, t=PACK),
+                sep[:, :, k * CHUNK : (k + 1) * CHUNK].rearrange("p t (g i) -> p g t i", i=RUN),
+            )
+            x_w = held("x_w%d" % k, [P, CHUNK], U32)
+            x_s = held("x_s%d" % k, [P, CHUNK], U8)
+            nc.vector.quantize_mx(out=x_w[:].bitcast(FP8X4), scales=x_s[:], in_=sep_grouped[k][:])
+            separations[k] = (x_w, x_s)
+
+        def separation_response(k):
+            x_w, x_s = separations[k]
+            for a in range(H_PASSES):
+                d_sq = ring.tile([P, PACK, CHUNK], F32, name="d_sq", bufs=4)
+                for t0 in range(0, PACK, PER_BANK):
+                    d = psum.tile([P, PER_BANK, CHUNK], F32, name="d", bufs=3)
+                    for u in range(PER_BANK):
+                        col = (t0 + u) * P
+                        nc.tensor.matmul_mx(
+                            out=d[:, u, :],
+                            lhsT=ws_w[a][:, col : col + P].bitcast(FP8X4),
+                            lhsT_scale=ws_s[a][:, col : col + P],
+                            rhs=x_w[:].bitcast(FP8X4), rhs_scale=x_s[:],
+                            start=True, stop=True,
+                        )
+                    nc.scalar.activation(d_sq[:, t0 : t0 + PER_BANK, :], d[:], ACT.Square)
+                d_squares[k, a] = d_sq
+
+        def soften(k):
+            for a in range(H_PASSES):
+                nc.vector.tensor_tensor(soft[k, a][:], soft[k, a][:], d_squares[k, a][:], ALU.add)
+                nc.scalar.activation(soft[k, a][:], soft[k, a][:], ACT.Abs_reciprocal_sqrt, bias=1.0)
+
+        def quantise_interaction(k):
+            h_w = []
+            h_s = []
+            for a in range(H_PASSES):
+                grouped = ring.tile([P, CHUNK, PACK], BF16, name="h_grouped", align_bytes=64)
+                nc.vector.tensor_tensor(
+                    grouped[:].rearrange("p (g i) t -> p g t i", i=RUN),
+                    gained[k, a][:].rearrange("p t (g i) -> p g t i", i=RUN),
+                    soft[k, a][:].rearrange("p t (g i) -> p g t i", i=RUN),
+                    ALU.mult,
+                )
+                words = ring.tile([P, CHUNK], U32, name="h_w", align_bytes=64, bufs=4)
+                scales = ring.tile([P, CHUNK], U8, name="h_s", align_bytes=64, bufs=4)
+                nc.vector.quantize_mx(
+                    out=words[:].bitcast(FP8X4), scales=scales[:], in_=grouped[:].rearrange("p n t -> p (n t)")
+                )
+                h_w.append(words)
+                h_s.append(scales)
+            interactions[k] = (h_w, h_s)
+
+        def forces_of(k):
+            h_w, h_s = interactions[k]
+            for m0 in range(0, N_TILES, PER_BANK):
+                y = psum.tile([P, PER_BANK, CHUNK], F32, name="c_or_y", bufs=5)
+                for u in range(PER_BANK):
+                    col = (m0 + u) * P
+                    for a in range(H_PASSES):
+                        nc.tensor.matmul_mx(
+                            out=y[:, u, :],
+                            lhsT=wf_w[:, a, col : col + P].bitcast(FP8X4),
+                            lhsT_scale=wf_s[:, a, col : col + P],
+                            rhs=h_w[a][:].bitcast(FP8X4), rhs_scale=h_s[a][:],
+                            start=(a == 0), stop=(a == H_PASSES - 1),
+                        )
+                rows = forces[k][:, m0 : m0 + PER_BANK, :]
+                nc.vector.tensor_tensor(rows, y[:], rows, ALU.add)
+                nc.sync.dma_start(out_rows[:, m0 : m0 + PER_BANK, k * CHUNK : (k + 1) * CHUNK], rows)
+
+        gather_species(0)
+        gather_species(1)
+        gather_species(2)
+        gather_species(3)
+        quantise_ws(0)
+        species_response(0)
+        quantise_ws(1)
+        species_response(1)
+        gather_plane(0)
+        gather_plane(1)
+        gather_last_planes(0)
+        quantise_separation(0)
+        gather_last_planes(1)
+        quantise_separation(1)
+        separation_response(0)
+        gather_last_planes(2)
+        quantise_separation(2)
+        separation_response(1)
+        species_response(2)
+        gather_last_planes(3)
+        quantise_separation(3)
+        soften(0)
+        separation_response(2)
+        soften(1)
+        species_response(3)
+        quantise_interaction(0)
+        separation_response(3)
+        soften(2)
+        quantise_interaction(1)
+        forces_of(0)
+        soften(3)
+        quantise_interaction(2)
+        forces_of(1)
+        quantise_interaction(3)
+        forces_of(2)
+        forces_of(3)

@@ -26,7 +26,7 @@ LIST_COLS = CHUNK // 16
 BANK = 512
 PER_BANK = BANK // CHUNK
 N_TILES = N // P
-RUN = 4
+RUN = 2
 WIDE_PLANES = 2
 LAG = 2
 
@@ -66,6 +66,9 @@ def tile_list_grain_sheath_forces_kernel(
             forces.append(flat[:, 0 : N_TILES * CHUNK].rearrange("p (m j) -> p m j", j=CHUNK))
         sep = held("sep", [P, PACK, S], F32)
         sep_grouped = [held("sep_grouped%d" % k, [P, CHUNK * PACK], BF16) for k in range(CHUNKS)]
+        warm = held("warm", [P, 2], F32)
+        nc.gpsimd.memset(warm[:, 0:1], 1.0)
+        nc.scalar.activation(warm[:, 1:2], warm[:, 0:1], ACT.Abs_reciprocal_sqrt)
 
         for plane in (tab_s, wc_s_raw):
             nc.vector.memset(plane[:].bitcast(I32), 0)
@@ -268,6 +271,7 @@ def tile_list_grain_sheath_forces_kernel(
         species_response(0)
         quantise_ws(1)
         species_response(1)
+        species_response(2)
         gather_plane(0)
         gather_plane(1)
         gather_last_planes(0)
@@ -278,7 +282,6 @@ def tile_list_grain_sheath_forces_kernel(
         gather_last_planes(2)
         quantise_separation(2)
         separation_response(1)
-        species_response(2)
         gather_last_planes(3)
         quantise_separation(3)
         soften(0)

@@ -1,6 +1,7 @@
 from contextlib import ExitStack
 
 import concourse.mybir as mybir
+from concourse.masks import make_identity
 
 K, H, N, T, S = 512, 1024, 768, 2048, 1024
 FLOPS = 2 * S * (2 * K * H + H * N)
@@ -29,6 +30,7 @@ N_TILES = N // P
 RUN = 2
 WIDE_PLANES = 2
 LAG = 2
+TURNED = 3
 
 
 def tile_list_grain_sheath_forces_kernel(
@@ -64,19 +66,21 @@ def tile_list_grain_sheath_forces_kernel(
         for a in range(H_PASSES):
             flat = ws_raw[a][:].rearrange("p t c -> p (t c)")
             forces.append(flat[:, 0 : N_TILES * CHUNK].rearrange("p (m j) -> p m j", j=CHUNK))
-        sep = held("sep", [P, PACK, S], F32)
+        sep = [held("sep%d" % k, [P, PACK, CHUNK], F32) for k in range(CHUNKS)]
         sep_grouped = [held("sep_grouped%d" % k, [P, CHUNK * PACK], BF16) for k in range(CHUNKS)]
+        ident = held("ident", [P, P], F32)
+        make_identity(nc, ident[:])
         warm = held("warm", [P, 2], F32)
         nc.gpsimd.memset(warm[:, 0:1], 1.0)
         nc.scalar.activation(warm[:, 1:2], warm[:, 0:1], ACT.Abs_reciprocal_sqrt)
 
-        for plane in (tab_s, wc_s_raw):
+        for plane in (wc_s_raw, tab_s):
             nc.vector.memset(plane[:].bitcast(I32), 0)
         nc.vector.memset(wf_s[:].rearrange("p a n -> p (a n)").bitcast(I32), 0)
 
         def load_scale_rows(plane, rows):
             for q in range(4):
-                nc.scalar.dma_start(plane[32 * q : 32 * q + 4, :].bitcast(I32), rows[4 * q : 4 * q + 4, :].bitcast(I32))
+                nc.sync.dma_start(plane[32 * q : 32 * q + 4, :].bitcast(I32), rows[4 * q : 4 * q + 4, :].bitcast(I32))
 
         x_rows = xT.rearrange("(p t) c -> p t c", t=PACK)
         ws_rows = ws.rearrange("(p t) c -> p t c", t=PACK)
@@ -84,18 +88,19 @@ def tile_list_grain_sheath_forces_kernel(
         out_rows = out.rearrange("(m p) j -> p m j", p=P)
 
         nc.sync.dma_start(idx_tab[:], offs)
-        nc.sync.dma_start(wc_w_raw[:], wc_words[0])
-        nc.sync.dma_start(tab_w[:].bitcast(I32), tab_words[0].rearrange("p n t -> p (n t)").bitcast(I32))
-        load_scale_rows(tab_s, tab_scales[0])
         load_scale_rows(wc_s_raw, wc_scales[0])
+        nc.sync.dma_start(wc_w_raw[:], wc_words[0])
+        load_scale_rows(tab_s, tab_scales[0])
+        nc.sync.dma_start(tab_w[:].bitcast(I32), tab_words[0].rearrange("p n t -> p (n t)").bitcast(I32))
         nc.scalar.dma_start(gains[:], gain.rearrange("(a p t) -> p a t", p=P, t=PACK))
-        nc.sync.dma_start(ws_raw[0][:], ws_rows[:, :, 0:PASS])
         nc.sync.dma_start(idx_b[:], offs3)
         nc.sync.dma_start(planes[0][:], x_rows[:, 0, :])
         nc.sync.dma_start(idx_a[:], offs2)
+        nc.sync.dma_start(ws_raw[0][:], ws_rows[:, :, 0:PASS])
+        nc.sync.dma_start(planes[1][:], x_rows[:, 1, :])
+        nc.sync.dma_start(planes[2][:], x_rows[:, 2, :])
         nc.sync.dma_start(ws_raw[1][:], ws_rows[:, :, PASS : 2 * PASS])
-        for t in range(1, PACK):
-            nc.sync.dma_start(planes[t][:], x_rows[:, t, :])
+        nc.sync.dma_start(planes[3][:], x_rows[:, 3, :])
         nc.sync.dma_start(
             wf_w[:].bitcast(I32), wf_words.rearrange("a p n t -> p a (n t)").bitcast(I32)
         )
@@ -121,10 +126,11 @@ def tile_list_grain_sheath_forces_kernel(
 
         def quantise_ws(a):
             grouped = ring.tile([P, PACK, P, PACK], BF16, name="ws_grouped", align_bytes=64)
-            nc.scalar.copy(
-                grouped[:].rearrange("p t (g i) j -> p g j i t", i=2),
-                ws_raw[a][:].rearrange("p j (g i t) -> p g j i t", i=2, t=PACK),
-            )
+            for t0 in range(0, PACK, 2):
+                nc.scalar.copy(
+                    grouped[:].rearrange("p t (g i) j -> p g j i t", i=2)[:, :, :, :, t0 : t0 + 2],
+                    ws_raw[a][:].rearrange("p j (g i t) -> p g j i t", i=2, t=PACK)[:, :, :, :, t0 : t0 + 2],
+                )
             nc.vector.quantize_mx(
                 out=ws_w[a][:].bitcast(FP8X4), scales=ws_s[a][:],
                 in_=grouped[:].rearrange("p t m j -> p (t m j)"),
@@ -136,48 +142,62 @@ def tile_list_grain_sheath_forces_kernel(
 
         species = {}
 
-        def gather_species(k):
-            cols = slice(k * LIST_COLS, (k + 1) * LIST_COLS)
-            v_w = held("v_w%d" % k, [P, CHUNK], U32)
-            v_s = held("v_s%d" % k, [P, CHUNK], U8)
+        def gather_species(pair):
+            cols = slice(pair * BANK // 16, (pair + 1) * BANK // 16)
+            v_w = held("v_w%d" % pair, [P, BANK], U32)
+            v_s = held("v_s%d" % pair, [P, BANK], U8)
             nc.vector.tensor_copy(v_w[:], tab_w[:].indirect(idx_tab[:, cols]))
             nc.vector.tensor_copy(v_s[:], tab_s[:].indirect(idx_tab[:, cols]))
-            species[k] = (v_w, v_s)
+            species[pair] = (v_w, v_s)
 
-        def species_response(k):
-            v_w, v_s = species[k]
-            for a in range(H_PASSES):
-                soft[k, a] = held("soft%d_%d" % (k, a), [P, PACK, CHUNK], F32)
-                gained[k, a] = held("gained%d_%d" % (k, a), [P, PACK, CHUNK], F32)
-                for t0 in range(0, PACK, PER_BANK):
-                    c = psum.tile([P, PER_BANK, CHUNK], F32, name="c_or_y", bufs=5)
-                    for u in range(PER_BANK):
-                        col = a * PASS + (t0 + u) * P
-                        nc.tensor.matmul_mx(
-                            out=c[:, u, :],
-                            lhsT=wc_w[:, 2 * col : 2 * (col + P)].bitcast(FP4X4),
-                            lhsT_scale=wc_s[:, col : col + P],
-                            rhs=v_w[:].bitcast(FP8X4), rhs_scale=v_s[:],
-                            start=True, stop=True,
-                        )
-                    nc.scalar.activation(soft[k, a][:, t0 : t0 + PER_BANK, :], c[:], ACT.Square)
-                    for u in range(PER_BANK):
-                        t = t0 + u
-                        nc.scalar.activation(
-                            gained[k, a][:, t, :], c[:, u, :], ACT.Copy, scale=gains[:, a, t : t + 1]
-                        )
+        def species_response(step):
+            pair, a = divmod(step, H_PASSES)
+            v_w, v_s = species[pair]
+            squares = held("soft%d_%d" % (pair, a), [P, PER_BANK, PACK, CHUNK], F32)
+            scaled = held("gained%d_%d" % (pair, a), [P, PER_BANK, PACK, CHUNK], F32)
+            for u in range(PER_BANK):
+                soft[pair * PER_BANK + u, a] = squares[:, u, :, :]
+                gained[pair * PER_BANK + u, a] = scaled[:, u, :, :]
+            for t in range(PACK):
+                c = psum.tile([P, PER_BANK, CHUNK], F32, name="c_or_y", bufs=5)
+                col = a * PASS + t * P
+                nc.tensor.matmul_mx(
+                    out=c[:].rearrange("p u j -> p (u j)"),
+                    lhsT=wc_w[:, 2 * col : 2 * (col + P)].bitcast(FP4X4),
+                    lhsT_scale=wc_s[:, col : col + P],
+                    rhs=v_w[:].bitcast(FP8X4), rhs_scale=v_s[:],
+                    start=True, stop=True,
+                )
+                if pair == TURNED // PER_BANK:
+                    u = 1 - TURNED % PER_BANK
+                    nc.scalar.activation(squares[:, u, t, :], c[:, u, :], ACT.Square)
+                else:
+                    nc.scalar.activation(squares[:, :, t, :], c[:], ACT.Square)
+                nc.scalar.activation(scaled[:, :, t, :], c[:], ACT.Copy, scale=gains[:, a, t : t + 1])
 
-        def gather_separation(t, first, count, second):
-            cols = slice(first // 16, (first + count) // 16)
+            if pair == TURNED // PER_BANK:
+                turned = soft[TURNED, a].rearrange("p t j -> p (t j)")
+                for b in range(CHUNK // P):
+                    c = psum.tile([P, PASS], F32, name="c_or_y", bufs=5)
+                    col = (TURNED % PER_BANK) * CHUNK + b * P
+                    nc.tensor.matmul_mx(
+                        out=c[:],
+                        lhsT=v_w[:, col : col + P].bitcast(FP8X4), lhsT_scale=v_s[:, col : col + P],
+                        rhs=wc_w[:, 2 * a * PASS : 2 * (a + 1) * PASS].bitcast(FP4X4),
+                        rhs_scale=wc_s[:, a * PASS : (a + 1) * PASS],
+                        start=True, stop=True,
+                    )
+                    nc.scalar.activation(turned[:, b * PASS : (b + 1) * PASS], c[:], ACT.Square)
+
+        def gather_separation(t, k, second):
+            cols = slice(k * LIST_COLS, (k + 1) * LIST_COLS)
             nc.vector.tensor_copy(second, planes[t][:].indirect(idx_b[:, cols]))
-            nc.vector.tensor_tensor(
-                sep[:, t, first : first + count], planes[t][:].indirect(idx_a[:, cols]), second, ALU.subtract
-            )
+            nc.vector.tensor_tensor(sep[k][:, t, :], planes[t][:].indirect(idx_a[:, cols]), second, ALU.subtract)
 
         def gather_plane(t):
-            for first in range(0, S, 2 * CHUNK):
-                second = ring.tile([P, 2 * CHUNK], F32, name="second", bufs=3)
-                gather_separation(t, first, 2 * CHUNK, second[:])
+            for k in range(CHUNKS):
+                second = ring.tile([P, CHUNK], F32, name="second", bufs=3)
+                gather_separation(t, k, second[:])
 
         def gather_last_planes(k):
             for t in range(WIDE_PLANES, PACK):
@@ -186,7 +206,7 @@ def tile_list_grain_sheath_forces_kernel(
                 else:
                     u = t - WIDE_PLANES
                     second = sep_grouped[k - LAG][:].bitcast(F32)[:, u * CHUNK : (u + 1) * CHUNK]
-                gather_separation(t, k * CHUNK, CHUNK, second)
+                gather_separation(t, k, second)
 
         separations = {}
         d_squares = {}
@@ -195,7 +215,7 @@ def tile_list_grain_sheath_forces_kernel(
         def quantise_separation(k):
             nc.scalar.copy(
                 sep_grouped[k][:].rearrange("p (g i t) -> p g t i", i=RUN, t=PACK),
-                sep[:, :, k * CHUNK : (k + 1) * CHUNK].rearrange("p t (g i) -> p g t i", i=RUN),
+                sep[k][:].rearrange("p t (g i) -> p g t i", i=RUN),
             )
             x_w = held("x_w%d" % k, [P, CHUNK], U32)
             x_s = held("x_s%d" % k, [P, CHUNK], U8)
@@ -206,6 +226,19 @@ def tile_list_grain_sheath_forces_kernel(
             x_w, x_s = separations[k]
             for a in range(H_PASSES):
                 d_sq = ring.tile([P, PACK, CHUNK], F32, name="d_sq", bufs=4)
+                d_squares[k, a] = d_sq
+                if k == TURNED:
+                    turned = d_sq[:].rearrange("p t j -> p (t j)")
+                    for b in range(CHUNK // P):
+                        d = psum.tile([P, PASS], F32, name="d", bufs=3)
+                        nc.tensor.matmul_mx(
+                            out=d[:],
+                            lhsT=x_w[:, b * P : (b + 1) * P].bitcast(FP8X4), lhsT_scale=x_s[:, b * P : (b + 1) * P],
+                            rhs=ws_w[a][:].bitcast(FP8X4), rhs_scale=ws_s[a][:],
+                            start=True, stop=True,
+                        )
+                        nc.scalar.activation(turned[:, b * PASS : (b + 1) * PASS], d[:], ACT.Square)
+                    continue
                 for t0 in range(0, PACK, PER_BANK):
                     d = psum.tile([P, PER_BANK, CHUNK], F32, name="d", bufs=3)
                     for u in range(PER_BANK):
@@ -218,12 +251,29 @@ def tile_list_grain_sheath_forces_kernel(
                             start=True, stop=True,
                         )
                     nc.scalar.activation(d_sq[:, t0 : t0 + PER_BANK, :], d[:], ACT.Square)
-                d_squares[k, a] = d_sq
 
         def soften(k):
             for a in range(H_PASSES):
-                nc.vector.tensor_tensor(soft[k, a][:], soft[k, a][:], d_squares[k, a][:], ALU.add)
-                nc.scalar.activation(soft[k, a][:], soft[k, a][:], ACT.Abs_reciprocal_sqrt, bias=1.0)
+                if k == TURNED:
+                    terms = [term.rearrange("p t j -> p (t j)") for term in (soft[k, a], d_squares[k, a][:])]
+                    sums = []
+                    for t0 in range(0, PACK, PER_BANK):
+                        total = psum.tile([P, PER_BANK, CHUNK], F32, name="d", bufs=3)
+                        for u in range(PER_BANK):
+                            for b in range(CHUNK // P):
+                                col = b * PASS + (t0 + u) * P
+                                for i, term in enumerate(terms):
+                                    nc.tensor.matmul(
+                                        total[:, u, b * P : (b + 1) * P], term[:, col : col + P], ident[:],
+                                        start=(i == 0), stop=(i == 1), is_transpose=True,
+                                    )
+                        sums.append(total)
+                    for i, total in enumerate(sums):
+                        rows = soft[k, a][:, i * PER_BANK : (i + 1) * PER_BANK, :]
+                        nc.scalar.activation(rows, total[:], ACT.Abs_reciprocal_sqrt, bias=1.0)
+                    continue
+                nc.vector.tensor_tensor(soft[k, a], soft[k, a], d_squares[k, a][:], ALU.add)
+                nc.scalar.activation(soft[k, a], soft[k, a], ACT.Abs_reciprocal_sqrt, bias=1.0)
 
         def quantise_interaction(k):
             h_w = []
@@ -232,8 +282,8 @@ def tile_list_grain_sheath_forces_kernel(
                 grouped = ring.tile([P, CHUNK, PACK], BF16, name="h_grouped", align_bytes=64)
                 nc.vector.tensor_tensor(
                     grouped[:].rearrange("p (g i) t -> p g t i", i=RUN),
-                    gained[k, a][:].rearrange("p t (g i) -> p g t i", i=RUN),
-                    soft[k, a][:].rearrange("p t (g i) -> p g t i", i=RUN),
+                    gained[k, a].rearrange("p t (g i) -> p g t i", i=RUN),
+                    soft[k, a].rearrange("p t (g i) -> p g t i", i=RUN),
                     ALU.mult,
                 )
                 words = ring.tile([P, CHUNK], U32, name="h_w", align_bytes=64, bufs=4)
@@ -249,15 +299,15 @@ def tile_list_grain_sheath_forces_kernel(
             h_w, h_s = interactions[k]
             for m0 in range(0, N_TILES, PER_BANK):
                 y = psum.tile([P, PER_BANK, CHUNK], F32, name="c_or_y", bufs=5)
-                for u in range(PER_BANK):
-                    col = (m0 + u) * P
-                    for a in range(H_PASSES):
+                for a in range(H_PASSES):
+                    for u in range(PER_BANK):
+                        col = (m0 + u) * P
                         nc.tensor.matmul_mx(
                             out=y[:, u, :],
                             lhsT=wf_w[:, a, col : col + P].bitcast(FP8X4),
                             lhsT_scale=wf_s[:, a, col : col + P],
                             rhs=h_w[a][:].bitcast(FP8X4), rhs_scale=h_s[a][:],
-                            start=(a == 0), stop=(a == H_PASSES - 1),
+                            start=(a == 0 and u == 0), stop=(a == H_PASSES - 1 and u == PER_BANK - 1),
                         )
                 rows = forces[k][:, m0 : m0 + PER_BANK, :]
                 nc.vector.tensor_tensor(rows, y[:], rows, ALU.add)
@@ -265,13 +315,10 @@ def tile_list_grain_sheath_forces_kernel(
 
         gather_species(0)
         gather_species(1)
-        gather_species(2)
-        gather_species(3)
         quantise_ws(0)
         species_response(0)
         quantise_ws(1)
         species_response(1)
-        species_response(2)
         gather_plane(0)
         gather_plane(1)
         gather_last_planes(0)
@@ -282,6 +329,7 @@ def tile_list_grain_sheath_forces_kernel(
         gather_last_planes(2)
         quantise_separation(2)
         separation_response(1)
+        species_response(2)
         gather_last_planes(3)
         quantise_separation(3)
         soften(0)

@@ -21,16 +21,17 @@ P = 128
 PACK = 4
 PASS = P * PACK
 H_PASSES = H // PASS
+BANK = 512
 CHUNK = 256
 CHUNKS = S // CHUNK
-LIST_COLS = CHUNK // 16
-BANK = 512
 PER_BANK = BANK // CHUNK
+LAST = CHUNKS - 1
+BLOCKS = CHUNK // P
 N_TILES = N // P
+PER_COLUMN = 16
 RUN = 2
-WIDE_PLANES = 2
+EARLY_PLANES = 2
 LAG = 2
-TURNED = 3
 
 
 def tile_list_grain_sheath_forces_kernel(
@@ -46,9 +47,15 @@ def tile_list_grain_sheath_forces_kernel(
         def held(name, shape, dtype):
             return keep.tile(shape, dtype, name=name, align_bytes=64)
 
-        idx_tab = keep.tile([P, S // 16], U16, name="idx_tab")
-        idx_a = keep.tile([P, S // 16], U16, name="idx_a")
-        idx_b = keep.tile([P, S // 16], U16, name="idx_b")
+        def c_or_y_bank(shape):
+            return psum.tile(shape, F32, name="c_or_y", bufs=5)
+
+        def d_bank(shape):
+            return psum.tile(shape, F32, name="d", bufs=3)
+
+        idx_tab = keep.tile([P, S // PER_COLUMN], U16, name="idx_tab")
+        idx_a = keep.tile([P, S // PER_COLUMN], U16, name="idx_a")
+        idx_b = keep.tile([P, S // PER_COLUMN], U16, name="idx_b")
         tab_w = held("tab_w", [P, T], U32)
         tab_s = held("tab_s", [P, T], U8)
         wc_w_raw = held("wc_w_raw", [P, 2 * H], U8)
@@ -59,17 +66,26 @@ def tile_list_grain_sheath_forces_kernel(
         wf_s = held("wf_s", [P, H_PASSES, N], U8)
         planes = [held("plane%d" % t, [P, T], F32) for t in range(PACK)]
         ws_raw = [held("ws_raw%d" % a, [P, PACK, PASS], F32) for a in range(H_PASSES)]
-        ws_w = [held("ws_w%d" % a, [P, PASS], U32) for a in range(H_PASSES)]
+        ws_grouped = [held("ws_grouped%d" % a, [P, PACK, P, PACK], BF16) for a in range(H_PASSES)]
         ws_s = [held("ws_s%d" % a, [P, PASS], U8) for a in range(H_PASSES)]
         gains = held("gains", [P, H_PASSES, PACK], F32)
-        forces = [held("forces%d" % k, [P, N_TILES, CHUNK], F32)[:] for k in range(CHUNKS - H_PASSES)]
-        for a in range(H_PASSES):
-            flat = ws_raw[a][:].rearrange("p t c -> p (t c)")
-            forces.append(flat[:, 0 : N_TILES * CHUNK].rearrange("p (m j) -> p m j", j=CHUNK))
         sep = [held("sep%d" % k, [P, PACK, CHUNK], F32) for k in range(CHUNKS)]
         sep_grouped = [held("sep_grouped%d" % k, [P, CHUNK * PACK], BF16) for k in range(CHUNKS)]
         ident = held("ident", [P, P], F32)
         make_identity(nc, ident[:])
+
+        drag_room = [held("forces%d" % k, [P, N_TILES * CHUNK], F32)[:] for k in range(CHUNKS - H_PASSES)]
+        for a in range(H_PASSES):
+            drag_room.append(ws_raw[a][:].rearrange("p t c -> p (t c)")[:, 0 : N_TILES * CHUNK])
+
+        def pieces(k):
+            width = P if k == LAST else CHUNK
+            return [(first, width) for first in range(0, CHUNK, width)]
+
+        def forces(k, first, width):
+            room = drag_room[k][:, N_TILES * first : N_TILES * (first + width)]
+            return room.rearrange("p (m j) -> p m j", j=width)
+
         warm = held("warm", [P, 2], F32)
         nc.gpsimd.memset(warm[:, 0:1], 1.0)
         nc.scalar.activation(warm[:, 1:2], warm[:, 0:1], ACT.Abs_reciprocal_sqrt)
@@ -87,6 +103,17 @@ def tile_list_grain_sheath_forces_kernel(
         drag_rows = drag.rearrange("(m p) j -> p m j", p=P)
         out_rows = out.rearrange("(m p) j -> p m j", p=P)
 
+        def load_ws(a):
+            nc.sync.dma_start(ws_raw[a][:], ws_rows[:, :, a * PASS : (a + 1) * PASS])
+
+        def load_plane(t):
+            nc.sync.dma_start(planes[t][:], x_rows[:, t, :])
+
+        def load_drag(k):
+            for first, width in pieces(k):
+                col = k * CHUNK + first
+                nc.sync.dma_start(forces(k, first, width), drag_rows[:, :, col : col + width])
+
         nc.sync.dma_start(idx_tab[:], offs)
         load_scale_rows(wc_s_raw, wc_scales[0])
         nc.sync.dma_start(wc_w_raw[:], wc_words[0])
@@ -94,24 +121,19 @@ def tile_list_grain_sheath_forces_kernel(
         nc.sync.dma_start(tab_w[:].bitcast(I32), tab_words[0].rearrange("p n t -> p (n t)").bitcast(I32))
         nc.scalar.dma_start(gains[:], gain.rearrange("(a p t) -> p a t", p=P, t=PACK))
         nc.sync.dma_start(idx_b[:], offs3)
-        nc.sync.dma_start(planes[0][:], x_rows[:, 0, :])
+        load_plane(0)
         nc.sync.dma_start(idx_a[:], offs2)
-        nc.sync.dma_start(ws_raw[0][:], ws_rows[:, :, 0:PASS])
-        nc.sync.dma_start(planes[1][:], x_rows[:, 1, :])
-        nc.sync.dma_start(planes[2][:], x_rows[:, 2, :])
-        nc.sync.dma_start(ws_raw[1][:], ws_rows[:, :, PASS : 2 * PASS])
-        nc.sync.dma_start(planes[3][:], x_rows[:, 3, :])
-        nc.sync.dma_start(
-            wf_w[:].bitcast(I32), wf_words.rearrange("a p n t -> p a (n t)").bitcast(I32)
-        )
+        load_ws(0)
+        load_plane(1)
+        load_plane(2)
+        load_ws(1)
+        load_plane(3)
+        nc.sync.dma_start(wf_w[:].bitcast(I32), wf_words.rearrange("a p n t -> p a (n t)").bitcast(I32))
         for q in range(4):
             nc.sync.dma_start(
                 wf_s[32 * q : 32 * q + 4, :, :].bitcast(I32),
                 wf_scales[:, 4 * q : 4 * q + 4, :].rearrange("a r n -> r a n").bitcast(I32),
             )
-        def load_drag(k):
-            nc.sync.dma_start(forces[k], drag_rows[:, :, k * CHUNK : (k + 1) * CHUNK])
-
         for k in range(CHUNKS - H_PASSES):
             load_drag(k)
 
@@ -124,62 +146,59 @@ def tile_list_grain_sheath_forces_kernel(
             wc_s_raw[:].rearrange("p (a m t) -> p a t m", a=H_PASSES, t=PACK),
         )
 
-        def quantise_ws(a):
-            grouped = ring.tile([P, PACK, P, PACK], BF16, name="ws_grouped", align_bytes=64)
+        def quantise(words, scales, grouped):
+            nc.vector.quantize_mx(out=words.bitcast(FP8X4), scales=scales, in_=grouped)
+
+        def round_ws(a):
+            target = ws_grouped[a][:].rearrange("p t (g i) j -> p g j i t", i=2)
+            source = ws_raw[a][:].rearrange("p j (g i t) -> p g j i t", i=2, t=PACK)
             for t0 in range(0, PACK, 2):
-                nc.scalar.copy(
-                    grouped[:].rearrange("p t (g i) j -> p g j i t", i=2)[:, :, :, :, t0 : t0 + 2],
-                    ws_raw[a][:].rearrange("p j (g i t) -> p g j i t", i=2, t=PACK)[:, :, :, :, t0 : t0 + 2],
-                )
-            nc.vector.quantize_mx(
-                out=ws_w[a][:].bitcast(FP8X4), scales=ws_s[a][:],
-                in_=grouped[:].rearrange("p t m j -> p (t m j)"),
-            )
+                nc.scalar.copy(target[:, :, :, :, t0 : t0 + 2], source[:, :, :, :, t0 : t0 + 2])
             load_drag(CHUNKS - H_PASSES + a)
 
+        ws_w = {}
+        species = {}
         soft = {}
         gained = {}
+        separations = {}
+        d_squares = {}
+        interactions = {}
 
-        species = {}
-
-        def gather_species(pair):
-            cols = slice(pair * BANK // 16, (pair + 1) * BANK // 16)
-            v_w = held("v_w%d" % pair, [P, BANK], U32)
-            v_s = held("v_s%d" % pair, [P, BANK], U8)
+        def gather_species(half):
+            cols = slice(half * BANK // PER_COLUMN, (half + 1) * BANK // PER_COLUMN)
+            v_w = held("v_w%d" % half, [P, BANK], U32)
+            v_s = held("v_s%d" % half, [P, BANK], U8)
             nc.vector.tensor_copy(v_w[:], tab_w[:].indirect(idx_tab[:, cols]))
             nc.vector.tensor_copy(v_s[:], tab_s[:].indirect(idx_tab[:, cols]))
-            species[pair] = (v_w, v_s)
+            species[half] = (v_w, v_s)
 
-        def species_response(step):
-            pair, a = divmod(step, H_PASSES)
-            v_w, v_s = species[pair]
-            squares = held("soft%d_%d" % (pair, a), [P, PER_BANK, PACK, CHUNK], F32)
-            scaled = held("gained%d_%d" % (pair, a), [P, PER_BANK, PACK, CHUNK], F32)
+        def turned(tile):
+            return tile.rearrange("p t j -> p (t j)").rearrange("p (b r) -> p b r", r=PASS)
+
+        def species_response(half, a):
+            v_w, v_s = species[half]
+            squares = held("soft%d_%d" % (half, a), [P, PER_BANK, PACK, CHUNK], F32)
+            scaled = held("gained%d_%d" % (half, a), [P, PER_BANK, PACK, CHUNK], F32)
             for u in range(PER_BANK):
-                soft[pair * PER_BANK + u, a] = squares[:, u, :, :]
-                gained[pair * PER_BANK + u, a] = scaled[:, u, :, :]
+                soft[half * PER_BANK + u, a] = squares[:, u, :, :]
+                gained[half * PER_BANK + u, a] = scaled[:, u, :, :]
+            has_last = half == LAST // PER_BANK
+            plain = PER_BANK - 1 if has_last else PER_BANK
             for t in range(PACK):
-                c = psum.tile([P, PER_BANK, CHUNK], F32, name="c_or_y", bufs=5)
+                c = c_or_y_bank([P, PER_BANK, CHUNK])
                 col = a * PASS + t * P
                 nc.tensor.matmul_mx(
                     out=c[:].rearrange("p u j -> p (u j)"),
-                    lhsT=wc_w[:, 2 * col : 2 * (col + P)].bitcast(FP4X4),
-                    lhsT_scale=wc_s[:, col : col + P],
+                    lhsT=wc_w[:, 2 * col : 2 * (col + P)].bitcast(FP4X4), lhsT_scale=wc_s[:, col : col + P],
                     rhs=v_w[:].bitcast(FP8X4), rhs_scale=v_s[:],
                     start=True, stop=True,
                 )
-                if pair == TURNED // PER_BANK:
-                    u = 1 - TURNED % PER_BANK
-                    nc.scalar.activation(squares[:, u, t, :], c[:, u, :], ACT.Square)
-                else:
-                    nc.scalar.activation(squares[:, :, t, :], c[:], ACT.Square)
+                nc.scalar.activation(squares[:, 0:plain, t, :], c[:, 0:plain, :], ACT.Square)
                 nc.scalar.activation(scaled[:, :, t, :], c[:], ACT.Copy, scale=gains[:, a, t : t + 1])
-
-            if pair == TURNED // PER_BANK:
-                turned = soft[TURNED, a].rearrange("p t j -> p (t j)")
-                for b in range(CHUNK // P):
-                    c = psum.tile([P, PASS], F32, name="c_or_y", bufs=5)
-                    col = (TURNED % PER_BANK) * CHUNK + b * P
+            if has_last:
+                for b in range(BLOCKS):
+                    c = c_or_y_bank([P, PASS])
+                    col = plain * CHUNK + b * P
                     nc.tensor.matmul_mx(
                         out=c[:],
                         lhsT=v_w[:, col : col + P].bitcast(FP8X4), lhsT_scale=v_s[:, col : col + P],
@@ -187,163 +206,149 @@ def tile_list_grain_sheath_forces_kernel(
                         rhs_scale=wc_s[:, a * PASS : (a + 1) * PASS],
                         start=True, stop=True,
                     )
-                    nc.scalar.activation(turned[:, b * PASS : (b + 1) * PASS], c[:], ACT.Square)
+                    nc.scalar.activation(turned(soft[LAST, a])[:, b, :], c[:], ACT.Square)
 
         def gather_separation(t, k, second):
-            cols = slice(k * LIST_COLS, (k + 1) * LIST_COLS)
+            cols = slice(k * CHUNK // PER_COLUMN, (k + 1) * CHUNK // PER_COLUMN)
             nc.vector.tensor_copy(second, planes[t][:].indirect(idx_b[:, cols]))
             nc.vector.tensor_tensor(sep[k][:, t, :], planes[t][:].indirect(idx_a[:, cols]), second, ALU.subtract)
 
-        def gather_plane(t):
-            for k in range(CHUNKS):
-                second = ring.tile([P, CHUNK], F32, name="second", bufs=3)
-                gather_separation(t, k, second[:])
+        def second_grains():
+            return ring.tile([P, CHUNK], F32, name="second", bufs=3)[:]
 
-        def gather_last_planes(k):
-            for t in range(WIDE_PLANES, PACK):
-                if k < LAG:
-                    second = ring.tile([P, CHUNK], F32, name="second", bufs=3)[:]
+        def ws_slot(a, shape, dtype):
+            return ring.tile(shape, dtype, name="ws_slot%d" % a, bufs=1, align_bytes=64)
+
+        def complete_separation(k):
+            for t in range(EARLY_PLANES, PACK):
+                if k < H_PASSES and t == PACK - 1:
+                    second = ws_slot(k, [P, CHUNK], F32)[:]
+                elif k < LAG:
+                    second = second_grains()
                 else:
-                    u = t - WIDE_PLANES
+                    u = t - EARLY_PLANES
                     second = sep_grouped[k - LAG][:].bitcast(F32)[:, u * CHUNK : (u + 1) * CHUNK]
                 gather_separation(t, k, second)
-
-        separations = {}
-        d_squares = {}
-        interactions = {}
-
-        def quantise_separation(k):
+            if k < H_PASSES:
+                ws_w[k] = ws_slot(k, [P, PASS], U32)
+                quantise(ws_w[k][:], ws_s[k][:], ws_grouped[k][:].rearrange("p t m j -> p (t m j)"))
             nc.scalar.copy(
                 sep_grouped[k][:].rearrange("p (g i t) -> p g t i", i=RUN, t=PACK),
                 sep[k][:].rearrange("p t (g i) -> p g t i", i=RUN),
             )
             x_w = held("x_w%d" % k, [P, CHUNK], U32)
             x_s = held("x_s%d" % k, [P, CHUNK], U8)
-            nc.vector.quantize_mx(out=x_w[:].bitcast(FP8X4), scales=x_s[:], in_=sep_grouped[k][:])
+            quantise(x_w[:], x_s[:], sep_grouped[k][:])
             separations[k] = (x_w, x_s)
 
         def separation_response(k):
             x_w, x_s = separations[k]
             for a in range(H_PASSES):
-                d_sq = ring.tile([P, PACK, CHUNK], F32, name="d_sq", bufs=4)
-                d_squares[k, a] = d_sq
-                if k == TURNED:
-                    turned = d_sq[:].rearrange("p t j -> p (t j)")
-                    for b in range(CHUNK // P):
-                        d = psum.tile([P, PASS], F32, name="d", bufs=3)
+                d_squares[k, a] = ring.tile([P, PACK, CHUNK], F32, name="d_sq", bufs=4)[:]
+            if k == LAST:
+                for b in range(BLOCKS):
+                    for a in range(H_PASSES):
+                        d = d_bank([P, PASS])
                         nc.tensor.matmul_mx(
                             out=d[:],
                             lhsT=x_w[:, b * P : (b + 1) * P].bitcast(FP8X4), lhsT_scale=x_s[:, b * P : (b + 1) * P],
                             rhs=ws_w[a][:].bitcast(FP8X4), rhs_scale=ws_s[a][:],
                             start=True, stop=True,
                         )
-                        nc.scalar.activation(turned[:, b * PASS : (b + 1) * PASS], d[:], ACT.Square)
-                    continue
+                        nc.scalar.activation(turned(d_squares[k, a])[:, b, :], d[:], ACT.Square)
+                return
+            for a in range(H_PASSES):
                 for t0 in range(0, PACK, PER_BANK):
-                    d = psum.tile([P, PER_BANK, CHUNK], F32, name="d", bufs=3)
+                    d = d_bank([P, PER_BANK, CHUNK])
                     for u in range(PER_BANK):
                         col = (t0 + u) * P
                         nc.tensor.matmul_mx(
                             out=d[:, u, :],
-                            lhsT=ws_w[a][:, col : col + P].bitcast(FP8X4),
-                            lhsT_scale=ws_s[a][:, col : col + P],
+                            lhsT=ws_w[a][:, col : col + P].bitcast(FP8X4), lhsT_scale=ws_s[a][:, col : col + P],
                             rhs=x_w[:].bitcast(FP8X4), rhs_scale=x_s[:],
                             start=True, stop=True,
                         )
-                    nc.scalar.activation(d_sq[:, t0 : t0 + PER_BANK, :], d[:], ACT.Square)
+                    nc.scalar.activation(d_squares[k, a][:, t0 : t0 + PER_BANK, :], d[:], ACT.Square)
+
+        def softening(k, a, first, width):
+            flat = soft[k, a].rearrange("p t j -> p (t j)")
+            return flat[:, PACK * first : PACK * (first + width)].rearrange("p (t j) -> p t j", t=PACK)
 
         def soften(k):
+            if k == LAST:
+                for b in range(BLOCKS):
+                    for a in range(H_PASSES):
+                        total = d_bank([P, PACK, P])
+                        for t in range(PACK):
+                            for i, term in enumerate((soft[k, a], d_squares[k, a])):
+                                nc.tensor.matmul(
+                                    total[:, t, :], turned(term)[:, b, t * P : (t + 1) * P], ident[:],
+                                    start=(i == 0), stop=(i == 1), is_transpose=True,
+                                )
+                        nc.scalar.activation(softening(k, a, b * P, P), total[:], ACT.Abs_reciprocal_sqrt, bias=1.0)
+                return
             for a in range(H_PASSES):
-                if k == TURNED:
-                    terms = [term.rearrange("p t j -> p (t j)") for term in (soft[k, a], d_squares[k, a][:])]
-                    sums = []
-                    for t0 in range(0, PACK, PER_BANK):
-                        total = psum.tile([P, PER_BANK, CHUNK], F32, name="d", bufs=3)
-                        for u in range(PER_BANK):
-                            for b in range(CHUNK // P):
-                                col = b * PASS + (t0 + u) * P
-                                for i, term in enumerate(terms):
-                                    nc.tensor.matmul(
-                                        total[:, u, b * P : (b + 1) * P], term[:, col : col + P], ident[:],
-                                        start=(i == 0), stop=(i == 1), is_transpose=True,
-                                    )
-                        sums.append(total)
-                    for i, total in enumerate(sums):
-                        rows = soft[k, a][:, i * PER_BANK : (i + 1) * PER_BANK, :]
-                        nc.scalar.activation(rows, total[:], ACT.Abs_reciprocal_sqrt, bias=1.0)
-                    continue
-                nc.vector.tensor_tensor(soft[k, a], soft[k, a], d_squares[k, a][:], ALU.add)
+                nc.vector.tensor_tensor(soft[k, a], soft[k, a], d_squares[k, a], ALU.add)
                 nc.scalar.activation(soft[k, a], soft[k, a], ACT.Abs_reciprocal_sqrt, bias=1.0)
 
-        def quantise_interaction(k):
-            h_w = []
-            h_s = []
+        def quantise_interaction(k, first, width):
             for a in range(H_PASSES):
-                grouped = ring.tile([P, CHUNK, PACK], BF16, name="h_grouped", align_bytes=64)
+                grouped = ring.tile([P, width, PACK], BF16, name="h_grouped", align_bytes=64)
                 nc.vector.tensor_tensor(
                     grouped[:].rearrange("p (g i) t -> p g t i", i=RUN),
-                    gained[k, a].rearrange("p t (g i) -> p g t i", i=RUN),
-                    soft[k, a].rearrange("p t (g i) -> p g t i", i=RUN),
+                    gained[k, a][:, :, first : first + width].rearrange("p t (g i) -> p g t i", i=RUN),
+                    softening(k, a, first, width).rearrange("p t (g i) -> p g t i", i=RUN),
                     ALU.mult,
                 )
-                words = ring.tile([P, CHUNK], U32, name="h_w", align_bytes=64, bufs=4)
-                scales = ring.tile([P, CHUNK], U8, name="h_s", align_bytes=64, bufs=4)
-                nc.vector.quantize_mx(
-                    out=words[:].bitcast(FP8X4), scales=scales[:], in_=grouped[:].rearrange("p n t -> p (n t)")
-                )
-                h_w.append(words)
-                h_s.append(scales)
-            interactions[k] = (h_w, h_s)
+                words = ring.tile([P, width], U32, name="h_w", align_bytes=64, bufs=4)
+                scales = ring.tile([P, width], U8, name="h_s", align_bytes=64, bufs=4)
+                quantise(words[:], scales[:], grouped[:].rearrange("p n t -> p (n t)"))
+                interactions[k, first, a] = (words, scales)
 
-        def forces_of(k):
-            h_w, h_s = interactions[k]
-            for m0 in range(0, N_TILES, PER_BANK):
-                y = psum.tile([P, PER_BANK, CHUNK], F32, name="c_or_y", bufs=5)
+        def store_forces(k, first, width):
+            tiles = BANK // width
+            for m0 in range(0, N_TILES, tiles):
+                count = min(tiles, N_TILES - m0)
+                y = c_or_y_bank([P, count, width])
                 for a in range(H_PASSES):
-                    for u in range(PER_BANK):
+                    h_w, h_s = interactions[k, first, a]
+                    for u in range(count):
                         col = (m0 + u) * P
                         nc.tensor.matmul_mx(
                             out=y[:, u, :],
-                            lhsT=wf_w[:, a, col : col + P].bitcast(FP8X4),
-                            lhsT_scale=wf_s[:, a, col : col + P],
-                            rhs=h_w[a][:].bitcast(FP8X4), rhs_scale=h_s[a][:],
-                            start=(a == 0 and u == 0), stop=(a == H_PASSES - 1 and u == PER_BANK - 1),
+                            lhsT=wf_w[:, a, col : col + P].bitcast(FP8X4), lhsT_scale=wf_s[:, a, col : col + P],
+                            rhs=h_w[:].bitcast(FP8X4), rhs_scale=h_s[:],
+                            start=(a == 0 and u == 0), stop=(a == H_PASSES - 1 and u == count - 1),
                         )
-                rows = forces[k][:, m0 : m0 + PER_BANK, :]
+                rows = forces(k, first, width)[:, m0 : m0 + count, :]
                 nc.vector.tensor_tensor(rows, y[:], rows, ALU.add)
-                nc.sync.dma_start(out_rows[:, m0 : m0 + PER_BANK, k * CHUNK : (k + 1) * CHUNK], rows)
+                col = k * CHUNK + first
+                nc.sync.dma_start(out_rows[:, m0 : m0 + count, col : col + width], rows)
 
-        gather_species(0)
-        gather_species(1)
-        quantise_ws(0)
-        species_response(0)
-        quantise_ws(1)
-        species_response(1)
-        gather_plane(0)
-        gather_plane(1)
-        gather_last_planes(0)
-        quantise_separation(0)
-        gather_last_planes(1)
-        quantise_separation(1)
-        separation_response(0)
-        gather_last_planes(2)
-        quantise_separation(2)
-        separation_response(1)
-        species_response(2)
-        gather_last_planes(3)
-        quantise_separation(3)
-        soften(0)
-        separation_response(2)
-        soften(1)
-        species_response(3)
-        quantise_interaction(0)
-        separation_response(3)
-        soften(2)
-        quantise_interaction(1)
-        forces_of(0)
-        soften(3)
-        quantise_interaction(2)
-        forces_of(1)
-        quantise_interaction(3)
-        forces_of(2)
-        forces_of(3)
+        for half in range(CHUNKS // PER_BANK):
+            gather_species(half)
+        for a in range(H_PASSES):
+            round_ws(a)
+            species_response(0, a)
+        for t in range(EARLY_PLANES):
+            for k in range(CHUNKS):
+                gather_separation(t, k, second_grains())
+
+        for s in range(CHUNKS):
+            complete_separation(s)
+            if s >= 1:
+                separation_response(s - 1)
+            if s >= 2:
+                soften(s - 2)
+                species_response(1, s - 2)
+
+        work = [(k, first, width) for k in range(CHUNKS) for first, width in pieces(k)]
+        for i, piece in enumerate(work):
+            quantise_interaction(*piece)
+            if i == 0:
+                separation_response(LAST)
+            else:
+                store_forces(*work[i - 1])
+            if i < 2:
+                soften(i + 2)
+        store_forces(*work[-1])

@@ -30,8 +30,9 @@ BLOCKS = CHUNK // P
 N_TILES = N // P
 PER_COLUMN = 16
 RUN = 2
+LINE = 4
 EARLY_PLANES = 2
-LAG = 2
+SCALAR_BANKS = 4
 
 
 def tile_list_grain_sheath_forces_kernel(
@@ -41,23 +42,29 @@ def tile_list_grain_sheath_forces_kernel(
     nc = tc.nc
     with ExitStack() as ctx:
         keep = ctx.enter_context(tc.tile_pool(name="keep", bufs=1))
-        ring = ctx.enter_context(tc.tile_pool(name="ring", bufs=2))
         psum = ctx.enter_context(tc.psum_pool(name="psum", bufs=1))
 
         def held(name, shape, dtype):
             return keep.tile(shape, dtype, name=name, align_bytes=64)
 
-        def c_or_y_bank(shape):
-            return psum.tile(shape, F32, name="c_or_y", bufs=5)
+        def in_turn(tiles):
+            handed = []
 
-        def d_bank(shape):
-            return psum.tile(shape, F32, name="d", bufs=3)
+            def take():
+                handed.append(None)
+                return tiles[(len(handed) - 1) % len(tiles)]
+
+            return take
+
+        banks = [psum.tile([P, BANK], F32, name="bank%d" % i) for i in range(8)]
+        scalar_bank = in_turn(banks[:SCALAR_BANKS])
+        vector_bank = in_turn(banks[SCALAR_BANKS:])
 
         idx_tab = keep.tile([P, S // PER_COLUMN], U16, name="idx_tab")
         idx_a = keep.tile([P, S // PER_COLUMN], U16, name="idx_a")
         idx_b = keep.tile([P, S // PER_COLUMN], U16, name="idx_b")
         tab_w = held("tab_w", [P, T], U32)
-        tab_s = held("tab_s", [P, T], U8)
+        tab_s = keep.tile([P, T], U8, name="tab_s", tag="scales_then_words", align_bytes=64)
         wc_w_raw = held("wc_w_raw", [P, 2 * H], U8)
         wc_s_raw = held("wc_s_raw", [P, H], U8)
         wc_w = held("wc_w", [P, 2 * H], U8)
@@ -67,12 +74,19 @@ def tile_list_grain_sheath_forces_kernel(
         planes = [held("plane%d" % t, [P, T], F32) for t in range(PACK)]
         ws_raw = [held("ws_raw%d" % a, [P, PACK, PASS], F32) for a in range(H_PASSES)]
         ws_grouped = [held("ws_grouped%d" % a, [P, PACK, P, PACK], BF16) for a in range(H_PASSES)]
+        ws_w = [held("ws_w%d" % a, [P, PASS], U32) for a in range(H_PASSES)]
         ws_s = [held("ws_s%d" % a, [P, PASS], U8) for a in range(H_PASSES)]
         gains = held("gains", [P, H_PASSES, PACK], F32)
         sep = [held("sep%d" % k, [P, PACK, CHUNK], F32) for k in range(CHUNKS)]
-        sep_grouped = [held("sep_grouped%d" % k, [P, CHUNK * PACK], BF16) for k in range(CHUNKS)]
         ident = held("ident", [P, P], F32)
-        make_identity(nc, ident[:])
+        second_grains = in_turn([held("second%d" % i, [P, CHUNK], F32) for i in range(3)])
+        crossed = [held("late_second%d" % i, [P, CHUNK], F32) for i in range(2)]
+        sep_grouped = in_turn([held("sep_grouped%d" % i, [P, CHUNK * PACK], BF16) for i in range(2)])
+        d_room = in_turn([held("d_sq%d" % i, [P, PACK, CHUNK], F32) for i in range(3)])
+        soft_room = in_turn([held("soft%d" % i, [P, BANK], F32) for i in range(4)])
+        h_grouped = in_turn([held("h_grouped%d" % i, [P, CHUNK * PACK], BF16) for i in range(3)])
+        h_words = in_turn([held("h_w%d" % i, [P, CHUNK], U32) for i in range(4)])
+        h_scales = in_turn([held("h_s%d" % i, [P, CHUNK], U8) for i in range(4)])
 
         drag_room = [held("forces%d" % k, [P, N_TILES * CHUNK], F32)[:] for k in range(CHUNKS - H_PASSES)]
         for a in range(H_PASSES):
@@ -86,17 +100,18 @@ def tile_list_grain_sheath_forces_kernel(
             room = drag_room[k][:, N_TILES * first : N_TILES * (first + width)]
             return room.rearrange("p (m j) -> p m j", j=width)
 
-        warm = held("warm", [P, 2], F32)
-        nc.gpsimd.memset(warm[:, 0:1], 1.0)
-        nc.scalar.activation(warm[:, 1:2], warm[:, 0:1], ACT.Abs_reciprocal_sqrt)
+        def load_scale_rows(queue, plane, rows):
+            for q in range(4):
+                queue.dma_start(plane[32 * q : 32 * q + 4, :].bitcast(I32), rows[4 * q : 4 * q + 4, :].bitcast(I32))
 
-        for plane in (wc_s_raw, tab_s):
-            nc.vector.memset(plane[:].bitcast(I32), 0)
+        nc.vector.memset(wc_s_raw[:].bitcast(I32), 0)
+        nc.vector.memset(tab_s[:].bitcast(I32), 0)
         nc.vector.memset(wf_s[:].rearrange("p a n -> p (a n)").bitcast(I32), 0)
 
-        def load_scale_rows(plane, rows):
-            for q in range(4):
-                nc.sync.dma_start(plane[32 * q : 32 * q + 4, :].bitcast(I32), rows[4 * q : 4 * q + 4, :].bitcast(I32))
+        warm = held("warm", [P, 2], F32)
+        nc.vector.memset(warm[:, 0:1], 1.0)
+        nc.scalar.activation(warm[:, 1:2], warm[:, 0:1], ACT.Abs_reciprocal_sqrt)
+        make_identity(nc, ident[:])
 
         x_rows = xT.rearrange("(p t) c -> p t c", t=PACK)
         ws_rows = ws.rearrange("(p t) c -> p t c", t=PACK)
@@ -115,18 +130,18 @@ def tile_list_grain_sheath_forces_kernel(
                 nc.sync.dma_start(forces(k, first, width), drag_rows[:, :, col : col + width])
 
         nc.sync.dma_start(idx_tab[:], offs)
-        load_scale_rows(wc_s_raw, wc_scales[0])
+        load_scale_rows(nc.sync, wc_s_raw, wc_scales[0])
         nc.sync.dma_start(wc_w_raw[:], wc_words[0])
-        load_scale_rows(tab_s, tab_scales[0])
         nc.sync.dma_start(tab_w[:].bitcast(I32), tab_words[0].rearrange("p n t -> p (n t)").bitcast(I32))
-        nc.scalar.dma_start(gains[:], gain.rearrange("(a p t) -> p a t", p=P, t=PACK))
-        nc.sync.dma_start(idx_b[:], offs3)
+        load_scale_rows(nc.sync, tab_s, tab_scales[0])
+        nc.sync.dma_start(gains[:], gain.rearrange("(a p t) -> p a t", p=P, t=PACK))
         load_plane(0)
+        nc.sync.dma_start(idx_b[:], offs3)
         nc.sync.dma_start(idx_a[:], offs2)
         load_ws(0)
+        load_ws(1)
         load_plane(1)
         load_plane(2)
-        load_ws(1)
         load_plane(3)
         nc.sync.dma_start(wf_w[:].bitcast(I32), wf_words.rearrange("a p n t -> p a (n t)").bitcast(I32))
         for q in range(4):
@@ -156,99 +171,113 @@ def tile_list_grain_sheath_forces_kernel(
                 nc.scalar.copy(target[:, :, :, :, t0 : t0 + 2], source[:, :, :, :, t0 : t0 + 2])
             load_drag(CHUNKS - H_PASSES + a)
 
-        ws_w = {}
+        def quantise_ws(a):
+            quantise(ws_w[a][:], ws_s[a][:], ws_grouped[a][:].rearrange("p t m j -> p (t m j)"))
+
         species = {}
-        soft = {}
+        c_rooms = {}
+        c_squares = {}
         gained = {}
         separations = {}
         d_squares = {}
+        softening = {}
+        grouped_h = {}
         interactions = {}
 
-        def gather_species(half):
+        def gather_species_scales(half):
             cols = slice(half * BANK // PER_COLUMN, (half + 1) * BANK // PER_COLUMN)
-            v_w = held("v_w%d" % half, [P, BANK], U32)
             v_s = held("v_s%d" % half, [P, BANK], U8)
-            nc.vector.tensor_copy(v_w[:], tab_w[:].indirect(idx_tab[:, cols]))
             nc.vector.tensor_copy(v_s[:], tab_s[:].indirect(idx_tab[:, cols]))
-            species[half] = (v_w, v_s)
+            species[half, "s"] = v_s
+
+        def gather_species_words(half):
+            cols = slice(half * BANK // PER_COLUMN, (half + 1) * BANK // PER_COLUMN)
+            if half == 0:
+                v_w = held("v_w0", [P, BANK], U32)
+            else:
+                v_w = keep.tile([P, BANK], U32, name="v_w1", tag="scales_then_words", align_bytes=64)
+            nc.vector.tensor_copy(v_w[:], tab_w[:].indirect(idx_tab[:, cols]))
+            species[half, "w"] = v_w
 
         def turned(tile):
             return tile.rearrange("p t j -> p (t j)").rearrange("p (b r) -> p b r", r=PASS)
 
+        for half in range(CHUNKS // PER_BANK):
+            for a in range(H_PASSES):
+                squares = held("c_sq%d_%d" % (half, a), [P, PER_BANK, PACK, CHUNK], F32)
+                scaled = held("gained%d_%d" % (half, a), [P, PER_BANK, PACK, CHUNK], F32)
+                c_rooms[half, a] = (squares, scaled)
+                for u in range(PER_BANK):
+                    c_squares[half * PER_BANK + u, a] = squares[:, u, :, :]
+                    gained[half * PER_BANK + u, a] = scaled[:, u, :, :]
+
         def species_response(half, a):
-            v_w, v_s = species[half]
-            squares = held("soft%d_%d" % (half, a), [P, PER_BANK, PACK, CHUNK], F32)
-            scaled = held("gained%d_%d" % (half, a), [P, PER_BANK, PACK, CHUNK], F32)
-            for u in range(PER_BANK):
-                soft[half * PER_BANK + u, a] = squares[:, u, :, :]
-                gained[half * PER_BANK + u, a] = scaled[:, u, :, :]
-            has_last = half == LAST // PER_BANK
-            plain = PER_BANK - 1 if has_last else PER_BANK
+            v_w, v_s = species[half, "w"], species[half, "s"]
+            squares, scaled = c_rooms[half, a]
+            plain = PER_BANK - 1 if half == LAST // PER_BANK else PER_BANK
             for t in range(PACK):
-                c = c_or_y_bank([P, PER_BANK, CHUNK])
+                bank = scalar_bank()
+                c = bank[:].rearrange("p (u j) -> p u j", u=PER_BANK)
                 col = a * PASS + t * P
                 nc.tensor.matmul_mx(
-                    out=c[:].rearrange("p u j -> p (u j)"),
+                    out=bank[:],
                     lhsT=wc_w[:, 2 * col : 2 * (col + P)].bitcast(FP4X4), lhsT_scale=wc_s[:, col : col + P],
                     rhs=v_w[:].bitcast(FP8X4), rhs_scale=v_s[:],
                     start=True, stop=True,
                 )
                 nc.scalar.activation(squares[:, 0:plain, t, :], c[:, 0:plain, :], ACT.Square)
-                nc.scalar.activation(scaled[:, :, t, :], c[:], ACT.Copy, scale=gains[:, a, t : t + 1])
-            if has_last:
-                for b in range(BLOCKS):
-                    c = c_or_y_bank([P, PASS])
-                    col = plain * CHUNK + b * P
-                    nc.tensor.matmul_mx(
-                        out=c[:],
-                        lhsT=v_w[:, col : col + P].bitcast(FP8X4), lhsT_scale=v_s[:, col : col + P],
-                        rhs=wc_w[:, 2 * a * PASS : 2 * (a + 1) * PASS].bitcast(FP4X4),
-                        rhs_scale=wc_s[:, a * PASS : (a + 1) * PASS],
-                        start=True, stop=True,
-                    )
-                    nc.scalar.activation(turned(soft[LAST, a])[:, b, :], c[:], ACT.Square)
+                nc.scalar.activation(scaled[:, :, t, :], c, ACT.Copy, scale=gains[:, a, t : t + 1])
 
-        def gather_separation(t, k, second):
+        def turned_species_response(a):
+            v_w, v_s = species[LAST // PER_BANK, "w"], species[LAST // PER_BANK, "s"]
+            for b in range(BLOCKS):
+                c = scalar_bank()
+                col = (PER_BANK - 1) * CHUNK + b * P
+                nc.tensor.matmul_mx(
+                    out=c[:],
+                    lhsT=v_w[:, col : col + P].bitcast(FP8X4), lhsT_scale=v_s[:, col : col + P],
+                    rhs=wc_w[:, 2 * a * PASS : 2 * (a + 1) * PASS].bitcast(FP4X4),
+                    rhs_scale=wc_s[:, a * PASS : (a + 1) * PASS],
+                    start=True, stop=True,
+                )
+                nc.scalar.activation(turned(c_squares[LAST, a])[:, b, :], c[:], ACT.Square)
+
+        def gather_second(t, k, second):
             cols = slice(k * CHUNK // PER_COLUMN, (k + 1) * CHUNK // PER_COLUMN)
             nc.vector.tensor_copy(second, planes[t][:].indirect(idx_b[:, cols]))
+
+        def gather_first(t, k, second):
+            cols = slice(k * CHUNK // PER_COLUMN, (k + 1) * CHUNK // PER_COLUMN)
             nc.vector.tensor_tensor(sep[k][:, t, :], planes[t][:].indirect(idx_a[:, cols]), second, ALU.subtract)
 
-        def second_grains():
-            return ring.tile([P, CHUNK], F32, name="second", bufs=3)[:]
-
-        def ws_slot(a, shape, dtype):
-            return ring.tile(shape, dtype, name="ws_slot%d" % a, bufs=1, align_bytes=64)
-
         def complete_separation(k):
-            for t in range(EARLY_PLANES, PACK):
-                if k < H_PASSES and t == PACK - 1:
-                    second = ws_slot(k, [P, CHUNK], F32)[:]
-                elif k < LAG:
-                    second = second_grains()
-                else:
-                    u = t - EARLY_PLANES
-                    second = sep_grouped[k - LAG][:].bitcast(F32)[:, u * CHUNK : (u + 1) * CHUNK]
-                gather_separation(t, k, second)
-            if k < H_PASSES:
-                ws_w[k] = ws_slot(k, [P, PASS], U32)
-                quantise(ws_w[k][:], ws_s[k][:], ws_grouped[k][:].rearrange("p t m j -> p (t m j)"))
-            nc.scalar.copy(
-                sep_grouped[k][:].rearrange("p (g i t) -> p g t i", i=RUN, t=PACK),
-                sep[k][:].rearrange("p t (g i) -> p g t i", i=RUN),
+            late = list(reversed(range(EARLY_PLANES, PACK)))
+            if k == LAST:
+                rooms = [gained[0, u][:, 0, :] for u in range(2)]
+            else:
+                rooms = [crossed[(k + u) % 2][:] for u in range(2)]
+            for t, second in zip(late, rooms):
+                gather_second(t, k, second)
+            for t, second in zip(late, rooms):
+                gather_first(t, k, second)
+            grouped = sep_grouped()
+            nc.vector.tensor_copy(
+                grouped[:].rearrange("p (g i t) -> p g t i", i=LINE, t=PACK),
+                sep[k][:].rearrange("p t (g i) -> p g t i", i=LINE),
             )
             x_w = held("x_w%d" % k, [P, CHUNK], U32)
             x_s = held("x_s%d" % k, [P, CHUNK], U8)
-            quantise(x_w[:], x_s[:], sep_grouped[k][:])
+            quantise(x_w[:], x_s[:], grouped[:])
             separations[k] = (x_w, x_s)
 
         def separation_response(k):
             x_w, x_s = separations[k]
             for a in range(H_PASSES):
-                d_squares[k, a] = ring.tile([P, PACK, CHUNK], F32, name="d_sq", bufs=4)[:]
+                d_squares[k, a] = d_room()[:]
             if k == LAST:
                 for b in range(BLOCKS):
                     for a in range(H_PASSES):
-                        d = d_bank([P, PASS])
+                        d = scalar_bank()
                         nc.tensor.matmul_mx(
                             out=d[:],
                             lhsT=x_w[:, b * P : (b + 1) * P].bitcast(FP8X4), lhsT_scale=x_s[:, b * P : (b + 1) * P],
@@ -259,7 +288,7 @@ def tile_list_grain_sheath_forces_kernel(
                 return
             for a in range(H_PASSES):
                 for t0 in range(0, PACK, PER_BANK):
-                    d = d_bank([P, PER_BANK, CHUNK])
+                    d = scalar_bank()[:].rearrange("p (u j) -> p u j", u=PER_BANK)
                     for u in range(PER_BANK):
                         col = (t0 + u) * P
                         nc.tensor.matmul_mx(
@@ -268,87 +297,121 @@ def tile_list_grain_sheath_forces_kernel(
                             rhs=x_w[:].bitcast(FP8X4), rhs_scale=x_s[:],
                             start=True, stop=True,
                         )
-                    nc.scalar.activation(d_squares[k, a][:, t0 : t0 + PER_BANK, :], d[:], ACT.Square)
+                    nc.scalar.activation(d_squares[k, a][:, t0 : t0 + PER_BANK, :], d, ACT.Square)
 
-        def softening(k, a, first, width):
-            flat = soft[k, a].rearrange("p t j -> p (t j)")
-            return flat[:, PACK * first : PACK * (first + width)].rearrange("p (t j) -> p t j", t=PACK)
-
-        def soften(k):
+        def units(k):
             if k == LAST:
-                for b in range(BLOCKS):
-                    for a in range(H_PASSES):
-                        total = d_bank([P, PACK, P])
-                        for t in range(PACK):
-                            for i, term in enumerate((soft[k, a], d_squares[k, a])):
-                                nc.tensor.matmul(
-                                    total[:, t, :], turned(term)[:, b, t * P : (t + 1) * P], ident[:],
-                                    start=(i == 0), stop=(i == 1), is_transpose=True,
-                                )
-                        nc.scalar.activation(softening(k, a, b * P, P), total[:], ACT.Abs_reciprocal_sqrt, bias=1.0)
-                return
-            for a in range(H_PASSES):
-                nc.vector.tensor_tensor(soft[k, a], soft[k, a], d_squares[k, a], ALU.add)
-                nc.scalar.activation(soft[k, a], soft[k, a], ACT.Abs_reciprocal_sqrt, bias=1.0)
+                return [(b, a) for b in range(BLOCKS) for a in range(H_PASSES)]
+            return [(b, a) for a in range(H_PASSES) for b in range(BLOCKS)]
 
-        def quantise_interaction(k, first, width):
-            for a in range(H_PASSES):
-                grouped = ring.tile([P, width, PACK], BF16, name="h_grouped", align_bytes=64)
-                nc.vector.tensor_tensor(
-                    grouped[:].rearrange("p (g i) t -> p g t i", i=RUN),
-                    gained[k, a][:, :, first : first + width].rearrange("p t (g i) -> p g t i", i=RUN),
-                    softening(k, a, first, width).rearrange("p t (g i) -> p g t i", i=RUN),
-                    ALU.mult,
-                )
-                words = ring.tile([P, width], U32, name="h_w", align_bytes=64, bufs=4)
-                scales = ring.tile([P, width], U8, name="h_s", align_bytes=64, bufs=4)
-                quantise(words[:], scales[:], grouped[:].rearrange("p n t -> p (n t)"))
-                interactions[k, first, a] = (words, scales)
+        def soften(k, b, a):
+            total = scalar_bank()
+            for t in range(PACK):
+                for i, term in enumerate((c_squares[k, a], d_squares[k, a])):
+                    if k == LAST:
+                        square = turned(term)[:, b, t * P : (t + 1) * P]
+                    else:
+                        square = term[:, t, b * P : (b + 1) * P]
+                    nc.tensor.matmul(
+                        total[:, t * P : (t + 1) * P], square, ident[:],
+                        start=(i == 0), stop=(i == 1), is_transpose=True,
+                    )
+            soft = soft_room()
+            nc.scalar.activation(soft[:], total[:], ACT.Abs_reciprocal_sqrt, bias=1.0)
+            softening[k, b, a] = soft
+
+        def turn_back(k, b, a):
+            back = vector_bank()
+            for t in range(PACK):
+                cols = slice(t * P, (t + 1) * P)
+                nc.tensor.transpose(back[:, cols], softening[k, b, a][:, cols], ident[:])
+            softening[k, b, a] = back
+
+        def form_interaction(k, b, a):
+            if k == LAST or b == 0:
+                grouped_h[k, a] = h_grouped()
+            first = 0 if k == LAST else b * P
+            target = grouped_h[k, a][:, PACK * first : PACK * (first + P)]
+            nc.vector.tensor_tensor(
+                target.rearrange("p (g i t) -> p g t i", i=RUN, t=PACK),
+                softening[k, b, a][:].rearrange("p (t g i) -> p g t i", t=PACK, i=RUN),
+                gained[k, a][:, :, b * P : (b + 1) * P].rearrange("p t (g i) -> p g t i", i=RUN),
+                ALU.mult,
+            )
+
+        def quantise_interaction(k, first, width, a):
+            words, scales = h_words(), h_scales()
+            quantise(words[:, 0:width], scales[:, 0:width], grouped_h[k, a][:, 0 : PACK * width])
+            interactions[k, first, a] = (words[:, 0:width], scales[:, 0:width])
 
         def store_forces(k, first, width):
-            tiles = BANK // width
+            tiles = N_TILES // 2 if k == LAST else BANK // width
             for m0 in range(0, N_TILES, tiles):
-                count = min(tiles, N_TILES - m0)
-                y = c_or_y_bank([P, count, width])
+                y = vector_bank()[:, 0 : tiles * width].rearrange("p (u j) -> p u j", j=width)
                 for a in range(H_PASSES):
                     h_w, h_s = interactions[k, first, a]
-                    for u in range(count):
+                    for u in range(tiles):
                         col = (m0 + u) * P
                         nc.tensor.matmul_mx(
                             out=y[:, u, :],
                             lhsT=wf_w[:, a, col : col + P].bitcast(FP8X4), lhsT_scale=wf_s[:, a, col : col + P],
-                            rhs=h_w[:].bitcast(FP8X4), rhs_scale=h_s[:],
-                            start=(a == 0 and u == 0), stop=(a == H_PASSES - 1 and u == count - 1),
+                            rhs=h_w.bitcast(FP8X4), rhs_scale=h_s,
+                            start=(a == 0 and u == 0), stop=(a == H_PASSES - 1 and u == tiles - 1),
                         )
-                rows = forces(k, first, width)[:, m0 : m0 + count, :]
-                nc.vector.tensor_tensor(rows, y[:], rows, ALU.add)
+                rows = forces(k, first, width)[:, m0 : m0 + tiles, :]
+                nc.vector.tensor_tensor(rows, y, rows, ALU.add)
                 col = k * CHUNK + first
-                nc.sync.dma_start(out_rows[:, m0 : m0 + count, col : col + width], rows)
+                nc.sync.dma_start(out_rows[:, m0 : m0 + tiles, col : col + width], rows)
 
-        for half in range(CHUNKS // PER_BANK):
-            gather_species(half)
-        for a in range(H_PASSES):
-            round_ws(a)
-            species_response(0, a)
+        def interact(k):
+            for b, a in units(k):
+                soften(k, b, a)
+            for b, a in units(k):
+                turn_back(k, b, a)
+            for b, a in units(k):
+                form_interaction(k, b, a)
+            for a in range(H_PASSES):
+                quantise_interaction(k, 0, CHUNK, a)
+
+        halves = range(CHUNKS // PER_BANK)
+        gather_species_words(0)
+        for half in halves:
+            gather_species_scales(half)
+        gather_species_words(1)
+        species_response(0, 0)
+        round_ws(0)
+        round_ws(1)
+        species_response(0, 1)
+        species_response(1, 0)
         for t in range(EARLY_PLANES):
             for k in range(CHUNKS):
-                gather_separation(t, k, second_grains())
+                second = second_grains()[:]
+                gather_second(t, k, second)
+                gather_first(t, k, second)
+        quantise_ws(0)
+        quantise_ws(1)
 
-        for s in range(CHUNKS):
-            complete_separation(s)
-            if s >= 1:
-                separation_response(s - 1)
-            if s >= 2:
-                soften(s - 2)
-                species_response(1, s - 2)
-
-        work = [(k, first, width) for k in range(CHUNKS) for first, width in pieces(k)]
-        for i, piece in enumerate(work):
-            quantise_interaction(*piece)
-            if i == 0:
-                separation_response(LAST)
-            else:
-                store_forces(*work[i - 1])
-            if i < 2:
-                soften(i + 2)
-        store_forces(*work[-1])
+        for k in range(LAST):
+            complete_separation(k)
+        separation_response(0)
+        interact(0)
+        separation_response(1)
+        store_forces(0, 0, CHUNK)
+        complete_separation(LAST)
+        interact(1)
+        species_response(1, 1)
+        separation_response(2)
+        store_forces(1, 0, CHUNK)
+        interact(2)
+        for a in range(H_PASSES):
+            turned_species_response(a)
+        separation_response(LAST)
+        store_forces(2, 0, CHUNK)
+        for b, a in units(LAST):
+            soften(LAST, b, a)
+        for b in range(BLOCKS):
+            for a in range(H_PASSES):
+                form_interaction(LAST, b, a)
+                quantise_interaction(LAST, b * P, P, a)
+        for b in range(BLOCKS):
+            store_forces(LAST, b * P, P)

@@ -32,6 +32,12 @@ PER_COLUMN = 16
 RUN = 2
 LINE = 4
 EARLY_PLANES = 2
+ON_VECTOR = 3
+WS_GROUPED_ROOM = 12288
+X_ROOM = 16384
+C_ROOM = 18432
+H_ROOM = 8192
+WS_ROOM = 4096
 SCALAR_BANKS = 4
 
 
@@ -42,6 +48,7 @@ def tile_list_grain_sheath_forces_kernel(
     nc = tc.nc
     with ExitStack() as ctx:
         keep = ctx.enter_context(tc.tile_pool(name="keep", bufs=1))
+        shared = ctx.enter_context(tc.tile_pool(name="shared", bufs=1))
         psum = ctx.enter_context(tc.psum_pool(name="psum", bufs=1))
 
         def held(name, shape, dtype):
@@ -64,62 +71,66 @@ def tile_list_grain_sheath_forces_kernel(
         idx_a = keep.tile([P, S // PER_COLUMN], U16, name="idx_a")
         idx_b = keep.tile([P, S // PER_COLUMN], U16, name="idx_b")
         tab_w = held("tab_w", [P, T], U32)
-        tab_s = keep.tile([P, T], U8, name="tab_s", tag="scales_then_words", align_bytes=64)
+        tab_s = held("tab_s", [P, T], U8)
         wc_w_raw = held("wc_w_raw", [P, 2 * H], U8)
-        wc_s_raw = held("wc_s_raw", [P, H], U8)
+        wc_s_raw = shared.tile([P, H], U8, name="wc_s_raw", offset=0, align_bytes=64)
         wc_w = held("wc_w", [P, 2 * H], U8)
         wc_s = held("wc_s", [P, H], U8)
         wf_w = held("wf_w", [P, H_PASSES, N], U32)
         wf_s = held("wf_s", [P, H_PASSES, N], U8)
         planes = [held("plane%d" % t, [P, T], F32) for t in range(PACK)]
-        ws_raw = [held("ws_raw%d" % a, [P, PACK, PASS], F32) for a in range(H_PASSES)]
-        ws_grouped = [held("ws_grouped%d" % a, [P, PACK, P, PACK], BF16) for a in range(H_PASSES)]
-        ws_w = [held("ws_w%d" % a, [P, PASS], U32) for a in range(H_PASSES)]
+        ws_first = [held("ws_raw0_%d" % u, [P, PACK, PASS // 2], F32) for u in range(2)]
+        ws_second = shared.tile([P, PACK, PASS], F32, name="ws_raw1", offset=C_ROOM + 4096, align_bytes=64)
+        ws_grouped = [
+            held("ws_grouped0", [P, PACK, P, PACK], BF16),
+            shared.tile([P, PACK, P, PACK], BF16, name="ws_grouped1", offset=WS_GROUPED_ROOM, align_bytes=64),
+        ]
+        ws_w = {}
         ws_s = [held("ws_s%d" % a, [P, PASS], U8) for a in range(H_PASSES)]
         gains = held("gains", [P, H_PASSES, PACK], F32)
-        sep = [held("sep%d" % k, [P, PACK, CHUNK], F32) for k in range(CHUNKS)]
-        ident = held("ident", [P, P], F32)
-        second_grains = in_turn([held("second%d" % i, [P, CHUNK], F32) for i in range(3)])
-        crossed = [held("late_second%d" % i, [P, CHUNK], F32) for i in range(2)]
-        sep_grouped = in_turn([held("sep_grouped%d" % i, [P, CHUNK * PACK], BF16) for i in range(2)])
-        d_room = in_turn([held("d_sq%d" % i, [P, PACK, CHUNK], F32) for i in range(3)])
+        sep_halves = [held("sep%d" % h, [P, PACK, BANK], F32) for h in range(CHUNKS // PER_BANK)]
+        sep = [
+            sep_halves[k // PER_BANK][:, :, (k % PER_BANK) * CHUNK : (k % PER_BANK + 1) * CHUNK] for k in range(CHUNKS)
+        ]
+        seconds = [held("second%d" % i, [P, BANK], F32) for i in range(2)]
+        d_room = in_turn([held("d_sq%d" % i, [P, PACK, CHUNK], F32) for i in range(4)])
         soft_room = in_turn([held("soft%d" % i, [P, BANK], F32) for i in range(4)])
-        h_grouped = in_turn([held("h_grouped%d" % i, [P, CHUNK * PACK], BF16) for i in range(3)])
-        h_words = in_turn([held("h_w%d" % i, [P, CHUNK], U32) for i in range(4)])
-        h_scales = in_turn([held("h_s%d" % i, [P, CHUNK], U8) for i in range(4)])
+        h_grouped = in_turn([held("h_grouped%d" % i, [P, H_PASSES * CHUNK * PACK], BF16) for i in range(2)])
+        h_words = in_turn([held("h_w%d" % i, [P, H_PASSES * CHUNK], U32) for i in range(2)])
+        h_scales = in_turn([held("h_s%d" % i, [P, H_PASSES * CHUNK], U8) for i in range(2)])
 
-        drag_room = [held("forces%d" % k, [P, N_TILES * CHUNK], F32)[:] for k in range(CHUNKS - H_PASSES)]
-        for a in range(H_PASSES):
-            drag_room.append(ws_raw[a][:].rearrange("p t c -> p (t c)")[:, 0 : N_TILES * CHUNK])
+        drag_room = [held("forces%d" % k, [P, N_TILES * CHUNK], F32)[:] for k in range(LAST)]
 
         def pieces(k):
             width = P if k == LAST else CHUNK
             return [(first, width) for first in range(0, CHUNK, width)]
 
         def forces(k, first, width):
-            room = drag_room[k][:, N_TILES * first : N_TILES * (first + width)]
+            if k == LAST:
+                room = ws_first[first // P][:].rearrange("p t c -> p (t c)")[:, 0 : N_TILES * P]
+            else:
+                room = drag_room[k]
             return room.rearrange("p (m j) -> p m j", j=width)
 
         def load_scale_rows(queue, plane, rows):
             for q in range(4):
                 queue.dma_start(plane[32 * q : 32 * q + 4, :].bitcast(I32), rows[4 * q : 4 * q + 4, :].bitcast(I32))
 
-        nc.vector.memset(wc_s_raw[:].bitcast(I32), 0)
         nc.vector.memset(tab_s[:].bitcast(I32), 0)
+        nc.vector.memset(wc_s_raw[:].bitcast(I32), 0)
         nc.vector.memset(wf_s[:].rearrange("p a n -> p (a n)").bitcast(I32), 0)
 
         warm = held("warm", [P, 2], F32)
         nc.vector.memset(warm[:, 0:1], 1.0)
         nc.scalar.activation(warm[:, 1:2], warm[:, 0:1], ACT.Abs_reciprocal_sqrt)
-        make_identity(nc, ident[:])
 
         x_rows = xT.rearrange("(p t) c -> p t c", t=PACK)
         ws_rows = ws.rearrange("(p t) c -> p t c", t=PACK)
         drag_rows = drag.rearrange("(m p) j -> p m j", p=P)
         out_rows = out.rearrange("(m p) j -> p m j", p=P)
 
-        def load_ws(a):
-            nc.sync.dma_start(ws_raw[a][:], ws_rows[:, :, a * PASS : (a + 1) * PASS])
+        def load_ws_first(u):
+            nc.sync.dma_start(ws_first[u][:], ws_rows[:, :, u * PASS // 2 : (u + 1) * PASS // 2])
 
         def load_plane(t):
             nc.sync.dma_start(planes[t][:], x_rows[:, t, :])
@@ -130,26 +141,27 @@ def tile_list_grain_sheath_forces_kernel(
                 nc.sync.dma_start(forces(k, first, width), drag_rows[:, :, col : col + width])
 
         nc.sync.dma_start(idx_tab[:], offs)
-        load_scale_rows(nc.sync, wc_s_raw, wc_scales[0])
+        load_scale_rows(nc.sync, tab_s, tab_scales[0])
         nc.sync.dma_start(wc_w_raw[:], wc_words[0])
         nc.sync.dma_start(tab_w[:].bitcast(I32), tab_words[0].rearrange("p n t -> p (n t)").bitcast(I32))
-        load_scale_rows(nc.sync, tab_s, tab_scales[0])
+        load_scale_rows(nc.sync, wc_s_raw, wc_scales[0])
         nc.sync.dma_start(gains[:], gain.rearrange("(a p t) -> p a t", p=P, t=PACK))
+        load_ws_first(0)
         load_plane(0)
         nc.sync.dma_start(idx_b[:], offs3)
         nc.sync.dma_start(idx_a[:], offs2)
-        load_ws(0)
-        load_ws(1)
+        load_ws_first(1)
         load_plane(1)
         load_plane(2)
         load_plane(3)
+        nc.sync.dma_start(ws_second[:], ws_rows[:, :, PASS:])
         nc.sync.dma_start(wf_w[:].bitcast(I32), wf_words.rearrange("a p n t -> p a (n t)").bitcast(I32))
         for q in range(4):
             nc.sync.dma_start(
                 wf_s[32 * q : 32 * q + 4, :, :].bitcast(I32),
                 wf_scales[:, 4 * q : 4 * q + 4, :].rearrange("a r n -> r a n").bitcast(I32),
             )
-        for k in range(CHUNKS - H_PASSES):
+        for k in range(LAST):
             load_drag(k)
 
         nc.vector.tensor_copy(
@@ -161,132 +173,170 @@ def tile_list_grain_sheath_forces_kernel(
             wc_s_raw[:].rearrange("p (a m t) -> p a t m", a=H_PASSES, t=PACK),
         )
 
+        ident = keep.tile([P, P], F32, name="ident", tag="wc_w_raw", align_bytes=64)
+        make_identity(nc, ident[:])
+
         def quantise(words, scales, grouped):
             nc.vector.quantize_mx(out=words.bitcast(FP8X4), scales=scales, in_=grouped)
 
-        def round_ws(a):
-            target = ws_grouped[a][:].rearrange("p t (g i) j -> p g j i t", i=2)
-            source = ws_raw[a][:].rearrange("p j (g i t) -> p g j i t", i=2, t=PACK)
+        def round_ws_on_scalar(target, source):
+            target = target.rearrange("p t (g i) j -> p g j i t", i=2)
+            source = source.rearrange("p j (g i t) -> p g j i t", i=2, t=PACK)
             for t0 in range(0, PACK, 2):
                 nc.scalar.copy(target[:, :, :, :, t0 : t0 + 2], source[:, :, :, :, t0 : t0 + 2])
-            load_drag(CHUNKS - H_PASSES + a)
+
+        def round_ws(a):
+            if a == 0:
+                by_t = ws_first[0][:].rearrange("p j (m t) -> p t m j", t=PACK)
+                for t in range(PACK):
+                    nc.gpsimd.tensor_scalar(
+                        ws_grouped[0][:, t, 0 : P // 2, :], by_t[:, t, :, :], 1.0, 0.0, ALU.mult, ALU.add
+                    )
+                round_ws_on_scalar(ws_grouped[0][:, :, P // 2 :, :], ws_first[1][:])
+                load_drag(LAST)
+            else:
+                round_ws_on_scalar(ws_grouped[1][:], ws_second[:])
 
         def quantise_ws(a):
+            ws_w[a] = shared.tile([P, PASS], U32, name="ws_w%d" % a, offset=WS_ROOM + a * 4 * PASS, align_bytes=64)
             quantise(ws_w[a][:], ws_s[a][:], ws_grouped[a][:].rearrange("p t m j -> p (t m j)"))
 
         species = {}
+        grouped_x = {}
         c_rooms = {}
         c_squares = {}
         gained = {}
         separations = {}
         d_squares = {}
         softening = {}
-        grouped_h = {}
+        sums = {}
+        rooms_h = {}
         interactions = {}
 
-        def gather_species_scales(half):
-            cols = slice(half * BANK // PER_COLUMN, (half + 1) * BANK // PER_COLUMN)
-            v_s = held("v_s%d" % half, [P, BANK], U8)
-            nc.vector.tensor_copy(v_s[:], tab_s[:].indirect(idx_tab[:, cols]))
-            species[half, "s"] = v_s
+        def gather_species_scales():
+            v_s = held("v_s", [P, S], U8)
+            nc.vector.tensor_copy(v_s[:], tab_s[:].indirect(idx_tab[:]))
+            for half in range(CHUNKS // PER_BANK):
+                species[half, "s"] = v_s[:, half * BANK : (half + 1) * BANK]
 
         def gather_species_words(half):
             cols = slice(half * BANK // PER_COLUMN, (half + 1) * BANK // PER_COLUMN)
             if half == 0:
                 v_w = held("v_w0", [P, BANK], U32)
             else:
-                v_w = keep.tile([P, BANK], U32, name="v_w1", tag="scales_then_words", align_bytes=64)
+                v_w = shared.tile([P, BANK], U32, name="v_w1", offset=0, align_bytes=64)
             nc.vector.tensor_copy(v_w[:], tab_w[:].indirect(idx_tab[:, cols]))
             species[half, "w"] = v_w
 
         def turned(tile):
             return tile.rearrange("p t j -> p (t j)").rearrange("p (b r) -> p b r", r=PASS)
 
-        for half in range(CHUNKS // PER_BANK):
-            for a in range(H_PASSES):
-                squares = held("c_sq%d_%d" % (half, a), [P, PER_BANK, PACK, CHUNK], F32)
-                scaled = held("gained%d_%d" % (half, a), [P, PER_BANK, PACK, CHUNK], F32)
-                c_rooms[half, a] = (squares, scaled)
-                for u in range(PER_BANK):
-                    c_squares[half * PER_BANK + u, a] = squares[:, u, :, :]
-                    gained[half * PER_BANK + u, a] = scaled[:, u, :, :]
+        def c_room(half, a):
+            shape = [P, PER_BANK, PACK, CHUNK]
+            if (half, a) == (1, 0):
+                squares = shared.tile(shape, F32, name="c_sq1_0", offset=C_ROOM, align_bytes=64)
+                scaled = shared.tile(shape, F32, name="gained1_0", offset=C_ROOM + 8192, align_bytes=64)
+            else:
+                squares = held("c_sq%d_%d" % (half, a), shape, F32)
+                scaled = held("gained%d_%d" % (half, a), shape, F32)
+            for u in range(PER_BANK):
+                c_squares[half * PER_BANK + u, a] = squares[:, u, :, :]
+                gained[half * PER_BANK + u, a] = scaled[:, u, :, :]
+            return squares, scaled
 
-        def species_response(half, a):
+        def species_response(half, a, slices):
             v_w, v_s = species[half, "w"], species[half, "s"]
             squares, scaled = c_rooms[half, a]
             plain = PER_BANK - 1 if half == LAST // PER_BANK else PER_BANK
-            for t in range(PACK):
+            for t in slices:
                 bank = scalar_bank()
                 c = bank[:].rearrange("p (u j) -> p u j", u=PER_BANK)
                 col = a * PASS + t * P
                 nc.tensor.matmul_mx(
                     out=bank[:],
                     lhsT=wc_w[:, 2 * col : 2 * (col + P)].bitcast(FP4X4), lhsT_scale=wc_s[:, col : col + P],
-                    rhs=v_w[:].bitcast(FP8X4), rhs_scale=v_s[:],
+                    rhs=v_w[:].bitcast(FP8X4), rhs_scale=v_s,
                     start=True, stop=True,
                 )
                 nc.scalar.activation(squares[:, 0:plain, t, :], c[:, 0:plain, :], ACT.Square)
                 nc.scalar.activation(scaled[:, :, t, :], c, ACT.Copy, scale=gains[:, a, t : t + 1])
 
-        def turned_species_response(a):
+        def turned_species_response(b, a):
             v_w, v_s = species[LAST // PER_BANK, "w"], species[LAST // PER_BANK, "s"]
-            for b in range(BLOCKS):
-                c = scalar_bank()
-                col = (PER_BANK - 1) * CHUNK + b * P
-                nc.tensor.matmul_mx(
-                    out=c[:],
-                    lhsT=v_w[:, col : col + P].bitcast(FP8X4), lhsT_scale=v_s[:, col : col + P],
-                    rhs=wc_w[:, 2 * a * PASS : 2 * (a + 1) * PASS].bitcast(FP4X4),
-                    rhs_scale=wc_s[:, a * PASS : (a + 1) * PASS],
-                    start=True, stop=True,
-                )
-                nc.scalar.activation(turned(c_squares[LAST, a])[:, b, :], c[:], ACT.Square)
+            c = scalar_bank()
+            col = (PER_BANK - 1) * CHUNK + b * P
+            nc.tensor.matmul_mx(
+                out=c[:],
+                lhsT=v_w[:, col : col + P].bitcast(FP8X4), lhsT_scale=v_s[:, col : col + P],
+                rhs=wc_w[:, 2 * a * PASS : 2 * (a + 1) * PASS].bitcast(FP4X4),
+                rhs_scale=wc_s[:, a * PASS : (a + 1) * PASS],
+                start=True, stop=True,
+            )
+            nc.scalar.activation(turned(c_squares[LAST, a])[:, b, :], c[:], ACT.Square)
 
-        def gather_second(t, k, second):
-            cols = slice(k * CHUNK // PER_COLUMN, (k + 1) * CHUNK // PER_COLUMN)
+        def turned_separation_response(b, a):
+            x_w, x_s = separations[LAST]
+            if b == 0:
+                d_squares[LAST, a] = d_room()[:]
+            d = scalar_bank()
+            nc.tensor.matmul_mx(
+                out=d[:],
+                lhsT=x_w[:, b * P : (b + 1) * P].bitcast(FP8X4), lhsT_scale=x_s[:, b * P : (b + 1) * P],
+                rhs=ws_w[a][:].bitcast(FP8X4), rhs_scale=ws_s[a][:],
+                start=True, stop=True,
+            )
+            nc.scalar.activation(turned(d_squares[LAST, a])[:, b, :], d[:], ACT.Square)
+
+        def gather_second(t, first, count, second):
+            cols = slice(first * CHUNK // PER_COLUMN, (first + count) * CHUNK // PER_COLUMN)
             nc.vector.tensor_copy(second, planes[t][:].indirect(idx_b[:, cols]))
 
-        def gather_first(t, k, second):
-            cols = slice(k * CHUNK // PER_COLUMN, (k + 1) * CHUNK // PER_COLUMN)
-            nc.vector.tensor_tensor(sep[k][:, t, :], planes[t][:].indirect(idx_a[:, cols]), second, ALU.subtract)
+        def gather_first(t, first, count, second):
+            cols = slice(first * CHUNK // PER_COLUMN, (first + count) * CHUNK // PER_COLUMN)
+            u = first % PER_BANK
+            target = sep_halves[first // PER_BANK][:, t, u * CHUNK : (u + count) * CHUNK]
+            nc.vector.tensor_tensor(target, planes[t][:].indirect(idx_a[:, cols]), second, ALU.subtract)
 
-        def complete_separation(k):
-            late = list(reversed(range(EARLY_PLANES, PACK)))
-            if k == LAST:
-                rooms = [gained[0, u][:, 0, :] for u in range(2)]
+        def gather(jobs):
+            for job in jobs:
+                gather_second(*job)
+            for job in jobs:
+                gather_first(*job)
+
+        def interleave_separation(k):
+            if k < ON_VECTOR:
+                grouped_x[k] = held("x_grouped%d" % k, [P, CHUNK * PACK], BF16)[:]
+                nc.vector.tensor_copy(
+                    grouped_x[k].rearrange("p (g i t) -> p g t i", i=LINE, t=PACK),
+                    sep[k].rearrange("p t (g i) -> p g t i", i=LINE),
+                )
             else:
-                rooms = [crossed[(k + u) % 2][:] for u in range(2)]
-            for t, second in zip(late, rooms):
-                gather_second(t, k, second)
-            for t, second in zip(late, rooms):
-                gather_first(t, k, second)
-            grouped = sep_grouped()
-            nc.vector.tensor_copy(
-                grouped[:].rearrange("p (g i t) -> p g t i", i=LINE, t=PACK),
-                sep[k][:].rearrange("p t (g i) -> p g t i", i=LINE),
-            )
-            x_w = held("x_w%d" % k, [P, CHUNK], U32)
-            x_s = held("x_s%d" % k, [P, CHUNK], U8)
-            quantise(x_w[:], x_s[:], grouped[:])
+                room = c_squares[0, k - ON_VECTOR][:, 0:2, :]
+                grouped_x[k] = room.rearrange("p t j -> p (t j)").bitcast(BF16)
+                target = grouped_x[k].rearrange("p (j t) -> p j t", t=PACK)
+                source = sep[k].rearrange("p t j -> p j t")
+                for b in range(BLOCKS):
+                    cols = slice(b * P, (b + 1) * P)
+                    nc.gpsimd.tensor_scalar(target[:, cols, :], source[:, cols, :], 1.0, 0.0, ALU.mult, ALU.add)
+
+        def quantise_separation(k):
+            if k == 2:
+                x_w = shared.tile([P, CHUNK], U32, name="x_w2", offset=X_ROOM, align_bytes=64)
+                x_s = held("x_s%d" % k, [P, CHUNK], U8)
+            elif k < ON_VECTOR:
+                x_w = held("x_w%d" % k, [P, CHUNK], U32)
+                x_s = held("x_s%d" % k, [P, CHUNK], U8)
+            else:
+                at = H_ROOM + (k - ON_VECTOR) * 2048
+                x_w = shared.tile([P, CHUNK], U32, name="x_w%d" % k, offset=at, align_bytes=64)
+                x_s = shared.tile([P, CHUNK], U8, name="x_s%d" % k, offset=at + 1024, align_bytes=64)
+            quantise(x_w[:], x_s[:], grouped_x[k])
             separations[k] = (x_w, x_s)
 
-        def separation_response(k):
+        def separation_response(k, passes):
             x_w, x_s = separations[k]
-            for a in range(H_PASSES):
+            for a in passes:
                 d_squares[k, a] = d_room()[:]
-            if k == LAST:
-                for b in range(BLOCKS):
-                    for a in range(H_PASSES):
-                        d = scalar_bank()
-                        nc.tensor.matmul_mx(
-                            out=d[:],
-                            lhsT=x_w[:, b * P : (b + 1) * P].bitcast(FP8X4), lhsT_scale=x_s[:, b * P : (b + 1) * P],
-                            rhs=ws_w[a][:].bitcast(FP8X4), rhs_scale=ws_s[a][:],
-                            start=True, stop=True,
-                        )
-                        nc.scalar.activation(turned(d_squares[k, a])[:, b, :], d[:], ACT.Square)
-                return
-            for a in range(H_PASSES):
                 for t0 in range(0, PACK, PER_BANK):
                     d = scalar_bank()[:].rearrange("p (u j) -> p u j", u=PER_BANK)
                     for u in range(PER_BANK):
@@ -304,45 +354,84 @@ def tile_list_grain_sheath_forces_kernel(
                 return [(b, a) for b in range(BLOCKS) for a in range(H_PASSES)]
             return [(b, a) for a in range(H_PASSES) for b in range(BLOCKS)]
 
-        def soften(k, b, a):
-            total = scalar_bank()
-            for t in range(PACK):
-                for i, term in enumerate((c_squares[k, a], d_squares[k, a])):
+        def sum_squares(k, b, a):
+            total = banks[SCALAR_BANKS + units(k).index((b, a))] if k == 0 else scalar_bank()
+            for i, term in enumerate((c_squares[k, a], d_squares[k, a])):
+                for t in range(PACK):
                     if k == LAST:
                         square = turned(term)[:, b, t * P : (t + 1) * P]
                     else:
                         square = term[:, t, b * P : (b + 1) * P]
                     nc.tensor.matmul(
                         total[:, t * P : (t + 1) * P], square, ident[:],
-                        start=(i == 0), stop=(i == 1), is_transpose=True,
+                        start=(i == 0 and t == 0), stop=(i == 1 and t == PACK - 1), is_transpose=True,
                     )
+            sums[k, b, a] = total
+
+        def soften(k, b, a):
             soft = soft_room()
-            nc.scalar.activation(soft[:], total[:], ACT.Abs_reciprocal_sqrt, bias=1.0)
-            softening[k, b, a] = soft
+            nc.scalar.activation(soft[:], sums[k, b, a][:], ACT.Abs_reciprocal_sqrt, bias=1.0)
+            softening[k, b, a] = soft[:].rearrange("p (t j) -> p t j", t=PACK)
+
+        def add_squares(k, a, first=0):
+            total = c_squares[k, a][:, first:, :]
+            nc.vector.tensor_tensor(total, total, d_squares[k, a][:, first:, :], ALU.add)
+
+        def add_squares_aside(k, a, slices):
+            for t in slices:
+                nc.gpsimd.tensor_tensor(c_squares[k, a][:, t, :], c_squares[k, a][:, t, :], d_squares[k, a][:, t, :], ALU.add)
+
+        def soften_in_place(k, a):
+            nc.scalar.activation(c_squares[k, a], c_squares[k, a], ACT.Abs_reciprocal_sqrt, bias=1.0)
+            softening[k, a] = c_squares[k, a]
 
         def turn_back(k, b, a):
             back = vector_bank()
             for t in range(PACK):
                 cols = slice(t * P, (t + 1) * P)
-                nc.tensor.transpose(back[:, cols], softening[k, b, a][:, cols], ident[:])
-            softening[k, b, a] = back
+                nc.tensor.transpose(back[:, cols], softening[k, b, a][:, t, :], ident[:])
+            softening[k, b, a] = back[:].rearrange("p (t j) -> p t j", t=PACK)
 
-        def form_interaction(k, b, a):
-            if k == LAST or b == 0:
-                grouped_h[k, a] = h_grouped()
-            first = 0 if k == LAST else b * P
-            target = grouped_h[k, a][:, PACK * first : PACK * (first + P)]
+        def form_interaction(target, soft, scaled):
             nc.vector.tensor_tensor(
                 target.rearrange("p (g i t) -> p g t i", i=RUN, t=PACK),
-                softening[k, b, a][:].rearrange("p (t g i) -> p g t i", t=PACK, i=RUN),
-                gained[k, a][:, :, b * P : (b + 1) * P].rearrange("p t (g i) -> p g t i", i=RUN),
+                soft.rearrange("p t (g i) -> p g t i", i=RUN),
+                scaled.rearrange("p t (g i) -> p g t i", i=RUN),
                 ALU.mult,
             )
 
-        def quantise_interaction(k, first, width, a):
-            words, scales = h_words(), h_scales()
-            quantise(words[:, 0:width], scales[:, 0:width], grouped_h[k, a][:, 0 : PACK * width])
-            interactions[k, first, a] = (words[:, 0:width], scales[:, 0:width])
+        def open_interaction(k):
+            if k == 0:
+                grouped = shared.tile([P, H_PASSES * CHUNK * PACK], BF16, name="h_first", offset=H_ROOM, align_bytes=64)
+                words = shared.tile([P, H_PASSES * CHUNK], U32, name="h_w_first", offset=X_ROOM, align_bytes=64)
+            else:
+                grouped = h_grouped()
+                words = h_words()
+            rooms_h[k] = (grouped, words, h_scales())
+
+        def form_pass(k, a):
+            room = rooms_h[k][0][:, a * CHUNK * PACK : (a + 1) * CHUNK * PACK]
+            form_interaction(room, softening[k, a], gained[k, a])
+
+        def form_unit(k, b, a):
+            first = (units(k).index((b, a))) * P
+            room = rooms_h[k][0][:, first * PACK : (first + P) * PACK]
+            form_interaction(room, softening[k, b, a], gained[k, a][:, :, b * P : (b + 1) * P])
+
+        def quantise_chunk(k):
+            grouped, words, scales = rooms_h[k]
+            quantise(words[:], scales[:], grouped[:])
+            for a in range(H_PASSES):
+                cols = slice(a * CHUNK, (a + 1) * CHUNK)
+                interactions[k, 0, a] = (words[:, cols], scales[:, cols])
+
+        def quantise_block(b):
+            grouped, words, scales = rooms_h[LAST]
+            cols = slice(b * CHUNK, (b + 1) * CHUNK)
+            quantise(words[:, cols], scales[:, cols], grouped[:, b * CHUNK * PACK : (b + 1) * CHUNK * PACK])
+            for a in range(H_PASSES):
+                cols = slice(b * CHUNK + a * P, b * CHUNK + (a + 1) * P)
+                interactions[LAST, b * P, a] = (words[:, cols], scales[:, cols])
 
         def store_forces(k, first, width):
             tiles = N_TILES // 2 if k == LAST else BANK // width
@@ -363,55 +452,104 @@ def tile_list_grain_sheath_forces_kernel(
                 col = k * CHUNK + first
                 nc.sync.dma_start(out_rows[:, m0 : m0 + tiles, col : col + width], rows)
 
-        def interact(k):
+        def sum_by_transposes(k):
+            for b, a in units(k):
+                sum_squares(k, b, a)
+
+        def soften_sums(k):
             for b, a in units(k):
                 soften(k, b, a)
+
+        def turn_chunk_back(k):
             for b, a in units(k):
                 turn_back(k, b, a)
-            for b, a in units(k):
-                form_interaction(k, b, a)
-            for a in range(H_PASSES):
-                quantise_interaction(k, 0, CHUNK, a)
 
         halves = range(CHUNKS // PER_BANK)
-        gather_species_words(0)
+        gather_species_scales()
         for half in halves:
-            gather_species_scales(half)
-        gather_species_words(1)
-        species_response(0, 0)
+            gather_species_words(half)
+        every = range(PACK)
+        for room in ((0, 0), (0, 1), (1, 1)):
+            c_rooms[room] = c_room(*room)
+        species_response(0, 0, every)
         round_ws(0)
+        species_response(0, 1, every)
         round_ws(1)
-        species_response(0, 1)
-        species_response(1, 0)
-        for t in range(EARLY_PLANES):
-            for k in range(CHUNKS):
-                second = second_grains()[:]
-                gather_second(t, k, second)
-                gather_first(t, k, second)
+        c_rooms[1, 0] = c_room(1, 0)
+        gather([(0, PER_BANK * half, PER_BANK, seconds[half][:]) for half in halves])
+        gather([(1, 0, PER_BANK, shared.tile([P, BANK], F32, name="ws_second", offset=WS_ROOM, align_bytes=64)[:])])
         quantise_ws(0)
-        quantise_ws(1)
+        for k in range(PER_BANK):
+            if k == 0:
+                rooms = [seconds[0][:, u * CHUNK : (u + 1) * CHUNK] for u in range(2)]
+            else:
+                late = shared.tile([P, BANK], F32, name="late_second", offset=WS_GROUPED_ROOM, align_bytes=64)
+                rooms = [late[:, u * CHUNK : (u + 1) * CHUNK] for u in range(2)]
+            gather([(3, k, 1, rooms[0]), (2, k, 1, rooms[1])])
+            interleave_separation(k)
+            quantise_separation(k)
+            if k == 0:
+                quantise_ws(1)
+            gather([(1, PER_BANK + k, 1, rooms[0] if k == 0 else sep[0][:, 2, :])])
+        gather([(3, PER_BANK, PER_BANK, sep_halves[0][:, 0, :]), (2, PER_BANK, PER_BANK, sep_halves[0][:, 1, :])])
 
-        for k in range(LAST):
-            complete_separation(k)
-        separation_response(0)
-        interact(0)
-        separation_response(1)
+        both = range(H_PASSES)
+        last = units(LAST)
+        for b in range(BLOCKS):
+            turned_species_response(b, 1)
+        separation_response(0, [0])
+        species_response(1, 0, [0, 1])
+        separation_response(0, [1])
+        sum_by_transposes(0)
+        species_response(1, 0, [2, 3])
+        soften_sums(0)
+        separation_response(1, both)
+        turn_chunk_back(0)
+        species_response(1, 1, every)
+        interleave_separation(2)
+        add_squares(1, 0)
+        quantise_separation(2)
+        add_squares(1, 1)
+        for b in range(BLOCKS):
+            turned_species_response(b, 0)
+        for a in both:
+            soften_in_place(1, a)
+        separation_response(2, both)
+        interleave_separation(LAST)
+        open_interaction(0)
+        for unit in units(0):
+            form_unit(0, *unit)
+        quantise_chunk(0)
+        quantise_separation(LAST)
+        add_squares_aside(2, 0, every)
+        add_squares_aside(2, 1, [0, 1])
+        open_interaction(1)
+        for a in both:
+            form_pass(1, a)
+        quantise_chunk(1)
         store_forces(0, 0, CHUNK)
-        complete_separation(LAST)
-        interact(1)
-        species_response(1, 1)
-        separation_response(2)
+        for unit in last:
+            turned_separation_response(*unit)
         store_forces(1, 0, CHUNK)
-        interact(2)
-        for a in range(H_PASSES):
-            turned_species_response(a)
-        separation_response(LAST)
+        sum_by_transposes(LAST)
+        add_squares(2, 1, 2)
+        soften_in_place(2, 0)
+        for unit in last[:2]:
+            soften(LAST, *unit)
+        soften_in_place(2, 1)
+        for unit in last[2:]:
+            soften(LAST, *unit)
+        open_interaction(2)
+        open_interaction(LAST)
+        form_pass(2, 0)
+        for unit in last[:2]:
+            form_unit(LAST, *unit)
+        form_pass(2, 1)
+        quantise_block(0)
+        quantise_chunk(2)
+        for unit in last[2:]:
+            form_unit(LAST, *unit)
+        store_forces(LAST, 0, P)
+        quantise_block(1)
         store_forces(2, 0, CHUNK)
-        for b, a in units(LAST):
-            soften(LAST, b, a)
-        for b in range(BLOCKS):
-            for a in range(H_PASSES):
-                form_interaction(LAST, b, a)
-                quantise_interaction(LAST, b * P, P, a)
-        for b in range(BLOCKS):
-            store_forces(LAST, b * P, P)
+        store_forces(LAST, P, P)

@@ -32,7 +32,7 @@ PER_COLUMN = 16
 RUN = 2
 LINE = 4
 EARLY_PLANES = 2
-ON_VECTOR = 3
+ON_VECTOR = 2
 WS_GROUPED_ROOM = 12288
 X_ROOM = 16384
 C_ROOM = 18432
@@ -64,8 +64,14 @@ def tile_list_grain_sheath_forces_kernel(
             return take
 
         banks = [psum.tile([P, BANK], F32, name="bank%d" % i) for i in range(8)]
-        scalar_bank = in_turn(banks[:SCALAR_BANKS])
-        vector_bank = in_turn(banks[SCALAR_BANKS:])
+        rings = {"scalar": in_turn(banks[:SCALAR_BANKS]), "vector": in_turn(banks[:3])}
+
+        def scalar_bank():
+            return rings["scalar"]()
+
+        def vector_bank():
+            return rings["vector"]()
+
 
         idx_tab = keep.tile([P, S // PER_COLUMN], U16, name="idx_tab")
         idx_a = keep.tile([P, S // PER_COLUMN], U16, name="idx_a")
@@ -80,7 +86,7 @@ def tile_list_grain_sheath_forces_kernel(
         wf_s = held("wf_s", [P, H_PASSES, N], U8)
         planes = [held("plane%d" % t, [P, T], F32) for t in range(PACK)]
         ws_first = [held("ws_raw0_%d" % u, [P, PACK, PASS // 2], F32) for u in range(2)]
-        ws_second = shared.tile([P, PACK, PASS], F32, name="ws_raw1", offset=C_ROOM + 4096, align_bytes=64)
+        ws_second = shared.tile([P, PACK, PASS], F32, name="ws_raw1", offset=C_ROOM + 6144, align_bytes=64)
         ws_grouped = [
             held("ws_grouped0", [P, PACK, P, PACK], BF16),
             shared.tile([P, PACK, P, PACK], BF16, name="ws_grouped1", offset=WS_GROUPED_ROOM, align_bytes=64),
@@ -93,7 +99,7 @@ def tile_list_grain_sheath_forces_kernel(
             sep_halves[k // PER_BANK][:, :, (k % PER_BANK) * CHUNK : (k % PER_BANK + 1) * CHUNK] for k in range(CHUNKS)
         ]
         seconds = [held("second%d" % i, [P, BANK], F32) for i in range(2)]
-        d_room = in_turn([held("d_sq%d" % i, [P, PACK, CHUNK], F32) for i in range(4)])
+        d_rooms = {}
         soft_room = in_turn([held("soft%d" % i, [P, BANK], F32) for i in range(4)])
         h_grouped = in_turn([held("h_grouped%d" % i, [P, H_PASSES * CHUNK * PACK], BF16) for i in range(2)])
         h_words = in_turn([held("h_w%d" % i, [P, H_PASSES * CHUNK], U32) for i in range(2)])
@@ -187,11 +193,7 @@ def tile_list_grain_sheath_forces_kernel(
 
         def round_ws(a):
             if a == 0:
-                by_t = ws_first[0][:].rearrange("p j (m t) -> p t m j", t=PACK)
-                for t in range(PACK):
-                    nc.gpsimd.tensor_scalar(
-                        ws_grouped[0][:, t, 0 : P // 2, :], by_t[:, t, :, :], 1.0, 0.0, ALU.mult, ALU.add
-                    )
+                round_ws_on_scalar(ws_grouped[0][:, :, 0 : P // 2, :], ws_first[0][:])
                 round_ws_on_scalar(ws_grouped[0][:, :, P // 2 :, :], ws_first[1][:])
                 load_drag(LAST)
             else:
@@ -228,6 +230,17 @@ def tile_list_grain_sheath_forces_kernel(
             nc.vector.tensor_copy(v_w[:], tab_w[:].indirect(idx_tab[:, cols]))
             species[half, "w"] = v_w
 
+        d_turn = in_turn(list(range(4)))
+
+        def d_room():
+            i = d_turn()
+            if i not in d_rooms:
+                if i == 0:
+                    d_rooms[i] = shared.tile([P, PACK, CHUNK], F32, name="d_sq0", offset=C_ROOM + 8192, align_bytes=64)
+                else:
+                    d_rooms[i] = held("d_sq%d" % i, [P, PACK, CHUNK], F32)
+            return d_rooms[i]
+
         def turned(tile):
             return tile.rearrange("p t j -> p (t j)").rearrange("p (b r) -> p b r", r=PASS)
 
@@ -235,7 +248,7 @@ def tile_list_grain_sheath_forces_kernel(
             shape = [P, PER_BANK, PACK, CHUNK]
             if (half, a) == (1, 0):
                 squares = shared.tile(shape, F32, name="c_sq1_0", offset=C_ROOM, align_bytes=64)
-                scaled = shared.tile(shape, F32, name="gained1_0", offset=C_ROOM + 8192, align_bytes=64)
+                scaled = shared.tile(shape, F32, name="gained1_0", offset=C_ROOM + 12288, align_bytes=64)
             else:
                 squares = held("c_sq%d_%d" % (half, a), shape, F32)
                 scaled = held("gained%d_%d" % (half, a), shape, F32)
@@ -313,17 +326,13 @@ def tile_list_grain_sheath_forces_kernel(
             else:
                 room = c_squares[0, k - ON_VECTOR][:, 0:2, :]
                 grouped_x[k] = room.rearrange("p t j -> p (t j)").bitcast(BF16)
-                target = grouped_x[k].rearrange("p (j t) -> p j t", t=PACK)
-                source = sep[k].rearrange("p t j -> p j t")
-                for b in range(BLOCKS):
-                    cols = slice(b * P, (b + 1) * P)
-                    nc.gpsimd.tensor_scalar(target[:, cols, :], source[:, cols, :], 1.0, 0.0, ALU.mult, ALU.add)
+                nc.scalar.copy(
+                    grouped_x[k].rearrange("p (g i t) -> p g t i", i=RUN, t=PACK),
+                    sep[k].rearrange("p t (g i) -> p g t i", i=RUN),
+                )
 
         def quantise_separation(k):
-            if k == 2:
-                x_w = shared.tile([P, CHUNK], U32, name="x_w2", offset=X_ROOM, align_bytes=64)
-                x_s = held("x_s%d" % k, [P, CHUNK], U8)
-            elif k < ON_VECTOR:
+            if k < ON_VECTOR:
                 x_w = held("x_w%d" % k, [P, CHUNK], U32)
                 x_s = held("x_s%d" % k, [P, CHUNK], U8)
             else:
@@ -377,16 +386,12 @@ def tile_list_grain_sheath_forces_kernel(
             total = c_squares[k, a][:, first:, :]
             nc.vector.tensor_tensor(total, total, d_squares[k, a][:, first:, :], ALU.add)
 
-        def add_squares_aside(k, a, slices):
-            for t in slices:
-                nc.gpsimd.tensor_tensor(c_squares[k, a][:, t, :], c_squares[k, a][:, t, :], d_squares[k, a][:, t, :], ALU.add)
-
         def soften_in_place(k, a):
             nc.scalar.activation(c_squares[k, a], c_squares[k, a], ACT.Abs_reciprocal_sqrt, bias=1.0)
             softening[k, a] = c_squares[k, a]
 
         def turn_back(k, b, a):
-            back = vector_bank()
+            back = sums[k, b, a]
             for t in range(PACK):
                 cols = slice(t * P, (t + 1) * P)
                 nc.tensor.transpose(back[:, cols], softening[k, b, a][:, t, :], ident[:])
@@ -403,11 +408,9 @@ def tile_list_grain_sheath_forces_kernel(
         def open_interaction(k):
             if k == 0:
                 grouped = shared.tile([P, H_PASSES * CHUNK * PACK], BF16, name="h_first", offset=H_ROOM, align_bytes=64)
-                words = shared.tile([P, H_PASSES * CHUNK], U32, name="h_w_first", offset=X_ROOM, align_bytes=64)
             else:
                 grouped = h_grouped()
-                words = h_words()
-            rooms_h[k] = (grouped, words, h_scales())
+            rooms_h[k] = (grouped, h_words(), h_scales())
 
         def form_pass(k, a):
             room = rooms_h[k][0][:, a * CHUNK * PACK : (a + 1) * CHUNK * PACK]
@@ -505,51 +508,52 @@ def tile_list_grain_sheath_forces_kernel(
         soften_sums(0)
         separation_response(1, both)
         turn_chunk_back(0)
-        species_response(1, 1, every)
         interleave_separation(2)
-        add_squares(1, 0)
-        quantise_separation(2)
-        add_squares(1, 1)
-        for b in range(BLOCKS):
-            turned_species_response(b, 0)
-        for a in both:
-            soften_in_place(1, a)
-        separation_response(2, both)
-        interleave_separation(LAST)
+        species_response(1, 1, [0, 1])
         open_interaction(0)
         for unit in units(0):
             form_unit(0, *unit)
+        for a in both:
+            add_squares(1, a)
         quantise_chunk(0)
-        quantise_separation(LAST)
-        add_squares_aside(2, 0, every)
-        add_squares_aside(2, 1, [0, 1])
+        quantise_separation(2)
+        for a in both:
+            soften_in_place(1, a)
+        rings["scalar"] = in_turn(banks[SCALAR_BANKS:] + [banks[3]])
+        separation_response(2, [0])
+        interleave_separation(LAST)
+        species_response(1, 1, [2, 3])
+        separation_response(2, [1])
         open_interaction(1)
         for a in both:
             form_pass(1, a)
-        quantise_chunk(1)
+        quantise_separation(LAST)
         store_forces(0, 0, CHUNK)
-        for unit in last:
+        quantise_chunk(1)
+        for a in both:
+            add_squares(2, a)
+        for b in range(BLOCKS):
+            turned_species_response(b, 0)
+        soften_in_place(2, 0)
+        for unit in last[:2]:
+            turned_separation_response(*unit)
+        soften_in_place(2, 1)
+        for unit in last[2:]:
             turned_separation_response(*unit)
         store_forces(1, 0, CHUNK)
         sum_by_transposes(LAST)
-        add_squares(2, 1, 2)
-        soften_in_place(2, 0)
-        for unit in last[:2]:
-            soften(LAST, *unit)
-        soften_in_place(2, 1)
-        for unit in last[2:]:
-            soften(LAST, *unit)
+        soften_sums(LAST)
         open_interaction(2)
         open_interaction(LAST)
-        form_pass(2, 0)
+        for a in both:
+            form_pass(2, a)
         for unit in last[:2]:
             form_unit(LAST, *unit)
-        form_pass(2, 1)
-        quantise_block(0)
         quantise_chunk(2)
+        quantise_block(0)
         for unit in last[2:]:
             form_unit(LAST, *unit)
-        store_forces(LAST, 0, P)
-        quantise_block(1)
         store_forces(2, 0, CHUNK)
+        quantise_block(1)
+        store_forces(LAST, 0, P)
         store_forces(LAST, P, P)

@@ -30,7 +30,6 @@ BLOCKS = CHUNK // P
 N_TILES = N // P
 PER_COLUMN = 16
 RUN = 2
-LINE = 4
 EARLY_PLANES = 2
 ON_VECTOR = 2
 WS_GROUPED_ROOM = 12288
@@ -320,8 +319,8 @@ def tile_list_grain_sheath_forces_kernel(
             if k < ON_VECTOR:
                 grouped_x[k] = held("x_grouped%d" % k, [P, CHUNK * PACK], BF16)[:]
                 nc.vector.tensor_copy(
-                    grouped_x[k].rearrange("p (g i t) -> p g t i", i=LINE, t=PACK),
-                    sep[k].rearrange("p t (g i) -> p g t i", i=LINE),
+                    grouped_x[k].rearrange("p (g i t) -> p g t i", i=RUN, t=PACK),
+                    sep[k].rearrange("p t (g i) -> p g t i", i=RUN),
                 )
             else:
                 room = c_squares[0, k - ON_VECTOR][:, 0:2, :]

@@ -31,7 +31,7 @@ N_TILES = N // P
 PER_COLUMN = 16
 RUN = 2
 EARLY_PLANES = 2
-ON_VECTOR = 2
+ON_VECTOR = 4
 WS_GROUPED_ROOM = 12288
 X_ROOM = 16384
 C_ROOM = 18432
@@ -63,7 +63,7 @@ def tile_list_grain_sheath_forces_kernel(
             return take
 
         banks = [psum.tile([P, BANK], F32, name="bank%d" % i) for i in range(8)]
-        rings = {"scalar": in_turn(banks[:SCALAR_BANKS]), "vector": in_turn(banks[:3])}
+        rings = {"scalar": in_turn(banks[:SCALAR_BANKS]), "vector": in_turn(banks[:2])}
 
         def scalar_bank():
             return rings["scalar"]()
@@ -204,6 +204,7 @@ def tile_list_grain_sheath_forces_kernel(
 
         species = {}
         grouped_x = {}
+        x_rooms = [held("x_grouped%d" % u, [P, CHUNK * PACK], BF16) for u in range(PER_BANK)]
         c_rooms = {}
         c_squares = {}
         gained = {}
@@ -317,7 +318,7 @@ def tile_list_grain_sheath_forces_kernel(
 
         def interleave_separation(k):
             if k < ON_VECTOR:
-                grouped_x[k] = held("x_grouped%d" % k, [P, CHUNK * PACK], BF16)[:]
+                grouped_x[k] = x_rooms[k % PER_BANK][:]
                 nc.vector.tensor_copy(
                     grouped_x[k].rearrange("p (g i t) -> p g t i", i=RUN, t=PACK),
                     sep[k].rearrange("p t (g i) -> p g t i", i=RUN),
@@ -363,7 +364,12 @@ def tile_list_grain_sheath_forces_kernel(
             return [(b, a) for a in range(H_PASSES) for b in range(BLOCKS)]
 
         def sum_squares(k, b, a):
-            total = banks[SCALAR_BANKS + units(k).index((b, a))] if k == 0 else scalar_bank()
+            if k == 0:
+                total = banks[SCALAR_BANKS + units(k).index((b, a))]
+            elif k == 1:
+                total = banks[b]
+            else:
+                total = scalar_bank()
             for i, term in enumerate((c_squares[k, a], d_squares[k, a])):
                 for t in range(PACK):
                     if k == LAST:
@@ -435,9 +441,9 @@ def tile_list_grain_sheath_forces_kernel(
                 cols = slice(b * CHUNK + a * P, b * CHUNK + (a + 1) * P)
                 interactions[LAST, b * P, a] = (words[:, cols], scales[:, cols])
 
-        def store_forces(k, first, width):
+        def store_forces(k, first, width, parts):
             tiles = N_TILES // 2 if k == LAST else BANK // width
-            for m0 in range(0, N_TILES, tiles):
+            for m0 in [part * tiles for part in parts]:
                 y = vector_bank()[:, 0 : tiles * width].rearrange("p (u j) -> p u j", j=width)
                 for a in range(H_PASSES):
                     h_w, h_s = interactions[k, first, a]
@@ -479,80 +485,76 @@ def tile_list_grain_sheath_forces_kernel(
         round_ws(1)
         c_rooms[1, 0] = c_room(1, 0)
         gather([(0, PER_BANK * half, PER_BANK, seconds[half][:]) for half in halves])
-        gather([(1, 0, PER_BANK, shared.tile([P, BANK], F32, name="ws_second", offset=WS_ROOM, align_bytes=64)[:])])
+        room = shared.tile([P, BANK], F32, name="ws_second", offset=WS_ROOM, align_bytes=64)
+        gather([(1, 0, PER_BANK, room[:]), (1, PER_BANK, PER_BANK, seconds[0][:])])
         quantise_ws(0)
+        gather([(2, 0, PER_BANK, seconds[1][:]), (3, 0, PER_BANK, seconds[0][:])])
         for k in range(PER_BANK):
-            if k == 0:
-                rooms = [seconds[0][:, u * CHUNK : (u + 1) * CHUNK] for u in range(2)]
-            else:
-                late = shared.tile([P, BANK], F32, name="late_second", offset=WS_GROUPED_ROOM, align_bytes=64)
-                rooms = [late[:, u * CHUNK : (u + 1) * CHUNK] for u in range(2)]
-            gather([(3, k, 1, rooms[0]), (2, k, 1, rooms[1])])
             interleave_separation(k)
+        for k in range(PER_BANK):
             quantise_separation(k)
-            if k == 0:
-                quantise_ws(1)
-            gather([(1, PER_BANK + k, 1, rooms[0] if k == 0 else sep[0][:, 2, :])])
-        gather([(3, PER_BANK, PER_BANK, sep_halves[0][:, 0, :]), (2, PER_BANK, PER_BANK, sep_halves[0][:, 1, :])])
+        quantise_ws(1)
+        late = shared.tile([P, 2, BANK], F32, name="late_second", offset=WS_GROUPED_ROOM, align_bytes=64)
+        gather([(2, PER_BANK, PER_BANK, late[:, 0, :]), (3, PER_BANK, PER_BANK, late[:, 1, :])])
+
+        for k in range(PER_BANK, CHUNKS):
+            interleave_separation(k)
+        for k in range(PER_BANK, CHUNKS):
+            quantise_separation(k)
 
         both = range(H_PASSES)
         last = units(LAST)
         for b in range(BLOCKS):
             turned_species_response(b, 1)
-        separation_response(0, [0])
-        species_response(1, 0, [0, 1])
-        separation_response(0, [1])
+        species_response(1, 0, every)
+        separation_response(0, both)
         sum_by_transposes(0)
-        species_response(1, 0, [2, 3])
-        soften_sums(0)
         separation_response(1, both)
+        soften_sums(0)
         turn_chunk_back(0)
-        interleave_separation(2)
-        species_response(1, 1, [0, 1])
         open_interaction(0)
         for unit in units(0):
             form_unit(0, *unit)
         for a in both:
             add_squares(1, a)
-        quantise_chunk(0)
-        quantise_separation(2)
+        species_response(1, 1, [0])
+        turned_species_response(0, 0)
         for a in both:
             soften_in_place(1, a)
-        rings["scalar"] = in_turn(banks[SCALAR_BANKS:] + [banks[3]])
+        quantise_chunk(0)
+        rings["scalar"] = in_turn(banks[SCALAR_BANKS:] + [banks[2], banks[3]])
         separation_response(2, [0])
-        interleave_separation(LAST)
-        species_response(1, 1, [2, 3])
+        species_response(1, 1, [1, 2, 3])
         separation_response(2, [1])
         open_interaction(1)
         for a in both:
             form_pass(1, a)
-        quantise_separation(LAST)
-        store_forces(0, 0, CHUNK)
+        add_squares(2, 0)
         quantise_chunk(1)
-        for a in both:
-            add_squares(2, a)
-        for b in range(BLOCKS):
-            turned_species_response(b, 0)
         soften_in_place(2, 0)
-        for unit in last[:2]:
-            turned_separation_response(*unit)
+        store_forces(0, 0, CHUNK, [0])
+        add_squares(2, 1)
+        turned_species_response(1, 0)
         soften_in_place(2, 1)
-        for unit in last[2:]:
+        for unit in last:
             turned_separation_response(*unit)
-        store_forces(1, 0, CHUNK)
+        open_interaction(2)
+        store_forces(0, 0, CHUNK, [1])
+        form_pass(2, 0)
+        store_forces(0, 0, CHUNK, [2])
+        form_pass(2, 1)
+        store_forces(1, 0, CHUNK, [0])
+        quantise_chunk(2)
+        store_forces(1, 0, CHUNK, [1, 2])
         sum_by_transposes(LAST)
         soften_sums(LAST)
-        open_interaction(2)
         open_interaction(LAST)
-        for a in both:
-            form_pass(2, a)
-        for unit in last[:2]:
+        for i, unit in enumerate(last):
+            if i < 3:
+                store_forces(2, 0, CHUNK, [i])
             form_unit(LAST, *unit)
-        quantise_chunk(2)
-        quantise_block(0)
-        for unit in last[2:]:
-            form_unit(LAST, *unit)
-        store_forces(2, 0, CHUNK)
-        quantise_block(1)
-        store_forces(LAST, 0, P)
-        store_forces(LAST, P, P)
+            if i % 2 == 1:
+                quantise_block(i // 2)
+        rings["vector"] = in_turn(banks[2:6])
+        store_forces(LAST, 0, P, [0, 1])
+        store_forces(LAST, P, P, [0, 1])

@@ -84,7 +84,7 @@ def tile_list_grain_sheath_forces_kernel(
         wf_w = held("wf_w", [P, H_PASSES, N], U32)
         wf_s = held("wf_s", [P, H_PASSES, N], U8)
         planes = [held("plane%d" % t, [P, T], F32) for t in range(PACK)]
-        ws_first = [held("ws_raw0_%d" % u, [P, PACK, PASS // 2], F32) for u in range(2)]
+        ws_first = held("ws_raw0", [P, PACK, PASS], F32)
         ws_second = shared.tile([P, PACK, PASS], F32, name="ws_raw1", offset=C_ROOM + 6144, align_bytes=64)
         ws_grouped = [
             held("ws_grouped0", [P, PACK, P, PACK], BF16),
@@ -112,7 +112,7 @@ def tile_list_grain_sheath_forces_kernel(
 
         def forces(k, first, width):
             if k == LAST:
-                room = ws_first[first // P][:].rearrange("p t c -> p (t c)")[:, 0 : N_TILES * P]
+                room = ws_first[:].rearrange("p t c -> p (t c)")[:, N_TILES * first : N_TILES * (first + width)]
             else:
                 room = drag_room[k]
             return room.rearrange("p (m j) -> p m j", j=width)
@@ -121,21 +121,20 @@ def tile_list_grain_sheath_forces_kernel(
             for q in range(4):
                 queue.dma_start(plane[32 * q : 32 * q + 4, :].bitcast(I32), rows[4 * q : 4 * q + 4, :].bitcast(I32))
 
-        nc.vector.memset(tab_s[:].bitcast(I32), 0)
-        nc.vector.memset(wc_s_raw[:].bitcast(I32), 0)
-        nc.vector.memset(wf_s[:].rearrange("p a n -> p (a n)").bitcast(I32), 0)
+        nc.gpsimd.memset(tab_s[:].bitcast(I32), 0)
+        nc.gpsimd.memset(wc_s_raw[:].bitcast(I32), 0)
 
         warm = held("warm", [P, 2], F32)
-        nc.vector.memset(warm[:, 0:1], 1.0)
+        nc.gpsimd.memset(warm[:, 0:1], 1.0)
         nc.scalar.activation(warm[:, 1:2], warm[:, 0:1], ACT.Abs_reciprocal_sqrt)
+        ident = held("ident", [P, P], F32)
+        make_identity(nc, ident[:])
+        nc.gpsimd.memset(wf_s[:].rearrange("p a n -> p (a n)").bitcast(I32), 0)
 
         x_rows = xT.rearrange("(p t) c -> p t c", t=PACK)
         ws_rows = ws.rearrange("(p t) c -> p t c", t=PACK)
         drag_rows = drag.rearrange("(m p) j -> p m j", p=P)
         out_rows = out.rearrange("(m p) j -> p m j", p=P)
-
-        def load_ws_first(u):
-            nc.sync.dma_start(ws_first[u][:], ws_rows[:, :, u * PASS // 2 : (u + 1) * PASS // 2])
 
         def load_plane(t):
             nc.sync.dma_start(planes[t][:], x_rows[:, t, :])
@@ -151,11 +150,10 @@ def tile_list_grain_sheath_forces_kernel(
         nc.sync.dma_start(tab_w[:].bitcast(I32), tab_words[0].rearrange("p n t -> p (n t)").bitcast(I32))
         load_scale_rows(nc.sync, wc_s_raw, wc_scales[0])
         nc.sync.dma_start(gains[:], gain.rearrange("(a p t) -> p a t", p=P, t=PACK))
-        load_ws_first(0)
         load_plane(0)
         nc.sync.dma_start(idx_b[:], offs3)
         nc.sync.dma_start(idx_a[:], offs2)
-        load_ws_first(1)
+        nc.sync.dma_start(ws_first[:], ws_rows[:, :, 0:PASS])
         load_plane(1)
         load_plane(2)
         load_plane(3)
@@ -178,9 +176,6 @@ def tile_list_grain_sheath_forces_kernel(
             wc_s_raw[:].rearrange("p (a m t) -> p a t m", a=H_PASSES, t=PACK),
         )
 
-        ident = keep.tile([P, P], F32, name="ident", tag="wc_w_raw", align_bytes=64)
-        make_identity(nc, ident[:])
-
         def quantise(words, scales, grouped):
             nc.vector.quantize_mx(out=words.bitcast(FP8X4), scales=scales, in_=grouped)
 
@@ -192,8 +187,7 @@ def tile_list_grain_sheath_forces_kernel(
 
         def round_ws(a):
             if a == 0:
-                round_ws_on_scalar(ws_grouped[0][:, :, 0 : P // 2, :], ws_first[0][:])
-                round_ws_on_scalar(ws_grouped[0][:, :, P // 2 :, :], ws_first[1][:])
+                round_ws_on_scalar(ws_grouped[0][:], ws_first[:])
                 load_drag(LAST)
             else:
                 round_ws_on_scalar(ws_grouped[1][:], ws_second[:])
@@ -549,12 +543,12 @@ def tile_list_grain_sheath_forces_kernel(
         sum_by_transposes(LAST)
         soften_sums(LAST)
         open_interaction(LAST)
-        for i, unit in enumerate(last):
-            if i < 3:
-                store_forces(2, 0, CHUNK, [i])
-            form_unit(LAST, *unit)
-            if i % 2 == 1:
-                quantise_block(i // 2)
+        for b in range(BLOCKS):
+            for a in both:
+                form_unit(LAST, b, a)
+            quantise_block(b)
+            store_forces(2, 0, CHUNK, [b])
+        store_forces(2, 0, CHUNK, [2])
         rings["vector"] = in_turn(banks[2:6])
         store_forces(LAST, 0, P, [0, 1])
         store_forces(LAST, P, P, [0, 1])

@@ -31,7 +31,7 @@ N_TILES = N // P
 PER_COLUMN = 16
 RUN = 2
 EARLY_PLANES = 2
-ON_VECTOR = 4
+ON_VECTOR = 2
 WS_GROUPED_ROOM = 12288
 X_ROOM = 16384
 C_ROOM = 18432
@@ -360,8 +360,8 @@ def tile_list_grain_sheath_forces_kernel(
         def sum_squares(k, b, a):
             if k == 0:
                 total = banks[SCALAR_BANKS + units(k).index((b, a))]
-            elif k == 1:
-                total = banks[b]
+            elif k == 2:
+                total = banks[2 + b]
             else:
                 total = scalar_bank()
             for i, term in enumerate((c_squares[k, a], d_squares[k, a])):
@@ -491,64 +491,75 @@ def tile_list_grain_sheath_forces_kernel(
         late = shared.tile([P, 2, BANK], F32, name="late_second", offset=WS_GROUPED_ROOM, align_bytes=64)
         gather([(2, PER_BANK, PER_BANK, late[:, 0, :]), (3, PER_BANK, PER_BANK, late[:, 1, :])])
 
-        for k in range(PER_BANK, CHUNKS):
-            interleave_separation(k)
-        for k in range(PER_BANK, CHUNKS):
-            quantise_separation(k)
 
         both = range(H_PASSES)
         last = units(LAST)
         for b in range(BLOCKS):
             turned_species_response(b, 1)
         species_response(1, 0, every)
+        species_response(1, 1, [0])
         separation_response(0, both)
         sum_by_transposes(0)
-        separation_response(1, both)
+        species_response(1, 1, [1])
         soften_sums(0)
         turn_chunk_back(0)
+        separation_response(1, both)
         open_interaction(0)
         for unit in units(0):
             form_unit(0, *unit)
-        for a in both:
-            add_squares(1, a)
-        species_response(1, 1, [0])
-        turned_species_response(0, 0)
-        for a in both:
-            soften_in_place(1, a)
+        interleave_separation(2)
+        add_squares(1, 0)
         quantise_chunk(0)
-        rings["scalar"] = in_turn(banks[SCALAR_BANKS:] + [banks[2], banks[3]])
+        add_squares(1, 1)
+        quantise_separation(2)
+        soften_in_place(1, 0)
+        interleave_separation(LAST)
+        soften_in_place(1, 1)
+        quantise_separation(LAST)
+        rings["scalar"] = in_turn(banks[SCALAR_BANKS:])
         separation_response(2, [0])
-        species_response(1, 1, [1, 2, 3])
+        for b in range(BLOCKS):
+            sum_squares(2, b, 0)
+        species_response(1, 1, [2, 3])
         separation_response(2, [1])
+        for b in range(BLOCKS):
+            soften(2, b, 0)
+        for b in range(BLOCKS):
+            turn_back(2, b, 0)
         open_interaction(1)
         for a in both:
             form_pass(1, a)
-        add_squares(2, 0)
-        quantise_chunk(1)
-        soften_in_place(2, 0)
         store_forces(0, 0, CHUNK, [0])
+        quantise_chunk(1)
+        store_forces(0, 0, CHUNK, [1])
         add_squares(2, 1)
-        turned_species_response(1, 0)
+        for b in range(BLOCKS):
+            turned_species_response(b, 0)
         soften_in_place(2, 1)
+        open_interaction(2)
+        store_forces(0, 0, CHUNK, [2])
+        for b in range(BLOCKS):
+            form_unit(2, b, 0)
         for unit in last:
             turned_separation_response(*unit)
-        open_interaction(2)
-        store_forces(0, 0, CHUNK, [1])
-        form_pass(2, 0)
-        store_forces(0, 0, CHUNK, [2])
-        form_pass(2, 1)
+        rings["scalar"] = in_turn([banks[2], banks[3]] + banks[SCALAR_BANKS:])
         store_forces(1, 0, CHUNK, [0])
+        form_pass(2, 1)
+        store_forces(1, 0, CHUNK, [1])
         quantise_chunk(2)
-        store_forces(1, 0, CHUNK, [1, 2])
+        store_forces(1, 0, CHUNK, [2])
         sum_by_transposes(LAST)
         soften_sums(LAST)
         open_interaction(LAST)
-        for b in range(BLOCKS):
-            for a in both:
-                form_unit(LAST, b, a)
-            quantise_block(b)
-            store_forces(2, 0, CHUNK, [b])
+        store_forces(2, 0, CHUNK, [0])
+        for a in both:
+            form_unit(LAST, 0, a)
+        quantise_block(0)
+        store_forces(2, 0, CHUNK, [1])
+        for a in both:
+            form_unit(LAST, 1, a)
+        quantise_block(1)
         store_forces(2, 0, CHUNK, [2])
-        rings["vector"] = in_turn(banks[2:6])
+        rings["vector"] = in_turn([banks[6], banks[7], banks[2], banks[3]])
         store_forces(LAST, 0, P, [0, 1])
         store_forces(LAST, P, P, [0, 1])

@@ -30,14 +30,11 @@ BLOCKS = CHUNK // P
 N_TILES = N // P
 PER_COLUMN = 16
 RUN = 2
-EARLY_PLANES = 2
-ON_VECTOR = 2
-WS_GROUPED_ROOM = 12288
-X_ROOM = 16384
-C_ROOM = 18432
-H_ROOM = 8192
-WS_ROOM = 4096
-SCALAR_BANKS = 4
+WS_PIECES = 2
+WC_SCALE_ROOM = 0
+LATE_ROOM = 2048
+C_ROOM = 8192
+TABLE_ROOM = 24576
 
 
 def tile_list_grain_sheath_forces_kernel(
@@ -53,6 +50,9 @@ def tile_list_grain_sheath_forces_kernel(
         def held(name, shape, dtype):
             return keep.tile(shape, dtype, name=name, align_bytes=64)
 
+        def placed(name, shape, dtype, at):
+            return shared.tile(shape, dtype, name=name, offset=at, align_bytes=64)
+
         def in_turn(tiles):
             handed = []
 
@@ -63,47 +63,40 @@ def tile_list_grain_sheath_forces_kernel(
             return take
 
         banks = [psum.tile([P, BANK], F32, name="bank%d" % i) for i in range(8)]
-        rings = {"scalar": in_turn(banks[:SCALAR_BANKS]), "vector": in_turn(banks[:2])}
-
-        def scalar_bank():
-            return rings["scalar"]()
-
-        def vector_bank():
-            return rings["vector"]()
-
+        rings = {"scalar": in_turn(banks[:4]), "sums": in_turn(banks[4:])}
 
         idx_tab = keep.tile([P, S // PER_COLUMN], U16, name="idx_tab")
         idx_a = keep.tile([P, S // PER_COLUMN], U16, name="idx_a")
         idx_b = keep.tile([P, S // PER_COLUMN], U16, name="idx_b")
-        tab_w = held("tab_w", [P, T], U32)
+        tab_w = placed("tab_w", [P, T], U32, TABLE_ROOM)
         tab_s = held("tab_s", [P, T], U8)
         wc_w_raw = held("wc_w_raw", [P, 2 * H], U8)
-        wc_s_raw = shared.tile([P, H], U8, name="wc_s_raw", offset=0, align_bytes=64)
+        wc_s_raw = placed("wc_s_raw", [P, H], U8, WC_SCALE_ROOM)
         wc_w = held("wc_w", [P, 2 * H], U8)
         wc_s = held("wc_s", [P, H], U8)
         wf_w = held("wf_w", [P, H_PASSES, N], U32)
         wf_s = held("wf_s", [P, H_PASSES, N], U8)
         planes = [held("plane%d" % t, [P, T], F32) for t in range(PACK)]
-        ws_first = held("ws_raw0", [P, PACK, PASS], F32)
-        ws_second = shared.tile([P, PACK, PASS], F32, name="ws_raw1", offset=C_ROOM + 6144, align_bytes=64)
+        piece = PASS // WS_PIECES
+        ws_raw = {}
+        for i in range(WS_PIECES):
+            ws_raw[0, i] = held("ws_raw0_%d" % i, [P, PACK, piece], F32)
+            ws_raw[1, i] = placed("ws_raw1_%d" % i, [P, PACK, piece], F32, C_ROOM + 4096 * (1 + i))
         ws_grouped = [
             held("ws_grouped0", [P, PACK, P, PACK], BF16),
-            shared.tile([P, PACK, P, PACK], BF16, name="ws_grouped1", offset=WS_GROUPED_ROOM, align_bytes=64),
+            placed("ws_grouped1", [P, PACK, P, PACK], BF16, LATE_ROOM + 1024),
         ]
-        ws_w = {}
+        ws_w = [placed("ws_w%d" % a, [P, PASS], U32, TABLE_ROOM + 4 * PASS * a) for a in range(H_PASSES)]
         ws_s = [held("ws_s%d" % a, [P, PASS], U8) for a in range(H_PASSES)]
         gains = held("gains", [P, H_PASSES, PACK], F32)
         sep_halves = [held("sep%d" % h, [P, PACK, BANK], F32) for h in range(CHUNKS // PER_BANK)]
-        sep = [
-            sep_halves[k // PER_BANK][:, :, (k % PER_BANK) * CHUNK : (k % PER_BANK + 1) * CHUNK] for k in range(CHUNKS)
-        ]
-        seconds = [held("second%d" % i, [P, BANK], F32) for i in range(2)]
-        d_rooms = {}
+        second_room = in_turn([held("second%d" % i, [P, BANK], F32) for i in range(2)])
+        x_room = in_turn([held("x_grouped%d" % u, [P, CHUNK * PACK], BF16) for u in range(2)])
+        d_room = in_turn([held("d_sq%d" % i, [P, PACK, CHUNK], F32) for i in range(4)])
         soft_room = in_turn([held("soft%d" % i, [P, BANK], F32) for i in range(4)])
         h_grouped = in_turn([held("h_grouped%d" % i, [P, H_PASSES * CHUNK * PACK], BF16) for i in range(2)])
         h_words = in_turn([held("h_w%d" % i, [P, H_PASSES * CHUNK], U32) for i in range(2)])
         h_scales = in_turn([held("h_s%d" % i, [P, H_PASSES * CHUNK], U8) for i in range(2)])
-
         drag_room = [held("forces%d" % k, [P, N_TILES * CHUNK], F32)[:] for k in range(LAST)]
 
         def pieces(k):
@@ -112,14 +105,14 @@ def tile_list_grain_sheath_forces_kernel(
 
         def forces(k, first, width):
             if k == LAST:
-                room = ws_first[:].rearrange("p t c -> p (t c)")[:, N_TILES * first : N_TILES * (first + width)]
+                room = ws_raw[0, first // P][:].rearrange("p t c -> p (t c)")[:, 0 : N_TILES * width]
             else:
                 room = drag_room[k]
             return room.rearrange("p (m j) -> p m j", j=width)
 
-        def load_scale_rows(queue, plane, rows):
+        def load_scale_rows(plane, rows):
             for q in range(4):
-                queue.dma_start(plane[32 * q : 32 * q + 4, :].bitcast(I32), rows[4 * q : 4 * q + 4, :].bitcast(I32))
+                nc.sync.dma_start(plane[32 * q : 32 * q + 4, :].bitcast(I32), rows[4 * q : 4 * q + 4, :].bitcast(I32))
 
         nc.gpsimd.memset(tab_s[:].bitcast(I32), 0)
         nc.gpsimd.memset(wc_s_raw[:].bitcast(I32), 0)
@@ -139,25 +132,30 @@ def tile_list_grain_sheath_forces_kernel(
         def load_plane(t):
             nc.sync.dma_start(planes[t][:], x_rows[:, t, :])
 
+        def load_ws(a, i):
+            col = a * PASS + i * piece
+            nc.sync.dma_start(ws_raw[a, i][:], ws_rows[:, :, col : col + piece])
+
         def load_drag(k):
             for first, width in pieces(k):
                 col = k * CHUNK + first
                 nc.sync.dma_start(forces(k, first, width), drag_rows[:, :, col : col + width])
 
         nc.sync.dma_start(idx_tab[:], offs)
-        load_scale_rows(nc.sync, tab_s, tab_scales[0])
+        load_scale_rows(tab_s, tab_scales[0])
         nc.sync.dma_start(wc_w_raw[:], wc_words[0])
+        load_ws(0, 0)
         nc.sync.dma_start(tab_w[:].bitcast(I32), tab_words[0].rearrange("p n t -> p (n t)").bitcast(I32))
-        load_scale_rows(nc.sync, wc_s_raw, wc_scales[0])
+        load_ws(0, 1)
+        load_scale_rows(wc_s_raw, wc_scales[0])
         nc.sync.dma_start(gains[:], gain.rearrange("(a p t) -> p a t", p=P, t=PACK))
         load_plane(0)
         nc.sync.dma_start(idx_b[:], offs3)
         nc.sync.dma_start(idx_a[:], offs2)
-        nc.sync.dma_start(ws_first[:], ws_rows[:, :, 0:PASS])
-        load_plane(1)
-        load_plane(2)
-        load_plane(3)
-        nc.sync.dma_start(ws_second[:], ws_rows[:, :, PASS:])
+        for t in range(1, PACK):
+            load_plane(t)
+        for i in range(WS_PIECES):
+            load_ws(1, i)
         nc.sync.dma_start(wf_w[:].bitcast(I32), wf_words.rearrange("a p n t -> p a (n t)").bitcast(I32))
         for q in range(4):
             nc.sync.dma_start(
@@ -179,26 +177,18 @@ def tile_list_grain_sheath_forces_kernel(
         def quantise(words, scales, grouped):
             nc.vector.quantize_mx(out=words.bitcast(FP8X4), scales=scales, in_=grouped)
 
-        def round_ws_on_scalar(target, source):
-            target = target.rearrange("p t (g i) j -> p g j i t", i=2)
-            source = source.rearrange("p j (g i t) -> p g j i t", i=2, t=PACK)
+        def round_ws(a, i):
+            rows = piece // PACK
+            target = ws_grouped[a][:, :, i * rows : (i + 1) * rows, :].rearrange("p t (g i) j -> p g j i t", i=2)
+            source = ws_raw[a, i][:].rearrange("p j (g i t) -> p g j i t", i=2, t=PACK)
             for t0 in range(0, PACK, 2):
                 nc.scalar.copy(target[:, :, :, :, t0 : t0 + 2], source[:, :, :, :, t0 : t0 + 2])
 
-        def round_ws(a):
-            if a == 0:
-                round_ws_on_scalar(ws_grouped[0][:], ws_first[:])
-                load_drag(LAST)
-            else:
-                round_ws_on_scalar(ws_grouped[1][:], ws_second[:])
-
         def quantise_ws(a):
-            ws_w[a] = shared.tile([P, PASS], U32, name="ws_w%d" % a, offset=WS_ROOM + a * 4 * PASS, align_bytes=64)
             quantise(ws_w[a][:], ws_s[a][:], ws_grouped[a][:].rearrange("p t m j -> p (t m j)"))
 
         species = {}
         grouped_x = {}
-        x_rooms = [held("x_grouped%d" % u, [P, CHUNK * PACK], BF16) for u in range(PER_BANK)]
         c_rooms = {}
         c_squares = {}
         gained = {}
@@ -209,6 +199,9 @@ def tile_list_grain_sheath_forces_kernel(
         rooms_h = {}
         interactions = {}
 
+        def entries(first, count):
+            return slice(first // PER_COLUMN, (first + count) // PER_COLUMN)
+
         def gather_species_scales():
             v_s = held("v_s", [P, S], U8)
             nc.vector.tensor_copy(v_s[:], tab_s[:].indirect(idx_tab[:]))
@@ -216,47 +209,49 @@ def tile_list_grain_sheath_forces_kernel(
                 species[half, "s"] = v_s[:, half * BANK : (half + 1) * BANK]
 
         def gather_species_words(half):
-            cols = slice(half * BANK // PER_COLUMN, (half + 1) * BANK // PER_COLUMN)
             if half == 0:
                 v_w = held("v_w0", [P, BANK], U32)
             else:
-                v_w = shared.tile([P, BANK], U32, name="v_w1", offset=0, align_bytes=64)
-            nc.vector.tensor_copy(v_w[:], tab_w[:].indirect(idx_tab[:, cols]))
+                v_w = placed("v_w1", [P, BANK], U32, WC_SCALE_ROOM)
+            nc.vector.tensor_copy(v_w[:], tab_w[:].indirect(idx_tab[:, entries(half * BANK, BANK)]))
             species[half, "w"] = v_w
 
-        d_turn = in_turn(list(range(4)))
+        def gather_second(t, first, second):
+            nc.vector.tensor_copy(second, planes[t][:].indirect(idx_b[:, entries(first, second.shape[1])]))
 
-        def d_room():
-            i = d_turn()
-            if i not in d_rooms:
-                if i == 0:
-                    d_rooms[i] = shared.tile([P, PACK, CHUNK], F32, name="d_sq0", offset=C_ROOM + 8192, align_bytes=64)
-                else:
-                    d_rooms[i] = held("d_sq%d" % i, [P, PACK, CHUNK], F32)
-            return d_rooms[i]
+        def gather_first(t, first, second):
+            count = second.shape[1]
+            target = sep_halves[first // BANK][:, t, first % BANK : first % BANK + count]
+            nc.vector.tensor_tensor(target, planes[t][:].indirect(idx_a[:, entries(first, count)]), second, ALU.subtract)
+
+        def gather(jobs):
+            for job in jobs:
+                gather_second(*job)
+            for job in jobs:
+                gather_first(*job)
 
         def turned(tile):
             return tile.rearrange("p t j -> p (t j)").rearrange("p (b r) -> p b r", r=PASS)
 
-        def c_room(half, a):
+        def open_c_room(half, a):
             shape = [P, PER_BANK, PACK, CHUNK]
             if (half, a) == (1, 0):
-                squares = shared.tile(shape, F32, name="c_sq1_0", offset=C_ROOM, align_bytes=64)
-                scaled = shared.tile(shape, F32, name="gained1_0", offset=C_ROOM + 12288, align_bytes=64)
+                squares = placed("c_sq1_0", shape, F32, C_ROOM)
+                scaled = placed("gained1_0", shape, F32, C_ROOM + 8192)
             else:
                 squares = held("c_sq%d_%d" % (half, a), shape, F32)
                 scaled = held("gained%d_%d" % (half, a), shape, F32)
             for u in range(PER_BANK):
                 c_squares[half * PER_BANK + u, a] = squares[:, u, :, :]
                 gained[half * PER_BANK + u, a] = scaled[:, u, :, :]
-            return squares, scaled
+            c_rooms[half, a] = (squares, scaled)
 
         def species_response(half, a, slices):
             v_w, v_s = species[half, "w"], species[half, "s"]
             squares, scaled = c_rooms[half, a]
             plain = PER_BANK - 1 if half == LAST // PER_BANK else PER_BANK
             for t in slices:
-                bank = scalar_bank()
+                bank = rings["scalar"]()
                 c = bank[:].rearrange("p (u j) -> p u j", u=PER_BANK)
                 col = a * PASS + t * P
                 nc.tensor.matmul_mx(
@@ -270,7 +265,7 @@ def tile_list_grain_sheath_forces_kernel(
 
         def turned_species_response(b, a):
             v_w, v_s = species[LAST // PER_BANK, "w"], species[LAST // PER_BANK, "s"]
-            c = scalar_bank()
+            c = rings["scalar"]()
             col = (PER_BANK - 1) * CHUNK + b * P
             nc.tensor.matmul_mx(
                 out=c[:],
@@ -285,7 +280,7 @@ def tile_list_grain_sheath_forces_kernel(
             x_w, x_s = separations[LAST]
             if b == 0:
                 d_squares[LAST, a] = d_room()[:]
-            d = scalar_bank()
+            d = rings["scalar"]()
             nc.tensor.matmul_mx(
                 out=d[:],
                 lhsT=x_w[:, b * P : (b + 1) * P].bitcast(FP8X4), lhsT_scale=x_s[:, b * P : (b + 1) * P],
@@ -294,54 +289,12 @@ def tile_list_grain_sheath_forces_kernel(
             )
             nc.scalar.activation(turned(d_squares[LAST, a])[:, b, :], d[:], ACT.Square)
 
-        def gather_second(t, first, count, second):
-            cols = slice(first * CHUNK // PER_COLUMN, (first + count) * CHUNK // PER_COLUMN)
-            nc.vector.tensor_copy(second, planes[t][:].indirect(idx_b[:, cols]))
-
-        def gather_first(t, first, count, second):
-            cols = slice(first * CHUNK // PER_COLUMN, (first + count) * CHUNK // PER_COLUMN)
-            u = first % PER_BANK
-            target = sep_halves[first // PER_BANK][:, t, u * CHUNK : (u + count) * CHUNK]
-            nc.vector.tensor_tensor(target, planes[t][:].indirect(idx_a[:, cols]), second, ALU.subtract)
-
-        def gather(jobs):
-            for job in jobs:
-                gather_second(*job)
-            for job in jobs:
-                gather_first(*job)
-
-        def interleave_separation(k):
-            if k < ON_VECTOR:
-                grouped_x[k] = x_rooms[k % PER_BANK][:]
-                nc.vector.tensor_copy(
-                    grouped_x[k].rearrange("p (g i t) -> p g t i", i=RUN, t=PACK),
-                    sep[k].rearrange("p t (g i) -> p g t i", i=RUN),
-                )
-            else:
-                room = c_squares[0, k - ON_VECTOR][:, 0:2, :]
-                grouped_x[k] = room.rearrange("p t j -> p (t j)").bitcast(BF16)
-                nc.scalar.copy(
-                    grouped_x[k].rearrange("p (g i t) -> p g t i", i=RUN, t=PACK),
-                    sep[k].rearrange("p t (g i) -> p g t i", i=RUN),
-                )
-
-        def quantise_separation(k):
-            if k < ON_VECTOR:
-                x_w = held("x_w%d" % k, [P, CHUNK], U32)
-                x_s = held("x_s%d" % k, [P, CHUNK], U8)
-            else:
-                at = H_ROOM + (k - ON_VECTOR) * 2048
-                x_w = shared.tile([P, CHUNK], U32, name="x_w%d" % k, offset=at, align_bytes=64)
-                x_s = shared.tile([P, CHUNK], U8, name="x_s%d" % k, offset=at + 1024, align_bytes=64)
-            quantise(x_w[:], x_s[:], grouped_x[k])
-            separations[k] = (x_w, x_s)
-
         def separation_response(k, passes):
             x_w, x_s = separations[k]
             for a in passes:
                 d_squares[k, a] = d_room()[:]
                 for t0 in range(0, PACK, PER_BANK):
-                    d = scalar_bank()[:].rearrange("p (u j) -> p u j", u=PER_BANK)
+                    d = rings["scalar"]()[:].rearrange("p (u j) -> p u j", u=PER_BANK)
                     for u in range(PER_BANK):
                         col = (t0 + u) * P
                         nc.tensor.matmul_mx(
@@ -357,24 +310,42 @@ def tile_list_grain_sheath_forces_kernel(
                 return [(b, a) for b in range(BLOCKS) for a in range(H_PASSES)]
             return [(b, a) for a in range(H_PASSES) for b in range(BLOCKS)]
 
-        def sum_squares(k, b, a):
-            if k == 0:
-                total = banks[SCALAR_BANKS + units(k).index((b, a))]
-            elif k == 2:
-                total = banks[2 + b]
-            else:
-                total = scalar_bank()
-            for i, term in enumerate((c_squares[k, a], d_squares[k, a])):
-                for t in range(PACK):
-                    if k == LAST:
-                        square = turned(term)[:, b, t * P : (t + 1) * P]
-                    else:
-                        square = term[:, t, b * P : (b + 1) * P]
-                    nc.tensor.matmul(
-                        total[:, t * P : (t + 1) * P], square, ident[:],
-                        start=(i == 0 and t == 0), stop=(i == 1 and t == PACK - 1), is_transpose=True,
-                    )
-            sums[k, b, a] = total
+        def interleave_separation(k, copy):
+            grouped_x[k] = x_room()[:]
+            u = k % PER_BANK
+            source = sep_halves[k // PER_BANK][:, :, u * CHUNK : (u + 1) * CHUNK]
+            copy(
+                grouped_x[k].rearrange("p (g i t) -> p g t i", i=RUN, t=PACK),
+                source.rearrange("p t (g i) -> p g t i", i=RUN),
+            )
+
+        def quantise_separation(k):
+            x_w = held("x_w%d" % k, [P, CHUNK], U32)
+            x_s = held("x_s%d" % k, [P, CHUNK], U8)
+            quantise(x_w[:], x_s[:], grouped_x[k])
+            separations[k] = (x_w, x_s)
+
+        def units(k):
+            if k == LAST:
+                return [(b, a) for b in range(BLOCKS) for a in range(H_PASSES)]
+            return [(b, a) for a in range(H_PASSES) for b in range(BLOCKS)]
+
+        def turn_squares(k, b, a, term):
+            if term == 0:
+                sums[k, b, a] = rings["sums"]()
+            squares = (c_squares, d_squares)[term][k, a]
+            for t in range(PACK):
+                if k == LAST:
+                    square = turned(squares)[:, b, t * P : (t + 1) * P]
+                else:
+                    square = squares[:, t, b * P : (b + 1) * P]
+                nc.tensor.matmul(
+                    sums[k, b, a][:, t * P : (t + 1) * P], square, ident[:],
+                    start=(term == 0 and t == 0), stop=(term == 1 and t == PACK - 1), is_transpose=True,
+                )
+
+        def open_interaction(k):
+            rooms_h[k] = (h_grouped(), h_words(), h_scales())
 
         def soften(k, b, a):
             soft = soft_room()
@@ -404,13 +375,6 @@ def tile_list_grain_sheath_forces_kernel(
                 ALU.mult,
             )
 
-        def open_interaction(k):
-            if k == 0:
-                grouped = shared.tile([P, H_PASSES * CHUNK * PACK], BF16, name="h_first", offset=H_ROOM, align_bytes=64)
-            else:
-                grouped = h_grouped()
-            rooms_h[k] = (grouped, h_words(), h_scales())
-
         def form_pass(k, a):
             room = rooms_h[k][0][:, a * CHUNK * PACK : (a + 1) * CHUNK * PACK]
             form_interaction(room, softening[k, a], gained[k, a])
@@ -438,7 +402,7 @@ def tile_list_grain_sheath_forces_kernel(
         def store_forces(k, first, width, parts):
             tiles = N_TILES // 2 if k == LAST else BANK // width
             for m0 in [part * tiles for part in parts]:
-                y = vector_bank()[:, 0 : tiles * width].rearrange("p (u j) -> p u j", j=width)
+                y = rings["vector"]()[:, 0 : tiles * width].rearrange("p (u j) -> p u j", j=width)
                 for a in range(H_PASSES):
                     h_w, h_s = interactions[k, first, a]
                     for u in range(tiles):
@@ -454,112 +418,106 @@ def tile_list_grain_sheath_forces_kernel(
                 col = k * CHUNK + first
                 nc.sync.dma_start(out_rows[:, m0 : m0 + tiles, col : col + width], rows)
 
-        def sum_by_transposes(k):
-            for b, a in units(k):
-                sum_squares(k, b, a)
-
-        def soften_sums(k):
-            for b, a in units(k):
-                soften(k, b, a)
-
-        def turn_chunk_back(k):
-            for b, a in units(k):
-                turn_back(k, b, a)
-
-        halves = range(CHUNKS // PER_BANK)
-        gather_species_scales()
-        for half in halves:
-            gather_species_words(half)
         every = range(PACK)
-        for room in ((0, 0), (0, 1), (1, 1)):
-            c_rooms[room] = c_room(*room)
-        species_response(0, 0, every)
-        round_ws(0)
-        species_response(0, 1, every)
-        round_ws(1)
-        c_rooms[1, 0] = c_room(1, 0)
-        gather([(0, PER_BANK * half, PER_BANK, seconds[half][:]) for half in halves])
-        room = shared.tile([P, BANK], F32, name="ws_second", offset=WS_ROOM, align_bytes=64)
-        gather([(1, 0, PER_BANK, room[:]), (1, PER_BANK, PER_BANK, seconds[0][:])])
+        both = range(H_PASSES)
+        last = units(LAST)
+        gather_species_scales()
+        for half in range(CHUNKS // PER_BANK):
+            gather_species_words(half)
+        for i in range(WS_PIECES):
+            round_ws(0, i)
+        load_drag(LAST)
         quantise_ws(0)
-        gather([(2, 0, PER_BANK, seconds[1][:]), (3, 0, PER_BANK, seconds[0][:])])
+        for room in ((0, 0), (0, 1), (1, 1)):
+            open_c_room(*room)
+        for a in both:
+            species_response(0, a, every)
+        for unit in units(0):
+            turn_squares(0, *unit, 0)
+        for i in range(WS_PIECES):
+            round_ws(1, i)
+        open_c_room(1, 0)
+        gather([(0, half * BANK, second_room()[:]) for half in range(2)])
+        for t in range(1, PACK):
+            room = second_room()
+            gather([(t, u * CHUNK, room[:, u * CHUNK : (u + 1) * CHUNK]) for u in range(PER_BANK)])
         for k in range(PER_BANK):
-            interleave_separation(k)
+            interleave_separation(k, nc.vector.tensor_copy)
         for k in range(PER_BANK):
             quantise_separation(k)
         quantise_ws(1)
-        late = shared.tile([P, 2, BANK], F32, name="late_second", offset=WS_GROUPED_ROOM, align_bytes=64)
-        gather([(2, PER_BANK, PER_BANK, late[:, 0, :]), (3, PER_BANK, PER_BANK, late[:, 1, :])])
+        late = [placed("late%d" % t, [P, BANK], F32, LATE_ROOM + 2048 * (t - 1)) for t in range(1, PACK)]
+        gather([(t, BANK, late[t - 1][:]) for t in range(1, PACK)])
 
+        def finish_units(k, a):
+            for b in range(BLOCKS):
+                soften(k, b, a)
+                turn_back(k, b, a)
 
-        both = range(H_PASSES)
-        last = units(LAST)
-        for b in range(BLOCKS):
-            turned_species_response(b, 1)
         species_response(1, 0, every)
-        species_response(1, 1, [0])
-        separation_response(0, both)
-        sum_by_transposes(0)
-        species_response(1, 1, [1])
-        soften_sums(0)
-        turn_chunk_back(0)
-        separation_response(1, both)
+        for a in both:
+            separation_response(0, [a])
+            for b in range(BLOCKS):
+                turn_squares(0, b, a, 1)
+            species_response(1, 1, [a])
         open_interaction(0)
-        for unit in units(0):
-            form_unit(0, *unit)
-        interleave_separation(2)
-        add_squares(1, 0)
-        quantise_chunk(0)
-        add_squares(1, 1)
+        for a in both:
+            separation_response(1, [a])
+            finish_units(0, a)
+            add_squares(1, a)
+            for b in range(BLOCKS):
+                form_unit(0, b, a)
+        interleave_separation(2, nc.scalar.copy)
         quantise_separation(2)
+        quantise_chunk(0)
         soften_in_place(1, 0)
-        interleave_separation(LAST)
+        interleave_separation(LAST, nc.scalar.copy)
         soften_in_place(1, 1)
-        quantise_separation(LAST)
-        rings["scalar"] = in_turn(banks[SCALAR_BANKS:])
+        rings["scalar"] = in_turn([banks[i] for i in (2, 3, 0, 1, 4, 5, 6, 7, 0, 2, 1, 0, 3, 2)])
+        rings["vector"] = in_turn([banks[i] for i in (2, 3, 4, 5, 4, 5, 4, 0, 5, 2, 6, 7, 1)])
+        rings["sums"] = in_turn([banks[i] for i in (6, 7, 1, 3)])
+        open_interaction(1)
         separation_response(2, [0])
-        for b in range(BLOCKS):
-            sum_squares(2, b, 0)
+        form_pass(1, 0)
+        quantise_separation(LAST)
+        form_pass(1, 1)
+        quantise_chunk(1)
         species_response(1, 1, [2, 3])
         separation_response(2, [1])
-        for b in range(BLOCKS):
-            soften(2, b, 0)
-        for b in range(BLOCKS):
-            turn_back(2, b, 0)
-        open_interaction(1)
-        for a in both:
-            form_pass(1, a)
         store_forces(0, 0, CHUNK, [0])
-        quantise_chunk(1)
+        add_squares(2, 0)
         store_forces(0, 0, CHUNK, [1])
         add_squares(2, 1)
-        for b in range(BLOCKS):
-            turned_species_response(b, 0)
-        soften_in_place(2, 1)
-        open_interaction(2)
         store_forces(0, 0, CHUNK, [2])
-        for b in range(BLOCKS):
-            form_unit(2, b, 0)
-        for unit in last:
-            turned_separation_response(*unit)
-        rings["scalar"] = in_turn([banks[2], banks[3]] + banks[SCALAR_BANKS:])
+        open_interaction(2)
+        for a in both:
+            turned_species_response(*last[a])
+            soften_in_place(2, a)
+        turn_squares(LAST, *last[0], 0)
+        form_pass(2, 0)
         store_forces(1, 0, CHUNK, [0])
+        turn_squares(LAST, *last[1], 0)
         form_pass(2, 1)
         store_forces(1, 0, CHUNK, [1])
         quantise_chunk(2)
         store_forces(1, 0, CHUNK, [2])
-        sum_by_transposes(LAST)
-        soften_sums(LAST)
+        for unit in last[:2]:
+            turned_separation_response(*unit)
+            turn_squares(LAST, *unit, 1)
         open_interaction(LAST)
-        store_forces(2, 0, CHUNK, [0])
-        for a in both:
-            form_unit(LAST, 0, a)
+        for early, unit in zip(last[:2], last[2:]):
+            turned_species_response(*unit)
+            turned_separation_response(*unit)
+            for term in range(2):
+                turn_squares(LAST, *unit, term)
+            soften(LAST, *early)
+            store_forces(2, 0, CHUNK, [early[1]])
+            form_unit(LAST, *early)
         quantise_block(0)
-        store_forces(2, 0, CHUNK, [1])
-        for a in both:
-            form_unit(LAST, 1, a)
-        quantise_block(1)
         store_forces(2, 0, CHUNK, [2])
-        rings["vector"] = in_turn([banks[6], banks[7], banks[2], banks[3]])
-        store_forces(LAST, 0, P, [0, 1])
-        store_forces(LAST, P, P, [0, 1])
+        for unit in last[2:]:
+            soften(LAST, *unit)
+            form_unit(LAST, *unit)
+        quantise_block(1)
+        for b in range(BLOCKS):
+            store_forces(LAST, b * P, P, [0, 1])

@@ -35,6 +35,7 @@ WC_SCALE_ROOM = 0
 LATE_ROOM = 2048
 C_ROOM = 8192
 TABLE_ROOM = 24576
+FIRST_C_ROOM = 32768
 
 
 def tile_list_grain_sheath_forces_kernel(
@@ -80,7 +81,7 @@ def tile_list_grain_sheath_forces_kernel(
         piece = PASS // WS_PIECES
         ws_raw = {}
         for i in range(WS_PIECES):
-            ws_raw[0, i] = held("ws_raw0_%d" % i, [P, PACK, piece], F32)
+            ws_raw[0, i] = placed("ws_raw0_%d" % i, [P, PACK, piece], F32, FIRST_C_ROOM + 4096 * i)
             ws_raw[1, i] = placed("ws_raw1_%d" % i, [P, PACK, piece], F32, C_ROOM + 4096 * (1 + i))
         ws_grouped = [
             held("ws_grouped0", [P, PACK, P, PACK], BF16),
@@ -97,7 +98,7 @@ def tile_list_grain_sheath_forces_kernel(
         h_grouped = in_turn([held("h_grouped%d" % i, [P, H_PASSES * CHUNK * PACK], BF16) for i in range(2)])
         h_words = in_turn([held("h_w%d" % i, [P, H_PASSES * CHUNK], U32) for i in range(2)])
         h_scales = in_turn([held("h_s%d" % i, [P, H_PASSES * CHUNK], U8) for i in range(2)])
-        drag_room = [held("forces%d" % k, [P, N_TILES * CHUNK], F32)[:] for k in range(LAST)]
+        drag_room = [held("forces%d" % k, [P, N_TILES * CHUNK], F32)[:] for k in range(CHUNKS)]
 
         def pieces(k):
             width = P if k == LAST else CHUNK
@@ -105,7 +106,7 @@ def tile_list_grain_sheath_forces_kernel(
 
         def forces(k, first, width):
             if k == LAST:
-                room = ws_raw[0, first // P][:].rearrange("p t c -> p (t c)")[:, 0 : N_TILES * width]
+                room = drag_room[k][:, N_TILES * first : N_TILES * (first + width)]
             else:
                 room = drag_room[k]
             return room.rearrange("p (m j) -> p m j", j=width)
@@ -144,10 +145,10 @@ def tile_list_grain_sheath_forces_kernel(
         nc.sync.dma_start(idx_tab[:], offs)
         load_scale_rows(tab_s, tab_scales[0])
         nc.sync.dma_start(wc_w_raw[:], wc_words[0])
-        load_ws(0, 0)
         nc.sync.dma_start(tab_w[:].bitcast(I32), tab_words[0].rearrange("p n t -> p (n t)").bitcast(I32))
-        load_ws(0, 1)
         load_scale_rows(wc_s_raw, wc_scales[0])
+        for i in range(WS_PIECES):
+            load_ws(0, i)
         nc.sync.dma_start(gains[:], gain.rearrange("(a p t) -> p a t", p=P, t=PACK))
         load_plane(0)
         nc.sync.dma_start(idx_b[:], offs3)
@@ -162,7 +163,7 @@ def tile_list_grain_sheath_forces_kernel(
                 wf_s[32 * q : 32 * q + 4, :, :].bitcast(I32),
                 wf_scales[:, 4 * q : 4 * q + 4, :].rearrange("a r n -> r a n").bitcast(I32),
             )
-        for k in range(LAST):
+        for k in range(CHUNKS):
             load_drag(k)
 
         nc.vector.tensor_copy(
@@ -238,6 +239,9 @@ def tile_list_grain_sheath_forces_kernel(
             if (half, a) == (1, 0):
                 squares = placed("c_sq1_0", shape, F32, C_ROOM)
                 scaled = placed("gained1_0", shape, F32, C_ROOM + 8192)
+            elif (half, a) == (0, 0):
+                squares = placed("c_sq0_0", shape, F32, FIRST_C_ROOM)
+                scaled = held("gained0_0", shape, F32)
             else:
                 squares = held("c_sq%d_%d" % (half, a), shape, F32)
                 scaled = held("gained%d_%d" % (half, a), shape, F32)
@@ -426,7 +430,6 @@ def tile_list_grain_sheath_forces_kernel(
             gather_species_words(half)
         for i in range(WS_PIECES):
             round_ws(0, i)
-        load_drag(LAST)
         quantise_ws(0)
         for room in ((0, 0), (0, 1), (1, 1)):
             open_c_room(*room)

@@ -36,6 +36,8 @@ LATE_ROOM = 2048
 C_ROOM = 8192
 TABLE_ROOM = 24576
 FIRST_C_ROOM = 32768
+SEP_ROOM = 40960
+H_ROOM = 49152
 
 
 def tile_list_grain_sheath_forces_kernel(
@@ -85,16 +87,16 @@ def tile_list_grain_sheath_forces_kernel(
             ws_raw[1, i] = placed("ws_raw1_%d" % i, [P, PACK, piece], F32, C_ROOM + 4096 * (1 + i))
         ws_grouped = [
             held("ws_grouped0", [P, PACK, P, PACK], BF16),
-            placed("ws_grouped1", [P, PACK, P, PACK], BF16, LATE_ROOM + 1024),
+            placed("ws_grouped1", [P, PACK, P, PACK], BF16, SEP_ROOM + 4096),
         ]
         ws_w = [placed("ws_w%d" % a, [P, PASS], U32, TABLE_ROOM + 4 * PASS * a) for a in range(H_PASSES)]
         ws_s = [held("ws_s%d" % a, [P, PASS], U8) for a in range(H_PASSES)]
         gains = held("gains", [P, H_PASSES, PACK], F32)
-        sep_halves = [held("sep%d" % h, [P, PACK, BANK], F32) for h in range(CHUNKS // PER_BANK)]
-        second_room = in_turn([held("second%d" % i, [P, BANK], F32) for i in range(2)])
-        x_room = in_turn([held("x_grouped%d" % u, [P, CHUNK * PACK], BF16) for u in range(2)])
+        sep_halves = [held("sep0", [P, PACK, BANK], F32), placed("sep1", [P, PACK, BANK], F32, SEP_ROOM)]
+        second_room = in_turn([placed("second%d" % i, [P, BANK], F32, LATE_ROOM + 2048 * i) for i in range(2)])
         d_room = in_turn([held("d_sq%d" % i, [P, PACK, CHUNK], F32) for i in range(4)])
-        soft_room = in_turn([held("soft%d" % i, [P, BANK], F32) for i in range(4)])
+        softs = [held("soft%d" % i, [P, BANK], F32) for i in range(4)]
+        soft_room = in_turn(softs[:3] + [placed("soft_first", [P, BANK], F32, H_ROOM)] + softs)
         h_grouped = in_turn([held("h_grouped%d" % i, [P, H_PASSES * CHUNK * PACK], BF16) for i in range(2)])
         h_words = in_turn([held("h_w%d" % i, [P, H_PASSES * CHUNK], U32) for i in range(2)])
         h_scales = in_turn([held("h_s%d" % i, [P, H_PASSES * CHUNK], U8) for i in range(2)])
@@ -236,9 +238,9 @@ def tile_list_grain_sheath_forces_kernel(
 
         def open_c_room(half, a):
             shape = [P, PER_BANK, PACK, CHUNK]
-            if (half, a) == (1, 0):
-                squares = placed("c_sq1_0", shape, F32, C_ROOM)
-                scaled = placed("gained1_0", shape, F32, C_ROOM + 8192)
+            if (half, a) == (1, 1):
+                squares = placed("c_sq1_1", shape, F32, C_ROOM)
+                scaled = placed("gained1_1", shape, F32, C_ROOM + 8192)
             elif (half, a) == (0, 0):
                 squares = placed("c_sq0_0", shape, F32, FIRST_C_ROOM)
                 scaled = held("gained0_0", shape, F32)
@@ -304,7 +306,7 @@ def tile_list_grain_sheath_forces_kernel(
                         nc.tensor.matmul_mx(
                             out=d[:, u, :],
                             lhsT=ws_w[a][:, col : col + P].bitcast(FP8X4), lhsT_scale=ws_s[a][:, col : col + P],
-                            rhs=x_w[:].bitcast(FP8X4), rhs_scale=x_s[:],
+                            rhs=x_w.bitcast(FP8X4), rhs_scale=x_s,
                             start=True, stop=True,
                         )
                     nc.scalar.activation(d_squares[k, a][:, t0 : t0 + PER_BANK, :], d, ACT.Square)
@@ -313,21 +315,6 @@ def tile_list_grain_sheath_forces_kernel(
             if k == LAST:
                 return [(b, a) for b in range(BLOCKS) for a in range(H_PASSES)]
             return [(b, a) for a in range(H_PASSES) for b in range(BLOCKS)]
-
-        def interleave_separation(k, copy):
-            grouped_x[k] = x_room()[:]
-            u = k % PER_BANK
-            source = sep_halves[k // PER_BANK][:, :, u * CHUNK : (u + 1) * CHUNK]
-            copy(
-                grouped_x[k].rearrange("p (g i t) -> p g t i", i=RUN, t=PACK),
-                source.rearrange("p t (g i) -> p g t i", i=RUN),
-            )
-
-        def quantise_separation(k):
-            x_w = held("x_w%d" % k, [P, CHUNK], U32)
-            x_s = held("x_s%d" % k, [P, CHUNK], U8)
-            quantise(x_w[:], x_s[:], grouped_x[k])
-            separations[k] = (x_w, x_s)
 
         def units(k):
             if k == LAST:
@@ -431,96 +418,113 @@ def tile_list_grain_sheath_forces_kernel(
         for i in range(WS_PIECES):
             round_ws(0, i)
         quantise_ws(0)
-        for room in ((0, 0), (0, 1), (1, 1)):
+        for room in ((0, 0), (0, 1), (1, 0)):
             open_c_room(*room)
         for a in both:
             species_response(0, a, every)
         for unit in units(0):
             turn_squares(0, *unit, 0)
+        species_response(1, 0, every)
         for i in range(WS_PIECES):
             round_ws(1, i)
-        open_c_room(1, 0)
-        gather([(0, half * BANK, second_room()[:]) for half in range(2)])
+        open_c_room(1, 1)
+        first_late = held("late0", [P, BANK], F32)
+        room = second_room()
+        gather_second(0, 0, room[:])
+        gather_second(0, BANK, first_late[:])
+        gather_first(0, 0, room[:])
         for t in range(1, PACK):
             room = second_room()
             gather([(t, u * CHUNK, room[:, u * CHUNK : (u + 1) * CHUNK]) for u in range(PER_BANK)])
+        early_x = placed("early_x", [P, BANK * PACK], BF16, SEP_ROOM)
+        nc.gpsimd.tensor_scalar(
+            early_x[:].rearrange("p (j t) -> p j t", t=PACK), sep_halves[0][:].rearrange("p t j -> p j t"),
+            1.0, 0.0, ALU.mult, ALU.add,
+        )
+        late = placed("late", [P, PACK - 1, BANK], F32, LATE_ROOM)
+        for t in range(1, PACK):
+            gather_second(t, BANK, late[:, t - 1, :])
+        early_w = held("early_w", [P, BANK], U32)
+        early_s = held("early_s", [P, BANK], U8)
+        quantise(early_w[:], early_s[:], early_x[:])
         for k in range(PER_BANK):
-            interleave_separation(k, nc.vector.tensor_copy)
-        for k in range(PER_BANK):
-            quantise_separation(k)
+            separations[k] = (early_w[:, k * CHUNK : (k + 1) * CHUNK], early_s[:, k * CHUNK : (k + 1) * CHUNK])
         quantise_ws(1)
-        late = [placed("late%d" % t, [P, BANK], F32, LATE_ROOM + 2048 * (t - 1)) for t in range(1, PACK)]
-        gather([(t, BANK, late[t - 1][:]) for t in range(1, PACK)])
+        gather_first(0, BANK, first_late[:])
+        for t in range(1, PACK):
+            gather_first(t, BANK, late[:, t - 1, :])
 
-        def finish_units(k, a):
-            for b in range(BLOCKS):
-                soften(k, b, a)
-                turn_back(k, b, a)
+        def quantise_pair(half, grouped, words, scales):
+            quantise(words[:], scales[:], grouped[:])
+            for u in range(PER_BANK):
+                cols = slice(u * CHUNK, (u + 1) * CHUNK)
+                separations[half * PER_BANK + u] = (words[:, cols], scales[:, cols])
 
-        species_response(1, 0, every)
+        late_x = held("late_x", [P, BANK * PACK], BF16)
+        nc.gpsimd.tensor_scalar(
+            late_x[:].rearrange("p (j t) -> p j t", t=PACK), sep_halves[1][:].rearrange("p t j -> p j t"),
+            1.0, 0.0, ALU.mult, ALU.add,
+        )
+        species_response(1, 1, [0])
         for a in both:
             separation_response(0, [a])
             for b in range(BLOCKS):
                 turn_squares(0, b, a, 1)
-            species_response(1, 1, [a])
         open_interaction(0)
         for a in both:
-            separation_response(1, [a])
-            finish_units(0, a)
-            add_squares(1, a)
             for b in range(BLOCKS):
+                soften(0, b, a)
+                turn_back(0, b, a)
                 form_unit(0, b, a)
-        interleave_separation(2, nc.scalar.copy)
-        quantise_separation(2)
+            if a == 0:
+                species_response(1, 1, [1])
+        quantise_pair(1, late_x, placed("late_w", [P, BANK], U32, H_ROOM), held("late_s", [P, BANK], U8))
         quantise_chunk(0)
-        soften_in_place(1, 0)
-        interleave_separation(LAST, nc.scalar.copy)
-        soften_in_place(1, 1)
-        rings["scalar"] = in_turn([banks[i] for i in (2, 3, 0, 1, 4, 5, 6, 7, 0, 2, 1, 0, 3, 2)])
-        rings["vector"] = in_turn([banks[i] for i in (2, 3, 4, 5, 4, 5, 4, 0, 5, 2, 6, 7, 1)])
-        rings["sums"] = in_turn([banks[i] for i in (6, 7, 1, 3)])
-        open_interaction(1)
-        separation_response(2, [0])
-        form_pass(1, 0)
-        quantise_separation(LAST)
-        form_pass(1, 1)
-        quantise_chunk(1)
+        for a in both:
+            separation_response(1, [a])
+            add_squares(1, a)
         species_response(1, 1, [2, 3])
-        separation_response(2, [1])
-        store_forces(0, 0, CHUNK, [0])
-        add_squares(2, 0)
+        rings["scalar"] = in_turn([banks[i] for i in (4, 5, 6, 7, 0, 1, 2, 3, 4, 5, 2, 3)])
+        rings["vector"] = in_turn([banks[i] for i in (6, 7, 6, 7, 6, 7, 6, 2, 3, 7, 0, 1, 4)])
+        rings["sums"] = in_turn([banks[i] for i in (0, 1, 4, 5)])
+        open_interaction(1)
+        for a in both:
+            separation_response(2, [a])
+            add_squares(2, a)
+            soften_in_place(1, a)
+            if a == 1:
+                store_forces(0, 0, CHUNK, [0])
+            form_pass(1, a)
         store_forces(0, 0, CHUNK, [1])
-        add_squares(2, 1)
+        quantise_chunk(1)
         store_forces(0, 0, CHUNK, [2])
         open_interaction(2)
-        for a in both:
-            turned_species_response(*last[a])
-            soften_in_place(2, a)
-        turn_squares(LAST, *last[0], 0)
-        form_pass(2, 0)
-        store_forces(1, 0, CHUNK, [0])
-        turn_squares(LAST, *last[1], 0)
-        form_pass(2, 1)
-        store_forces(1, 0, CHUNK, [1])
-        quantise_chunk(2)
-        store_forces(1, 0, CHUNK, [2])
+        for unit in last[:2]:
+            turned_species_response(*unit)
+            turn_squares(LAST, *unit, 0)
         for unit in last[:2]:
             turned_separation_response(*unit)
             turn_squares(LAST, *unit, 1)
-        open_interaction(LAST)
-        for early, unit in zip(last[:2], last[2:]):
-            turned_species_response(*unit)
-            turned_separation_response(*unit)
-            for term in range(2):
-                turn_squares(LAST, *unit, term)
-            soften(LAST, *early)
-            store_forces(2, 0, CHUNK, [early[1]])
-            form_unit(LAST, *early)
-        quantise_block(0)
-        store_forces(2, 0, CHUNK, [2])
+        soften_in_place(2, 0)
+        form_pass(2, 0)
+        store_forces(1, 0, CHUNK, [0, 1])
         for unit in last[2:]:
-            soften(LAST, *unit)
-            form_unit(LAST, *unit)
-        quantise_block(1)
+            turned_species_response(*unit)
+            turn_squares(LAST, *unit, 0)
+        soften_in_place(2, 1)
+        form_pass(2, 1)
+        for unit in last[2:]:
+            turned_separation_response(*unit)
+            turn_squares(LAST, *unit, 1)
+        store_forces(1, 0, CHUNK, [2])
+        quantise_chunk(2)
+        open_interaction(LAST)
+        for b in range(BLOCKS):
+            for a in both:
+                soften(LAST, b, a)
+                form_unit(LAST, b, a)
+            store_forces(2, 0, CHUNK, [b])
+            quantise_block(b)
+        store_forces(2, 0, CHUNK, [2])
         for b in range(BLOCKS):
             store_forces(LAST, b * P, P, [0, 1])

@@ -37,7 +37,8 @@ C_ROOM = 8192
 TABLE_ROOM = 24576
 FIRST_C_ROOM = 32768
 SEP_ROOM = 40960
-H_ROOM = 49152
+EARLY_ROOM = 49152
+STAGGER = 1984
 
 
 def tile_list_grain_sheath_forces_kernel(
@@ -96,8 +97,11 @@ def tile_list_grain_sheath_forces_kernel(
         second_room = in_turn([placed("second%d" % i, [P, BANK], F32, LATE_ROOM + 2048 * i) for i in range(2)])
         d_room = in_turn([held("d_sq%d" % i, [P, PACK, CHUNK], F32) for i in range(4)])
         softs = [held("soft%d" % i, [P, BANK], F32) for i in range(4)]
-        soft_room = in_turn(softs[:3] + [placed("soft_first", [P, BANK], F32, H_ROOM)] + softs)
-        h_grouped = in_turn([held("h_grouped%d" % i, [P, H_PASSES * CHUNK * PACK], BF16) for i in range(2)])
+        soft_room = in_turn(softs)
+        x_room = in_turn([held("x_grouped%d" % u, [P, CHUNK * PACK], BF16) for u in range(2)])
+        h_rooms = [held("h_grouped%d" % i, [P, H_PASSES * CHUNK * PACK], BF16) for i in range(2)]
+        first_h = placed("h_first", [P, H_PASSES * CHUNK * PACK], BF16, EARLY_ROOM + STAGGER * 3 + 64)
+        h_grouped = in_turn([first_h] + h_rooms)
         h_words = in_turn([held("h_w%d" % i, [P, H_PASSES * CHUNK], U32) for i in range(2)])
         h_scales = in_turn([held("h_s%d" % i, [P, H_PASSES * CHUNK], U8) for i in range(2)])
         drag_room = [held("forces%d" % k, [P, N_TILES * CHUNK], F32)[:] for k in range(CHUNKS)]
@@ -197,6 +201,7 @@ def tile_list_grain_sheath_forces_kernel(
         gained = {}
         separations = {}
         d_squares = {}
+        d_slices = {}
         softening = {}
         sums = {}
         rooms_h = {}
@@ -227,6 +232,13 @@ def tile_list_grain_sheath_forces_kernel(
             target = sep_halves[first // BANK][:, t, first % BANK : first % BANK + count]
             nc.vector.tensor_tensor(target, planes[t][:].indirect(idx_a[:, entries(first, count)]), second, ALU.subtract)
 
+        def interleave_on_gpsimd(grouped, source):
+            nc.gpsimd.tensor_scalar(
+                grouped[:].rearrange("p (j t) -> p j t", t=PACK),
+                source.rearrange("p t j -> p j t"),
+                1.0, 0.0, ALU.mult, ALU.add,
+            )
+
         def gather(jobs):
             for job in jobs:
                 gather_second(*job)
@@ -238,9 +250,9 @@ def tile_list_grain_sheath_forces_kernel(
 
         def open_c_room(half, a):
             shape = [P, PER_BANK, PACK, CHUNK]
-            if (half, a) == (1, 1):
-                squares = placed("c_sq1_1", shape, F32, C_ROOM)
-                scaled = placed("gained1_1", shape, F32, C_ROOM + 8192)
+            if (half, a) == (1, 0):
+                squares = placed("c_sq1_0", shape, F32, C_ROOM)
+                scaled = placed("gained1_0", shape, F32, C_ROOM + 8192)
             elif (half, a) == (0, 0):
                 squares = placed("c_sq0_0", shape, F32, FIRST_C_ROOM)
                 scaled = held("gained0_0", shape, F32)
@@ -309,7 +321,27 @@ def tile_list_grain_sheath_forces_kernel(
                             rhs=x_w.bitcast(FP8X4), rhs_scale=x_s,
                             start=True, stop=True,
                         )
-                    nc.scalar.activation(d_squares[k, a][:, t0 : t0 + PER_BANK, :], d, ACT.Square)
+                    room = d_squares[k, a][:, t0 : t0 + PER_BANK, :]
+                    if (k, a, t0) == (0, 1, 0):
+                        room = sep_halves[1][:, PACK - 1, :].rearrange("p (u j) -> p u j", u=PER_BANK)
+                    for u in range(PER_BANK):
+                        d_slices[k, a, t0 + u] = room[:, u, :]
+                    nc.scalar.activation(room, d, ACT.Square)
+
+        def interleave_separation(k, copy):
+            grouped_x[k] = x_room()[:]
+            u = k % PER_BANK
+            source = sep_halves[k // PER_BANK][:, :, u * CHUNK : (u + 1) * CHUNK]
+            copy(
+                grouped_x[k].rearrange("p (g i t) -> p g t i", i=RUN, t=PACK),
+                source.rearrange("p t (g i) -> p g t i", i=RUN),
+            )
+
+        def quantise_separation(k):
+            x_w = held("x_w%d" % k, [P, CHUNK], U32)
+            x_s = held("x_s%d" % k, [P, CHUNK], U8)
+            quantise(x_w[:], x_s[:], grouped_x[k])
+            separations[k] = (x_w[:], x_s[:])
 
         def units(k):
             if k == LAST:
@@ -328,8 +360,10 @@ def tile_list_grain_sheath_forces_kernel(
             for t in range(PACK):
                 if k == LAST:
                     square = turned(squares)[:, b, t * P : (t + 1) * P]
-                else:
+                elif term == 0:
                     square = squares[:, t, b * P : (b + 1) * P]
+                else:
+                    square = d_slices[k, a, t][:, b * P : (b + 1) * P]
                 nc.tensor.matmul(
                     sums[k, b, a][:, t * P : (t + 1) * P], square, ident[:],
                     start=(term == 0 and t == 0), stop=(term == 1 and t == PACK - 1), is_transpose=True,
@@ -418,16 +452,16 @@ def tile_list_grain_sheath_forces_kernel(
         for i in range(WS_PIECES):
             round_ws(0, i)
         quantise_ws(0)
-        for room in ((0, 0), (0, 1), (1, 0)):
+        for room in ((0, 0), (0, 1), (1, 1)):
             open_c_room(*room)
         for a in both:
             species_response(0, a, every)
         for unit in units(0):
             turn_squares(0, *unit, 0)
-        species_response(1, 0, every)
         for i in range(WS_PIECES):
             round_ws(1, i)
-        open_c_room(1, 1)
+        open_c_room(1, 0)
+        species_response(1, 0, every)
         first_late = held("late0", [P, BANK], F32)
         room = second_room()
         gather_second(0, 0, room[:])
@@ -436,88 +470,88 @@ def tile_list_grain_sheath_forces_kernel(
         for t in range(1, PACK):
             room = second_room()
             gather([(t, u * CHUNK, room[:, u * CHUNK : (u + 1) * CHUNK]) for u in range(PER_BANK)])
-        early_x = placed("early_x", [P, BANK * PACK], BF16, SEP_ROOM)
-        nc.gpsimd.tensor_scalar(
-            early_x[:].rearrange("p (j t) -> p j t", t=PACK), sep_halves[0][:].rearrange("p t j -> p j t"),
-            1.0, 0.0, ALU.mult, ALU.add,
-        )
-        late = placed("late", [P, PACK - 1, BANK], F32, LATE_ROOM)
-        for t in range(1, PACK):
-            gather_second(t, BANK, late[:, t - 1, :])
-        early_w = held("early_w", [P, BANK], U32)
-        early_s = held("early_s", [P, BANK], U8)
-        quantise(early_w[:], early_s[:], early_x[:])
+        late = {0: first_late}
         for k in range(PER_BANK):
-            separations[k] = (early_w[:, k * CHUNK : (k + 1) * CHUNK], early_s[:, k * CHUNK : (k + 1) * CHUNK])
+            grouped = placed("early_x%d" % k, [P, CHUNK * PACK], BF16, EARLY_ROOM + STAGGER * (k + 1))
+            interleave_on_gpsimd(grouped, sep_halves[0][:, :, k * CHUNK : (k + 1) * CHUNK])
+            late[1 + k] = placed("late%d" % (1 + k), [P, BANK], F32, LATE_ROOM + 1024 if k == 0 else EARLY_ROOM)
+            gather_second(1 + k, BANK, late[1 + k][:])
+            x_w = held("x_w%d" % k, [P, CHUNK], U32)
+            x_s = held("x_s%d" % k, [P, CHUNK], U8)
+            quantise(x_w[:], x_s[:], grouped[:])
+            separations[k] = (x_w[:], x_s[:])
+        late[3] = placed("late3", [P, BANK], F32, EARLY_ROOM + STAGGER * 3)
+        gather_second(3, BANK, late[3][:])
         quantise_ws(1)
-        gather_first(0, BANK, first_late[:])
-        for t in range(1, PACK):
-            gather_first(t, BANK, late[:, t - 1, :])
+        for t in range(PACK - 1):
+            gather_first(t, BANK, late[t][:])
 
-        def quantise_pair(half, grouped, words, scales):
-            quantise(words[:], scales[:], grouped[:])
-            for u in range(PER_BANK):
-                cols = slice(u * CHUNK, (u + 1) * CHUNK)
-                separations[half * PER_BANK + u] = (words[:, cols], scales[:, cols])
-
-        late_x = held("late_x", [P, BANK * PACK], BF16)
-        nc.gpsimd.tensor_scalar(
-            late_x[:].rearrange("p (j t) -> p j t", t=PACK), sep_halves[1][:].rearrange("p t j -> p j t"),
-            1.0, 0.0, ALU.mult, ALU.add,
-        )
-        species_response(1, 1, [0])
-        for a in both:
-            separation_response(0, [a])
+        rings["scalar"] = in_turn([banks[i] for i in (2, 3, 0, 1, 0, 1, 2, 3, 0, 1, 2, 3, 0, 1, 4, 5, 6, 7, 0, 1, 3, 2, 0, 1)])
+        def finish_pass(k, a):
             for b in range(BLOCKS):
-                turn_squares(0, b, a, 1)
+                soften(k, b, a)
+                turn_back(k, b, a)
+                form_unit(k, b, a)
+
         open_interaction(0)
-        for a in both:
-            for b in range(BLOCKS):
-                soften(0, b, a)
-                turn_back(0, b, a)
-                form_unit(0, b, a)
-            if a == 0:
-                species_response(1, 1, [1])
-        quantise_pair(1, late_x, placed("late_w", [P, BANK], U32, H_ROOM), held("late_s", [P, BANK], U8))
+        separation_response(0, [0])
+        for b in range(BLOCKS):
+            turn_squares(0, b, 0, 1)
+        species_response(1, 1, [0, 1])
+        for b in range(BLOCKS):
+            soften(0, b, 0)
+            turn_back(0, b, 0)
+        separation_response(0, [1])
+        for b in range(BLOCKS):
+            turn_squares(0, b, 1, 1)
+        gather_first(PACK - 1, BANK, late[PACK - 1][:])
+        for b in range(BLOCKS):
+            form_unit(0, b, 0)
+        separation_response(1, [0])
+        rings["vector"] = in_turn([banks[i] for i in (2, 3, 2, 4, 5, 3, 5, 0, 1, 6, 7, 3, 5)])
+        rings["sums"] = in_turn([banks[i] for i in (6, 7, 4, 2)])
+        finish_pass(0, 1)
+        add_squares(1, 0)
+        interleave_separation(2, nc.scalar.copy)
+        quantise_separation(2)
+        separation_response(1, [1])
+        add_squares(1, 1)
         quantise_chunk(0)
-        for a in both:
-            separation_response(1, [a])
-            add_squares(1, a)
-        species_response(1, 1, [2, 3])
-        rings["scalar"] = in_turn([banks[i] for i in (4, 5, 6, 7, 0, 1, 2, 3, 4, 5, 2, 3)])
-        rings["vector"] = in_turn([banks[i] for i in (6, 7, 6, 7, 6, 7, 6, 2, 3, 7, 0, 1, 4)])
-        rings["sums"] = in_turn([banks[i] for i in (0, 1, 4, 5)])
+        interleave_separation(LAST, nc.scalar.copy)
+        quantise_separation(LAST)
         open_interaction(1)
-        for a in both:
-            separation_response(2, [a])
-            add_squares(2, a)
-            soften_in_place(1, a)
-            if a == 1:
-                store_forces(0, 0, CHUNK, [0])
-            form_pass(1, a)
-        store_forces(0, 0, CHUNK, [1])
+        soften_in_place(1, 0)
+        form_pass(1, 0)
+        separation_response(2, [0])
+        add_squares(2, 0)
+        soften_in_place(1, 1)
+        form_pass(1, 1)
+        store_forces(0, 0, CHUNK, [0])
         quantise_chunk(1)
+        species_response(1, 1, [2, 3])
+        separation_response(2, [1])
+        add_squares(2, 1)
+        store_forces(0, 0, CHUNK, [1])
         store_forces(0, 0, CHUNK, [2])
-        open_interaction(2)
         for unit in last[:2]:
             turned_species_response(*unit)
             turn_squares(LAST, *unit, 0)
         for unit in last[:2]:
             turned_separation_response(*unit)
             turn_squares(LAST, *unit, 1)
-        soften_in_place(2, 0)
-        form_pass(2, 0)
         store_forces(1, 0, CHUNK, [0, 1])
+        open_interaction(2)
+        for a in both:
+            soften_in_place(2, a)
+            form_pass(2, a)
         for unit in last[2:]:
             turned_species_response(*unit)
             turn_squares(LAST, *unit, 0)
-        soften_in_place(2, 1)
-        form_pass(2, 1)
-        for unit in last[2:]:
-            turned_separation_response(*unit)
-            turn_squares(LAST, *unit, 1)
         store_forces(1, 0, CHUNK, [2])
         quantise_chunk(2)
+        for unit in last[2:]:
+            turned_separation_response(*unit)
+            turn_squares(LAST, *unit, 1)
         open_interaction(LAST)
         for b in range(BLOCKS):
             for a in both:

@@ -32,13 +32,12 @@ PER_COLUMN = 16
 RUN = 2
 WS_PIECES = 2
 WC_SCALE_ROOM = 0
-LATE_ROOM = 2048
-C_ROOM = 8192
-TABLE_ROOM = 24576
-FIRST_C_ROOM = 32768
-SEP_ROOM = 40960
-EARLY_ROOM = 49152
-STAGGER = 1984
+C_ROOM = 2048
+TABLE_ROOM = 18432
+FIRST_C_ROOM = 26624
+LATE_ROOM = 34816
+SUM_ROOM = LATE_ROOM + 64
+H_ROOM = SUM_ROOM + 4096
 
 
 def tile_list_grain_sheath_forces_kernel(
@@ -88,19 +87,19 @@ def tile_list_grain_sheath_forces_kernel(
             ws_raw[1, i] = placed("ws_raw1_%d" % i, [P, PACK, piece], F32, C_ROOM + 4096 * (1 + i))
         ws_grouped = [
             held("ws_grouped0", [P, PACK, P, PACK], BF16),
-            placed("ws_grouped1", [P, PACK, P, PACK], BF16, SEP_ROOM + 4096),
+            placed("ws_grouped1", [P, PACK, P, PACK], BF16, LATE_ROOM + 1024),
         ]
         ws_w = [placed("ws_w%d" % a, [P, PASS], U32, TABLE_ROOM + 4 * PASS * a) for a in range(H_PASSES)]
         ws_s = [held("ws_s%d" % a, [P, PASS], U8) for a in range(H_PASSES)]
         gains = held("gains", [P, H_PASSES, PACK], F32)
-        sep_halves = [held("sep0", [P, PACK, BANK], F32), placed("sep1", [P, PACK, BANK], F32, SEP_ROOM)]
-        second_room = in_turn([placed("second%d" % i, [P, BANK], F32, LATE_ROOM + 2048 * i) for i in range(2)])
+        sep_halves = [held("sep%d" % h, [P, PACK, BANK], F32) for h in range(CHUNKS // PER_BANK)]
+        second_room = in_turn([held("second%d" % i, [P, BANK], F32) for i in range(2)])
         d_room = in_turn([held("d_sq%d" % i, [P, PACK, CHUNK], F32) for i in range(4)])
         softs = [held("soft%d" % i, [P, BANK], F32) for i in range(4)]
         soft_room = in_turn(softs)
         x_room = in_turn([held("x_grouped%d" % u, [P, CHUNK * PACK], BF16) for u in range(2)])
         h_rooms = [held("h_grouped%d" % i, [P, H_PASSES * CHUNK * PACK], BF16) for i in range(2)]
-        first_h = placed("h_first", [P, H_PASSES * CHUNK * PACK], BF16, EARLY_ROOM + STAGGER * 3 + 64)
+        first_h = placed("h_first", [P, H_PASSES * CHUNK * PACK], BF16, H_ROOM)
         h_grouped = in_turn([first_h] + h_rooms)
         h_words = in_turn([held("h_w%d" % i, [P, H_PASSES * CHUNK], U32) for i in range(2)])
         h_scales = in_turn([held("h_s%d" % i, [P, H_PASSES * CHUNK], U8) for i in range(2)])
@@ -202,6 +201,8 @@ def tile_list_grain_sheath_forces_kernel(
         separations = {}
         d_squares = {}
         d_slices = {}
+        totals = {}
+        sum_room = placed("sum_room", [P, PACK, CHUNK], F32, SUM_ROOM)
         softening = {}
         sums = {}
         rooms_h = {}
@@ -231,13 +232,6 @@ def tile_list_grain_sheath_forces_kernel(
             count = second.shape[1]
             target = sep_halves[first // BANK][:, t, first % BANK : first % BANK + count]
             nc.vector.tensor_tensor(target, planes[t][:].indirect(idx_a[:, entries(first, count)]), second, ALU.subtract)
-
-        def interleave_on_gpsimd(grouped, source):
-            nc.gpsimd.tensor_scalar(
-                grouped[:].rearrange("p (j t) -> p j t", t=PACK),
-                source.rearrange("p t j -> p j t"),
-                1.0, 0.0, ALU.mult, ALU.add,
-            )
 
         def gather(jobs):
             for job in jobs:
@@ -381,9 +375,14 @@ def tile_list_grain_sheath_forces_kernel(
             total = c_squares[k, a][:, first:, :]
             nc.vector.tensor_tensor(total, total, d_squares[k, a][:, first:, :], ALU.add)
 
+        def add_squares_in_room(engine, k, a, slices):
+            totals[k, a] = sum_room[:]
+            engine.tensor_tensor(sum_room[:, slices, :], c_squares[k, a][:, slices, :], d_squares[k, a][:, slices, :], ALU.add)
+
         def soften_in_place(k, a):
-            nc.scalar.activation(c_squares[k, a], c_squares[k, a], ACT.Abs_reciprocal_sqrt, bias=1.0)
-            softening[k, a] = c_squares[k, a]
+            total = totals.get((k, a), c_squares[k, a])
+            nc.scalar.activation(total, total, ACT.Abs_reciprocal_sqrt, bias=1.0)
+            softening[k, a] = total
 
         def turn_back(k, b, a):
             back = sums[k, b, a]
@@ -462,42 +461,30 @@ def tile_list_grain_sheath_forces_kernel(
             round_ws(1, i)
         open_c_room(1, 0)
         species_response(1, 0, every)
-        first_late = held("late0", [P, BANK], F32)
-        room = second_room()
-        gather_second(0, 0, room[:])
-        gather_second(0, BANK, first_late[:])
-        gather_first(0, 0, room[:])
+        gather([(0, half * BANK, second_room()[:]) for half in range(2)])
         for t in range(1, PACK):
             room = second_room()
             gather([(t, u * CHUNK, room[:, u * CHUNK : (u + 1) * CHUNK]) for u in range(PER_BANK)])
-        late = {0: first_late}
         for k in range(PER_BANK):
-            grouped = placed("early_x%d" % k, [P, CHUNK * PACK], BF16, EARLY_ROOM + STAGGER * (k + 1))
-            interleave_on_gpsimd(grouped, sep_halves[0][:, :, k * CHUNK : (k + 1) * CHUNK])
-            late[1 + k] = placed("late%d" % (1 + k), [P, BANK], F32, LATE_ROOM + 1024 if k == 0 else EARLY_ROOM)
-            gather_second(1 + k, BANK, late[1 + k][:])
-            x_w = held("x_w%d" % k, [P, CHUNK], U32)
-            x_s = held("x_s%d" % k, [P, CHUNK], U8)
-            quantise(x_w[:], x_s[:], grouped[:])
-            separations[k] = (x_w[:], x_s[:])
-        late[3] = placed("late3", [P, BANK], F32, EARLY_ROOM + STAGGER * 3)
-        gather_second(3, BANK, late[3][:])
+            interleave_separation(k, nc.vector.tensor_copy)
+        for k in range(PER_BANK):
+            quantise_separation(k)
         quantise_ws(1)
-        for t in range(PACK - 1):
+        late = {t: placed("late%d" % t, [P, BANK], F32, LATE_ROOM + 2048 * (t - 1)) for t in range(1, PACK)}
+        for t in late:
+            gather_second(t, BANK, late[t][:])
+        for t in range(1, PACK - 1):
             gather_first(t, BANK, late[t][:])
 
-        rings["scalar"] = in_turn([banks[i] for i in (2, 3, 0, 1, 0, 1, 2, 3, 0, 1, 2, 3, 0, 1, 4, 5, 6, 7, 0, 1, 3, 2, 0, 1)])
-        def finish_pass(k, a):
-            for b in range(BLOCKS):
-                soften(k, b, a)
-                turn_back(k, b, a)
-                form_unit(k, b, a)
-
+        rings["scalar"] = in_turn([banks[i] for i in (0, 2, 3, 1, 0, 1, 2, 3, 2, 0, 1, 2, 3, 0, 4, 5, 6, 7, 0, 1, 3, 2, 0, 1)])
+        rings["vector"] = in_turn([banks[i] for i in (2, 3, 2, 4, 5, 3, 5, 0, 1, 6, 7, 3, 5)])
+        whole = slice(0, PACK)
         open_interaction(0)
+        species_response(1, 1, [0])
         separation_response(0, [0])
         for b in range(BLOCKS):
             turn_squares(0, b, 0, 1)
-        species_response(1, 1, [0, 1])
+        species_response(1, 1, [1])
         for b in range(BLOCKS):
             soften(0, b, 0)
             turn_back(0, b, 0)
@@ -505,18 +492,20 @@ def tile_list_grain_sheath_forces_kernel(
         for b in range(BLOCKS):
             turn_squares(0, b, 1, 1)
         gather_first(PACK - 1, BANK, late[PACK - 1][:])
-        for b in range(BLOCKS):
-            form_unit(0, b, 0)
         separation_response(1, [0])
-        rings["vector"] = in_turn([banks[i] for i in (2, 3, 2, 4, 5, 3, 5, 0, 1, 6, 7, 3, 5)])
+        add_squares_in_room(nc.gpsimd, 1, 0, whole)
+        for b in range(BLOCKS):
+            soften(0, b, 1)
+            turn_back(0, b, 1)
+        for unit in units(0):
+            form_unit(0, *unit)
         rings["sums"] = in_turn([banks[i] for i in (6, 7, 4, 2)])
-        finish_pass(0, 1)
-        add_squares(1, 0)
+        species_response(1, 1, [2])
         interleave_separation(2, nc.scalar.copy)
+        quantise_chunk(0)
         quantise_separation(2)
         separation_response(1, [1])
         add_squares(1, 1)
-        quantise_chunk(0)
         interleave_separation(LAST, nc.scalar.copy)
         quantise_separation(LAST)
         open_interaction(1)
@@ -528,7 +517,7 @@ def tile_list_grain_sheath_forces_kernel(
         form_pass(1, 1)
         store_forces(0, 0, CHUNK, [0])
         quantise_chunk(1)
-        species_response(1, 1, [2, 3])
+        species_response(1, 1, [3])
         separation_response(2, [1])
         add_squares(2, 1)
         store_forces(0, 0, CHUNK, [1])

@@ -457,6 +457,7 @@ def tile_list_grain_sheath_forces_kernel(
             species_response(0, a, every)
         for unit in units(0):
             turn_squares(0, *unit, 0)
+        species_response(1, 1, [0, 1])
         for i in range(WS_PIECES):
             round_ws(1, i)
         open_c_room(1, 0)
@@ -476,15 +477,14 @@ def tile_list_grain_sheath_forces_kernel(
         for t in range(1, PACK - 1):
             gather_first(t, BANK, late[t][:])
 
-        rings["scalar"] = in_turn([banks[i] for i in (0, 2, 3, 1, 0, 1, 2, 3, 2, 0, 1, 2, 3, 0, 4, 5, 6, 7, 0, 1, 3, 2, 0, 1)])
+        rings["scalar"] = in_turn([banks[i] for i in (2, 3, 0, 1, 0, 2, 3, 2, 0, 1, 2, 3, 4, 5, 6, 7, 0, 1, 3, 2, 0, 1)])
         rings["vector"] = in_turn([banks[i] for i in (2, 3, 2, 4, 5, 3, 5, 0, 1, 6, 7, 3, 5)])
         whole = slice(0, PACK)
         open_interaction(0)
-        species_response(1, 1, [0])
         separation_response(0, [0])
         for b in range(BLOCKS):
             turn_squares(0, b, 0, 1)
-        species_response(1, 1, [1])
+        species_response(1, 1, [2])
         for b in range(BLOCKS):
             soften(0, b, 0)
             turn_back(0, b, 0)
@@ -500,7 +500,7 @@ def tile_list_grain_sheath_forces_kernel(
         for unit in units(0):
             form_unit(0, *unit)
         rings["sums"] = in_turn([banks[i] for i in (6, 7, 4, 2)])
-        species_response(1, 1, [2])
+        species_response(1, 1, [3])
         interleave_separation(2, nc.scalar.copy)
         quantise_chunk(0)
         quantise_separation(2)
@@ -517,7 +517,6 @@ def tile_list_grain_sheath_forces_kernel(
         form_pass(1, 1)
         store_forces(0, 0, CHUNK, [0])
         quantise_chunk(1)
-        species_response(1, 1, [3])
         separation_response(2, [1])
         add_squares(2, 1)
         store_forces(0, 0, CHUNK, [1])

@@ -154,10 +154,10 @@ def tile_list_grain_sheath_forces_kernel(
         load_scale_rows(wc_s_raw, wc_scales[0])
         for i in range(WS_PIECES):
             load_ws(0, i)
-        nc.sync.dma_start(gains[:], gain.rearrange("(a p t) -> p a t", p=P, t=PACK))
         load_plane(0)
         nc.sync.dma_start(idx_b[:], offs3)
         nc.sync.dma_start(idx_a[:], offs2)
+        nc.sync.dma_start(gains[:], gain.rearrange("(a p t) -> p a t", p=P, t=PACK))
         for t in range(1, PACK):
             load_plane(t)
         for i in range(WS_PIECES):

@@ -36,6 +36,7 @@ C_ROOM = 2048
 TABLE_ROOM = 18432
 FIRST_C_ROOM = 26624
 LATE_ROOM = 34816
+WARM = 3
 SUM_ROOM = LATE_ROOM + 64
 H_ROOM = SUM_ROOM + 4096
 
@@ -66,7 +67,6 @@ def tile_list_grain_sheath_forces_kernel(
             return take
 
         banks = [psum.tile([P, BANK], F32, name="bank%d" % i) for i in range(8)]
-        rings = {"scalar": in_turn(banks[:4]), "sums": in_turn(banks[4:])}
 
         idx_tab = keep.tile([P, S // PER_COLUMN], U16, name="idx_tab")
         idx_a = keep.tile([P, S // PER_COLUMN], U16, name="idx_a")
@@ -258,12 +258,12 @@ def tile_list_grain_sheath_forces_kernel(
                 gained[half * PER_BANK + u, a] = scaled[:, u, :, :]
             c_rooms[half, a] = (squares, scaled)
 
-        def species_response(half, a, slices):
+        def species_response(half, a, slices, homes):
             v_w, v_s = species[half, "w"], species[half, "s"]
             squares, scaled = c_rooms[half, a]
             plain = PER_BANK - 1 if half == LAST // PER_BANK else PER_BANK
-            for t in slices:
-                bank = rings["scalar"]()
+            for t, home in zip(slices, homes):
+                bank = banks[home]
                 c = bank[:].rearrange("p (u j) -> p u j", u=PER_BANK)
                 col = a * PASS + t * P
                 nc.tensor.matmul_mx(
@@ -275,9 +275,9 @@ def tile_list_grain_sheath_forces_kernel(
                 nc.scalar.activation(squares[:, 0:plain, t, :], c[:, 0:plain, :], ACT.Square)
                 nc.scalar.activation(scaled[:, :, t, :], c, ACT.Copy, scale=gains[:, a, t : t + 1])
 
-        def turned_species_response(b, a):
+        def turned_species_response(b, a, home):
             v_w, v_s = species[LAST // PER_BANK, "w"], species[LAST // PER_BANK, "s"]
-            c = rings["scalar"]()
+            c = banks[home]
             col = (PER_BANK - 1) * CHUNK + b * P
             nc.tensor.matmul_mx(
                 out=c[:],
@@ -288,11 +288,11 @@ def tile_list_grain_sheath_forces_kernel(
             )
             nc.scalar.activation(turned(c_squares[LAST, a])[:, b, :], c[:], ACT.Square)
 
-        def turned_separation_response(b, a):
+        def turned_separation_response(b, a, home):
             x_w, x_s = separations[LAST]
             if b == 0:
                 d_squares[LAST, a] = d_room()[:]
-            d = rings["scalar"]()
+            d = banks[home]
             nc.tensor.matmul_mx(
                 out=d[:],
                 lhsT=x_w[:, b * P : (b + 1) * P].bitcast(FP8X4), lhsT_scale=x_s[:, b * P : (b + 1) * P],
@@ -301,26 +301,26 @@ def tile_list_grain_sheath_forces_kernel(
             )
             nc.scalar.activation(turned(d_squares[LAST, a])[:, b, :], d[:], ACT.Square)
 
-        def separation_response(k, passes):
+        def separation_response(k, a, homes):
             x_w, x_s = separations[k]
-            for a in passes:
-                d_squares[k, a] = d_room()[:]
-                for t0 in range(0, PACK, PER_BANK):
-                    d = rings["scalar"]()[:].rearrange("p (u j) -> p u j", u=PER_BANK)
-                    for u in range(PER_BANK):
-                        col = (t0 + u) * P
-                        nc.tensor.matmul_mx(
-                            out=d[:, u, :],
-                            lhsT=ws_w[a][:, col : col + P].bitcast(FP8X4), lhsT_scale=ws_s[a][:, col : col + P],
-                            rhs=x_w.bitcast(FP8X4), rhs_scale=x_s,
-                            start=True, stop=True,
-                        )
-                    room = d_squares[k, a][:, t0 : t0 + PER_BANK, :]
-                    if (k, a, t0) == (0, 1, 0):
-                        room = sep_halves[1][:, PACK - 1, :].rearrange("p (u j) -> p u j", u=PER_BANK)
-                    for u in range(PER_BANK):
-                        d_slices[k, a, t0 + u] = room[:, u, :]
-                    nc.scalar.activation(room, d, ACT.Square)
+            d_squares[k, a] = d_room()[:]
+            for t0, home in zip(range(0, PACK, PER_BANK), homes):
+                d = banks[home][:].rearrange("p (u j) -> p u j", u=PER_BANK)
+                repeats = [0] * WARM if (k, a, t0) == (1, 1, 2) else []
+                for u in repeats + list(range(PER_BANK)):
+                    col = (t0 + u) * P
+                    nc.tensor.matmul_mx(
+                        out=d[:, u, :],
+                        lhsT=ws_w[a][:, col : col + P].bitcast(FP8X4), lhsT_scale=ws_s[a][:, col : col + P],
+                        rhs=x_w.bitcast(FP8X4), rhs_scale=x_s,
+                        start=True, stop=True,
+                    )
+                room = d_squares[k, a][:, t0 : t0 + PER_BANK, :]
+                if (k, a, t0) == (0, 1, 0):
+                    room = sep_halves[1][:, PACK - 1, :].rearrange("p (u j) -> p u j", u=PER_BANK)
+                for u in range(PER_BANK):
+                    d_slices[k, a, t0 + u] = room[:, u, :]
+                nc.scalar.activation(room, d, ACT.Square)
 
         def interleave_separation(k, copy):
             grouped_x[k] = x_room()[:]
@@ -342,14 +342,9 @@ def tile_list_grain_sheath_forces_kernel(
                 return [(b, a) for b in range(BLOCKS) for a in range(H_PASSES)]
             return [(b, a) for a in range(H_PASSES) for b in range(BLOCKS)]
 
-        def units(k):
-            if k == LAST:
-                return [(b, a) for b in range(BLOCKS) for a in range(H_PASSES)]
-            return [(b, a) for a in range(H_PASSES) for b in range(BLOCKS)]
-
-        def turn_squares(k, b, a, term):
+        def turn_squares(k, b, a, term, home=None):
             if term == 0:
-                sums[k, b, a] = rings["sums"]()
+                sums[k, b, a] = banks[home]
             squares = (c_squares, d_squares)[term][k, a]
             for t in range(PACK):
                 if k == LAST:
@@ -371,9 +366,9 @@ def tile_list_grain_sheath_forces_kernel(
             nc.scalar.activation(soft[:], sums[k, b, a][:], ACT.Abs_reciprocal_sqrt, bias=1.0)
             softening[k, b, a] = soft[:].rearrange("p (t j) -> p t j", t=PACK)
 
-        def add_squares(k, a, first=0):
-            total = c_squares[k, a][:, first:, :]
-            nc.vector.tensor_tensor(total, total, d_squares[k, a][:, first:, :], ALU.add)
+        def add_squares(k, a):
+            total = c_squares[k, a]
+            nc.vector.tensor_tensor(total, total, d_squares[k, a], ALU.add)
 
         def add_squares_in_room(engine, k, a, slices):
             totals[k, a] = sum_room[:]
@@ -423,10 +418,11 @@ def tile_list_grain_sheath_forces_kernel(
                 cols = slice(b * CHUNK + a * P, b * CHUNK + (a + 1) * P)
                 interactions[LAST, b * P, a] = (words[:, cols], scales[:, cols])
 
-        def store_forces(k, first, width, parts):
+        def store_forces(k, first, width, parts, homes):
             tiles = N_TILES // 2 if k == LAST else BANK // width
-            for m0 in [part * tiles for part in parts]:
-                y = rings["vector"]()[:, 0 : tiles * width].rearrange("p (u j) -> p u j", j=width)
+            for part, home in zip(parts, homes):
+                m0 = part * tiles
+                y = banks[home][:, 0 : tiles * width].rearrange("p (u j) -> p u j", j=width)
                 for a in range(H_PASSES):
                     h_w, h_s = interactions[k, first, a]
                     for u in range(tiles):
@@ -444,7 +440,8 @@ def tile_list_grain_sheath_forces_kernel(
 
         every = range(PACK)
         both = range(H_PASSES)
-        last = units(LAST)
+        blocks = range(BLOCKS)
+        whole = slice(0, PACK)
         gather_species_scales()
         for half in range(CHUNKS // PER_BANK):
             gather_species_words(half)
@@ -454,14 +451,14 @@ def tile_list_grain_sheath_forces_kernel(
         for room in ((0, 0), (0, 1), (1, 1)):
             open_c_room(*room)
         for a in both:
-            species_response(0, a, every)
-        for unit in units(0):
-            turn_squares(0, *unit, 0)
-        species_response(1, 1, [0, 1])
+            species_response(0, a, every, every)
+        for i, unit in enumerate(units(0)):
+            turn_squares(0, *unit, 0, PACK + i)
+        species_response(1, 1, [0, 1], [0, 1])
         for i in range(WS_PIECES):
             round_ws(1, i)
         open_c_room(1, 0)
-        species_response(1, 0, every)
+        species_response(1, 0, every, [2, 3, 0, 1])
         gather([(0, half * BANK, second_room()[:]) for half in range(2)])
         for t in range(1, PACK):
             room = second_room()
@@ -477,76 +474,71 @@ def tile_list_grain_sheath_forces_kernel(
         for t in range(1, PACK - 1):
             gather_first(t, BANK, late[t][:])
 
-        rings["scalar"] = in_turn([banks[i] for i in (2, 3, 0, 1, 0, 2, 3, 2, 0, 1, 2, 3, 4, 5, 6, 7, 0, 1, 3, 2, 0, 1)])
-        rings["vector"] = in_turn([banks[i] for i in (2, 3, 2, 4, 5, 3, 5, 0, 1, 6, 7, 3, 5)])
-        whole = slice(0, PACK)
         open_interaction(0)
-        separation_response(0, [0])
-        for b in range(BLOCKS):
+        separation_response(0, 0, [2, 3])
+        for b in blocks:
             turn_squares(0, b, 0, 1)
-        species_response(1, 1, [2])
-        for b in range(BLOCKS):
+        species_response(1, 1, [2], [0])
+        for b in blocks:
             soften(0, b, 0)
             turn_back(0, b, 0)
-        separation_response(0, [1])
-        for b in range(BLOCKS):
+        separation_response(0, 1, [1, 0])
+        for b in blocks:
             turn_squares(0, b, 1, 1)
         gather_first(PACK - 1, BANK, late[PACK - 1][:])
-        separation_response(1, [0])
+        separation_response(1, 0, [2, 3])
         add_squares_in_room(nc.gpsimd, 1, 0, whole)
-        for b in range(BLOCKS):
+        for b in blocks:
             soften(0, b, 1)
             turn_back(0, b, 1)
         for unit in units(0):
             form_unit(0, *unit)
-        rings["sums"] = in_turn([banks[i] for i in (6, 7, 4, 2)])
-        species_response(1, 1, [3])
+        species_response(1, 1, [3], [2])
         interleave_separation(2, nc.scalar.copy)
         quantise_chunk(0)
         quantise_separation(2)
-        separation_response(1, [1])
+        separation_response(1, 1, [0, 1])
         add_squares(1, 1)
         interleave_separation(LAST, nc.scalar.copy)
         quantise_separation(LAST)
         open_interaction(1)
         soften_in_place(1, 0)
         form_pass(1, 0)
-        separation_response(2, [0])
+        separation_response(2, 0, [2, 3])
         add_squares(2, 0)
         soften_in_place(1, 1)
         form_pass(1, 1)
-        store_forces(0, 0, CHUNK, [0])
+        store_forces(0, 0, CHUNK, [0], [2])
         quantise_chunk(1)
-        separation_response(2, [1])
+        separation_response(2, 1, [4, 5])
         add_squares(2, 1)
-        store_forces(0, 0, CHUNK, [1])
-        store_forces(0, 0, CHUNK, [2])
-        for unit in last[:2]:
-            turned_species_response(*unit)
-            turn_squares(LAST, *unit, 0)
-        for unit in last[:2]:
-            turned_separation_response(*unit)
-            turn_squares(LAST, *unit, 1)
-        store_forces(1, 0, CHUNK, [0, 1])
+        store_forces(0, 0, CHUNK, [1, 2], [3, 2])
+        for a in both:
+            turned_species_response(0, a, 6 + a)
+            turn_squares(LAST, 0, a, 0, 6 + a)
+        for a in both:
+            turned_separation_response(0, a, a)
+            turn_squares(LAST, 0, a, 1)
+        store_forces(1, 0, CHUNK, [0, 1], [4, 5])
         open_interaction(2)
         for a in both:
             soften_in_place(2, a)
             form_pass(2, a)
-        for unit in last[2:]:
-            turned_species_response(*unit)
-            turn_squares(LAST, *unit, 0)
-        store_forces(1, 0, CHUNK, [2])
+        for a in both:
+            turned_species_response(1, a, (3, 2)[a])
+            turn_squares(LAST, 1, a, 0, (4, 2)[a])
+        store_forces(1, 0, CHUNK, [2], [3])
         quantise_chunk(2)
-        for unit in last[2:]:
-            turned_separation_response(*unit)
-            turn_squares(LAST, *unit, 1)
+        for a in both:
+            turned_separation_response(1, a, a)
+            turn_squares(LAST, 1, a, 1)
         open_interaction(LAST)
-        for b in range(BLOCKS):
+        for b in blocks:
             for a in both:
                 soften(LAST, b, a)
                 form_unit(LAST, b, a)
-            store_forces(2, 0, CHUNK, [b])
+            store_forces(2, 0, CHUNK, [b], [(5, 0)[b]])
             quantise_block(b)
-        store_forces(2, 0, CHUNK, [2])
-        for b in range(BLOCKS):
-            store_forces(LAST, b * P, P, [0, 1])
+        store_forces(2, 0, CHUNK, [2], [1])
+        store_forces(LAST, 0, P, [0, 1], [6, 7])
+        store_forces(LAST, P, P, [0, 1], [3, 5])

@@ -29,7 +29,7 @@ LAST = CHUNKS - 1
 BLOCKS = CHUNK // P
 N_TILES = N // P
 PER_COLUMN = 16
-RUN = 2
+RUN = 4
 WS_PIECES = 2
 WC_SCALE_ROOM = 0
 C_ROOM = 2048

@@ -37,8 +37,8 @@ TABLE_ROOM = 18432
 FIRST_C_ROOM = 26624
 LATE_ROOM = 34816
 WARM = 3
-SUM_ROOM = LATE_ROOM + 64
-H_ROOM = SUM_ROOM + 4096
+H_ROOM = LATE_ROOM + 64
+SUM_ROOM = H_ROOM + 4096
 
 
 def tile_list_grain_sheath_forces_kernel(
@@ -202,7 +202,9 @@ def tile_list_grain_sheath_forces_kernel(
         d_squares = {}
         d_slices = {}
         totals = {}
-        sum_room = placed("sum_room", [P, PACK, CHUNK], F32, SUM_ROOM)
+        sum_rooms = placed("sum_rooms", [P, 2 * PACK - 1, CHUNK], F32, SUM_ROOM)
+        sum_room = sum_rooms[:, 0:PACK, :]
+        shared_sum = held("shared_sum", [P, PACK + PER_BANK, CHUNK], F32)
         softening = {}
         sums = {}
         rooms_h = {}
@@ -303,7 +305,7 @@ def tile_list_grain_sheath_forces_kernel(
 
         def separation_response(k, a, homes):
             x_w, x_s = separations[k]
-            d_squares[k, a] = d_room()[:]
+            d_squares[k, a] = shared_sum[:, PER_BANK:, :] if (k, a) == (2, 1) else d_room()[:]
             for t0, home in zip(range(0, PACK, PER_BANK), homes):
                 d = banks[home][:].rearrange("p (u j) -> p u j", u=PER_BANK)
                 repeats = [0] * WARM if (k, a, t0) == (1, 1, 2) else []
@@ -369,6 +371,16 @@ def tile_list_grain_sheath_forces_kernel(
         def add_squares(k, a):
             total = c_squares[k, a]
             nc.vector.tensor_tensor(total, total, d_squares[k, a], ALU.add)
+
+        def add_squares_shared(k, a):
+            totals[k, a] = shared_sum[:, 0:PACK, :]
+            for engine, part in ((nc.vector, slice(0, PER_BANK)), (nc.gpsimd, slice(PER_BANK, PACK))):
+                engine.tensor_tensor(totals[k, a][:, part, :], c_squares[k, a][:, part, :], d_squares[k, a][:, part, :], ALU.add)
+
+        def add_squares_mostly(k, a):
+            totals[k, a] = sum_rooms[:, PACK - 1 :, :]
+            for engine, part in ((nc.vector, slice(1, PACK)), (nc.gpsimd, slice(0, 1))):
+                engine.tensor_tensor(totals[k, a][:, part, :], c_squares[k, a][:, part, :], d_squares[k, a][:, part, :], ALU.add)
 
         def add_squares_in_room(engine, k, a, slices):
             totals[k, a] = sum_room[:]
@@ -505,40 +517,44 @@ def tile_list_grain_sheath_forces_kernel(
         soften_in_place(1, 0)
         form_pass(1, 0)
         separation_response(2, 0, [2, 3])
-        add_squares(2, 0)
+        add_squares_mostly(2, 0)
         soften_in_place(1, 1)
         form_pass(1, 1)
         store_forces(0, 0, CHUNK, [0], [2])
-        quantise_chunk(1)
         separation_response(2, 1, [4, 5])
-        add_squares(2, 1)
+        add_squares_shared(2, 1)
+        quantise_chunk(1)
         store_forces(0, 0, CHUNK, [1, 2], [3, 2])
         for a in both:
             turned_species_response(0, a, 6 + a)
             turn_squares(LAST, 0, a, 0, 6 + a)
+        open_interaction(2)
+        soften_in_place(2, 0)
+        form_pass(2, 0)
         for a in both:
             turned_separation_response(0, a, a)
             turn_squares(LAST, 0, a, 1)
         store_forces(1, 0, CHUNK, [0, 1], [4, 5])
-        open_interaction(2)
-        for a in both:
-            soften_in_place(2, a)
-            form_pass(2, a)
+        soften_in_place(2, 1)
+        form_pass(2, 1)
+        store_forces(1, 0, CHUNK, [2], [0])
+        quantise_chunk(2)
         for a in both:
             turned_species_response(1, a, (3, 2)[a])
             turn_squares(LAST, 1, a, 0, (4, 2)[a])
-        store_forces(1, 0, CHUNK, [2], [3])
-        quantise_chunk(2)
-        for a in both:
-            turned_separation_response(1, a, a)
-            turn_squares(LAST, 1, a, 1)
         open_interaction(LAST)
-        for b in blocks:
-            for a in both:
-                soften(LAST, b, a)
-                form_unit(LAST, b, a)
-            store_forces(2, 0, CHUNK, [b], [(5, 0)[b]])
-            quantise_block(b)
-        store_forces(2, 0, CHUNK, [2], [1])
-        store_forces(LAST, 0, P, [0, 1], [6, 7])
-        store_forces(LAST, P, P, [0, 1], [3, 5])
+        for a in both:
+            soften(LAST, 0, a)
+            form_unit(LAST, 0, a)
+            turned_separation_response(1, a, (1, 5)[a])
+            turn_squares(LAST, 1, a, 1)
+        store_forces(2, 0, CHUNK, [0], [1])
+        quantise_block(0)
+        for a in both:
+            soften(LAST, 1, a)
+            form_unit(LAST, 1, a)
+        store_forces(2, 0, CHUNK, [1], [5])
+        quantise_block(1)
+        store_forces(2, 0, CHUNK, [2], [7])
+        store_forces(LAST, 0, P, [0, 1], [6, 3])
+        store_forces(LAST, P, P, [0, 1], [0, 1])

from contextlib import ExitStack

import concourse.mybir as mybir
from concourse.masks import make_identity

K, H, N, T, S = 512, 1024, 768, 2048, 1024
FLOPS = 2 * S * (2 * K * H + H * N)

F32 = mybir.dt.float32
BF16 = mybir.dt.bfloat16
I32 = mybir.dt.int32
U32 = mybir.dt.uint32
U16 = mybir.dt.uint16
U8 = mybir.dt.uint8
FP8X4 = mybir.dt.float8_e4m3fn_x4
FP4X4 = mybir.dt.float4_e2m1fn_x4
ACT = mybir.ActivationFunctionType
ALU = mybir.AluOpType

P = 128
PACK = 4
PASS = P * PACK
H_PASSES = H // PASS
BANK = 512
CHUNK = 256
CHUNKS = S // CHUNK
PER_BANK = BANK // CHUNK
LAST = CHUNKS - 1
BLOCKS = CHUNK // P
N_TILES = N // P
PER_COLUMN = 16
RUN = 4
WS_PIECES = 2
WC_SCALE_ROOM = 0
C_ROOM = 2048
TABLE_ROOM = 18432
FIRST_C_ROOM = 26624
LATE_ROOM = 34816
WARM = 3
H_ROOM = LATE_ROOM + 64
SUM_ROOM = H_ROOM + 4096


def tile_list_grain_sheath_forces_kernel(
    tc, tab_words, tab_scales, xT, offs, offs2, offs3, wc_words, wc_scales,
    ws, gain, wf_words, wf_scales, drag, out,
):
    nc = tc.nc
    with ExitStack() as ctx:
        keep = ctx.enter_context(tc.tile_pool(name="keep", bufs=1))
        shared = ctx.enter_context(tc.tile_pool(name="shared", bufs=1))
        psum = ctx.enter_context(tc.psum_pool(name="psum", bufs=1))

        def held(name, shape, dtype):
            return keep.tile(shape, dtype, name=name, align_bytes=64)

        def placed(name, shape, dtype, at):
            return shared.tile(shape, dtype, name=name, offset=at, align_bytes=64)

        def in_turn(tiles):
            handed = []

            def take():
                handed.append(None)
                return tiles[(len(handed) - 1) % len(tiles)]

            return take

        banks = [psum.tile([P, BANK], F32, name="bank%d" % i) for i in range(8)]

        idx_tab = keep.tile([P, S // PER_COLUMN], U16, name="idx_tab")
        idx_a = keep.tile([P, S // PER_COLUMN], U16, name="idx_a")
        idx_b = keep.tile([P, S // PER_COLUMN], U16, name="idx_b")
        tab_w = placed("tab_w", [P, T], U32, TABLE_ROOM)
        tab_s = held("tab_s", [P, T], U8)
        wc_w_raw = held("wc_w_raw", [P, 2 * H], U8)
        wc_s_raw = placed("wc_s_raw", [P, H], U8, WC_SCALE_ROOM)
        wc_w = held("wc_w", [P, 2 * H], U8)
        wc_s = held("wc_s", [P, H], U8)
        wf_w = held("wf_w", [P, H_PASSES, N], U32)
        wf_s = held("wf_s", [P, H_PASSES, N], U8)
        planes = [held("plane%d" % t, [P, T], F32) for t in range(PACK)]
        piece = PASS // WS_PIECES
        ws_raw = {}
        for i in range(WS_PIECES):
            ws_raw[0, i] = placed("ws_raw0_%d" % i, [P, PACK, piece], F32, FIRST_C_ROOM + 4096 * i)
            ws_raw[1, i] = placed("ws_raw1_%d" % i, [P, PACK, piece], F32, C_ROOM + 4096 * (1 + i))
        ws_grouped = [
            held("ws_grouped0", [P, PACK, P, PACK], BF16),
            placed("ws_grouped1", [P, PACK, P, PACK], BF16, LATE_ROOM + 1024),
        ]
        ws_w = [placed("ws_w%d" % a, [P, PASS], U32, TABLE_ROOM + 4 * PASS * a) for a in range(H_PASSES)]
        ws_s = [held("ws_s%d" % a, [P, PASS], U8) for a in range(H_PASSES)]
        gains = held("gains", [P, H_PASSES, PACK], F32)
        sep_halves = [held("sep%d" % h, [P, PACK, BANK], F32) for h in range(CHUNKS // PER_BANK)]
        second_room = in_turn([held("second%d" % i, [P, BANK], F32) for i in range(2)])
        d_room = in_turn([held("d_sq%d" % i, [P, PACK, CHUNK], F32) for i in range(4)])
        softs = [held("soft%d" % i, [P, BANK], F32) for i in range(4)]
        soft_room = in_turn(softs)
        x_room = in_turn([held("x_grouped%d" % u, [P, CHUNK * PACK], BF16) for u in range(2)])
        h_rooms = [held("h_grouped%d" % i, [P, H_PASSES * CHUNK * PACK], BF16) for i in range(2)]
        first_h = placed("h_first", [P, H_PASSES * CHUNK * PACK], BF16, H_ROOM)
        h_grouped = in_turn([first_h] + h_rooms)
        h_words = in_turn([held("h_w%d" % i, [P, H_PASSES * CHUNK], U32) for i in range(2)])
        h_scales = in_turn([held("h_s%d" % i, [P, H_PASSES * CHUNK], U8) for i in range(2)])
        drag_room = [held("forces%d" % k, [P, N_TILES * CHUNK], F32)[:] for k in range(CHUNKS)]

        def pieces(k):
            width = P if k == LAST else CHUNK
            return [(first, width) for first in range(0, CHUNK, width)]

        def forces(k, first, width):
            if k == LAST:
                room = drag_room[k][:, N_TILES * first : N_TILES * (first + width)]
            else:
                room = drag_room[k]
            return room.rearrange("p (m j) -> p m j", j=width)

        def load_scale_rows(plane, rows):
            for q in range(4):
                nc.sync.dma_start(plane[32 * q : 32 * q + 4, :].bitcast(I32), rows[4 * q : 4 * q + 4, :].bitcast(I32))

        nc.gpsimd.memset(tab_s[:].bitcast(I32), 0)
        nc.gpsimd.memset(wc_s_raw[:].bitcast(I32), 0)

        warm = held("warm", [P, 2], F32)
        nc.gpsimd.memset(warm[:, 0:1], 1.0)
        nc.scalar.activation(warm[:, 1:2], warm[:, 0:1], ACT.Abs_reciprocal_sqrt)
        ident = held("ident", [P, P], F32)
        make_identity(nc, ident[:])
        nc.gpsimd.memset(wf_s[:].rearrange("p a n -> p (a n)").bitcast(I32), 0)

        x_rows = xT.rearrange("(p t) c -> p t c", t=PACK)
        ws_rows = ws.rearrange("(p t) c -> p t c", t=PACK)
        drag_rows = drag.rearrange("(m p) j -> p m j", p=P)
        out_rows = out.rearrange("(m p) j -> p m j", p=P)

        def load_plane(t):
            nc.sync.dma_start(planes[t][:], x_rows[:, t, :])

        def load_ws(a, i):
            col = a * PASS + i * piece
            nc.sync.dma_start(ws_raw[a, i][:], ws_rows[:, :, col : col + piece])

        def load_drag(k):
            for first, width in pieces(k):
                col = k * CHUNK + first
                nc.sync.dma_start(forces(k, first, width), drag_rows[:, :, col : col + width])

        nc.sync.dma_start(idx_tab[:], offs)
        load_scale_rows(tab_s, tab_scales[0])
        nc.sync.dma_start(wc_w_raw[:], wc_words[0])
        nc.sync.dma_start(tab_w[:].bitcast(I32), tab_words[0].rearrange("p n t -> p (n t)").bitcast(I32))
        load_scale_rows(wc_s_raw, wc_scales[0])
        for i in range(WS_PIECES):
            load_ws(0, i)
        load_plane(0)
        nc.sync.dma_start(idx_b[:], offs3)
        nc.sync.dma_start(idx_a[:], offs2)
        nc.sync.dma_start(gains[:], gain.rearrange("(a p t) -> p a t", p=P, t=PACK))
        for t in range(1, PACK):
            load_plane(t)
        for i in range(WS_PIECES):
            load_ws(1, i)
        nc.sync.dma_start(wf_w[:].bitcast(I32), wf_words.rearrange("a p n t -> p a (n t)").bitcast(I32))
        for q in range(4):
            nc.sync.dma_start(
                wf_s[32 * q : 32 * q + 4, :, :].bitcast(I32),
                wf_scales[:, 4 * q : 4 * q + 4, :].rearrange("a r n -> r a n").bitcast(I32),
            )
        for k in range(CHUNKS):
            load_drag(k)

        nc.vector.tensor_copy(
            wc_w[:].bitcast(U16).rearrange("p (a t m) -> p a t m", a=H_PASSES, t=PACK),
            wc_w_raw[:].bitcast(U16).rearrange("p (a m t) -> p a t m", a=H_PASSES, t=PACK),
        )
        nc.vector.tensor_copy(
            wc_s[:].rearrange("p (a t m) -> p a t m", a=H_PASSES, t=PACK),
            wc_s_raw[:].rearrange("p (a m t) -> p a t m", a=H_PASSES, t=PACK),
        )

        def quantise(words, scales, grouped):
            nc.vector.quantize_mx(out=words.bitcast(FP8X4), scales=scales, in_=grouped)

        def round_ws(a, i):
            rows = piece // PACK
            target = ws_grouped[a][:, :, i * rows : (i + 1) * rows, :].rearrange("p t (g i) j -> p g j i t", i=2)
            source = ws_raw[a, i][:].rearrange("p j (g i t) -> p g j i t", i=2, t=PACK)
            for t0 in range(0, PACK, 2):
                nc.scalar.copy(target[:, :, :, :, t0 : t0 + 2], source[:, :, :, :, t0 : t0 + 2])

        def quantise_ws(a):
            quantise(ws_w[a][:], ws_s[a][:], ws_grouped[a][:].rearrange("p t m j -> p (t m j)"))

        species = {}
        grouped_x = {}
        c_rooms = {}
        c_squares = {}
        gained = {}
        separations = {}
        d_squares = {}
        d_slices = {}
        totals = {}
        sum_rooms = placed("sum_rooms", [P, 2 * PACK - 1, CHUNK], F32, SUM_ROOM)
        sum_room = sum_rooms[:, 0:PACK, :]
        shared_sum = held("shared_sum", [P, PACK + PER_BANK, CHUNK], F32)
        softening = {}
        sums = {}
        rooms_h = {}
        interactions = {}

        def entries(first, count):
            return slice(first // PER_COLUMN, (first + count) // PER_COLUMN)

        def gather_species_scales():
            v_s = held("v_s", [P, S], U8)
            nc.vector.tensor_copy(v_s[:], tab_s[:].indirect(idx_tab[:]))
            for half in range(CHUNKS // PER_BANK):
                species[half, "s"] = v_s[:, half * BANK : (half + 1) * BANK]

        def gather_species_words(half):
            if half == 0:
                v_w = held("v_w0", [P, BANK], U32)
            else:
                v_w = placed("v_w1", [P, BANK], U32, WC_SCALE_ROOM)
            nc.vector.tensor_copy(v_w[:], tab_w[:].indirect(idx_tab[:, entries(half * BANK, BANK)]))
            species[half, "w"] = v_w

        def gather_second(t, first, second):
            nc.vector.tensor_copy(second, planes[t][:].indirect(idx_b[:, entries(first, second.shape[1])]))

        def gather_first(t, first, second):
            count = second.shape[1]
            target = sep_halves[first // BANK][:, t, first % BANK : first % BANK + count]
            nc.vector.tensor_tensor(target, planes[t][:].indirect(idx_a[:, entries(first, count)]), second, ALU.subtract)

        def gather(jobs):
            for job in jobs:
                gather_second(*job)
            for job in jobs:
                gather_first(*job)

        def turned(tile):
            return tile.rearrange("p t j -> p (t j)").rearrange("p (b r) -> p b r", r=PASS)

        def open_c_room(half, a):
            shape = [P, PER_BANK, PACK, CHUNK]
            if (half, a) == (1, 0):
                squares = placed("c_sq1_0", shape, F32, C_ROOM)
                scaled = placed("gained1_0", shape, F32, C_ROOM + 8192)
            elif (half, a) == (0, 0):
                squares = placed("c_sq0_0", shape, F32, FIRST_C_ROOM)
                scaled = held("gained0_0", shape, F32)
            else:
                squares = held("c_sq%d_%d" % (half, a), shape, F32)
                scaled = held("gained%d_%d" % (half, a), shape, F32)
            for u in range(PER_BANK):
                c_squares[half * PER_BANK + u, a] = squares[:, u, :, :]
                gained[half * PER_BANK + u, a] = scaled[:, u, :, :]
            c_rooms[half, a] = (squares, scaled)

        def species_response(half, a, slices, homes):
            v_w, v_s = species[half, "w"], species[half, "s"]
            squares, scaled = c_rooms[half, a]
            plain = PER_BANK - 1 if half == LAST // PER_BANK else PER_BANK
            for t, home in zip(slices, homes):
                bank = banks[home]
                c = bank[:].rearrange("p (u j) -> p u j", u=PER_BANK)
                col = a * PASS + t * P
                nc.tensor.matmul_mx(
                    out=bank[:],
                    lhsT=wc_w[:, 2 * col : 2 * (col + P)].bitcast(FP4X4), lhsT_scale=wc_s[:, col : col + P],
                    rhs=v_w[:].bitcast(FP8X4), rhs_scale=v_s,
                    start=True, stop=True,
                )
                nc.scalar.activation(squares[:, 0:plain, t, :], c[:, 0:plain, :], ACT.Square)
                nc.scalar.activation(scaled[:, :, t, :], c, ACT.Copy, scale=gains[:, a, t : t + 1])

        def turned_species_response(b, a, home):
            v_w, v_s = species[LAST // PER_BANK, "w"], species[LAST // PER_BANK, "s"]
            c = banks[home]
            col = (PER_BANK - 1) * CHUNK + b * P
            nc.tensor.matmul_mx(
                out=c[:],
                lhsT=v_w[:, col : col + P].bitcast(FP8X4), lhsT_scale=v_s[:, col : col + P],
                rhs=wc_w[:, 2 * a * PASS : 2 * (a + 1) * PASS].bitcast(FP4X4),
                rhs_scale=wc_s[:, a * PASS : (a + 1) * PASS],
                start=True, stop=True,
            )
            nc.scalar.activation(turned(c_squares[LAST, a])[:, b, :], c[:], ACT.Square)

        def turned_separation_response(b, a, home):
            x_w, x_s = separations[LAST]
            if b == 0:
                d_squares[LAST, a] = d_room()[:]
            d = banks[home]
            nc.tensor.matmul_mx(
                out=d[:],
                lhsT=x_w[:, b * P : (b + 1) * P].bitcast(FP8X4), lhsT_scale=x_s[:, b * P : (b + 1) * P],
                rhs=ws_w[a][:].bitcast(FP8X4), rhs_scale=ws_s[a][:],
                start=True, stop=True,
            )
            nc.scalar.activation(turned(d_squares[LAST, a])[:, b, :], d[:], ACT.Square)

        def separation_response(k, a, homes):
            x_w, x_s = separations[k]
            d_squares[k, a] = shared_sum[:, PER_BANK:, :] if (k, a) == (2, 1) else d_room()[:]
            for t0, home in zip(range(0, PACK, PER_BANK), homes):
                d = banks[home][:].rearrange("p (u j) -> p u j", u=PER_BANK)
                repeats = [0] * WARM if (k, a, t0) == (1, 1, 2) else []
                for u in repeats + list(range(PER_BANK)):
                    col = (t0 + u) * P
                    nc.tensor.matmul_mx(
                        out=d[:, u, :],
                        lhsT=ws_w[a][:, col : col + P].bitcast(FP8X4), lhsT_scale=ws_s[a][:, col : col + P],
                        rhs=x_w.bitcast(FP8X4), rhs_scale=x_s,
                        start=True, stop=True,
                    )
                room = d_squares[k, a][:, t0 : t0 + PER_BANK, :]
                if (k, a, t0) == (0, 1, 0):
                    room = sep_halves[1][:, PACK - 1, :].rearrange("p (u j) -> p u j", u=PER_BANK)
                for u in range(PER_BANK):
                    d_slices[k, a, t0 + u] = room[:, u, :]
                nc.scalar.activation(room, d, ACT.Square)

        def interleave_separation(k, copy):
            grouped_x[k] = x_room()[:]
            u = k % PER_BANK
            source = sep_halves[k // PER_BANK][:, :, u * CHUNK : (u + 1) * CHUNK]
            copy(
                grouped_x[k].rearrange("p (g i t) -> p g t i", i=RUN, t=PACK),
                source.rearrange("p t (g i) -> p g t i", i=RUN),
            )

        def quantise_separation(k):
            x_w = held("x_w%d" % k, [P, CHUNK], U32)
            x_s = held("x_s%d" % k, [P, CHUNK], U8)
            quantise(x_w[:], x_s[:], grouped_x[k])
            separations[k] = (x_w[:], x_s[:])

        def units(k):
            if k == LAST:
                return [(b, a) for b in range(BLOCKS) for a in range(H_PASSES)]
            return [(b, a) for a in range(H_PASSES) for b in range(BLOCKS)]

        def turn_squares(k, b, a, term, home=None):
            if term == 0:
                sums[k, b, a] = banks[home]
            squares = (c_squares, d_squares)[term][k, a]
            for t in range(PACK):
                if k == LAST:
                    square = turned(squares)[:, b, t * P : (t + 1) * P]
                elif term == 0:
                    square = squares[:, t, b * P : (b + 1) * P]
                else:
                    square = d_slices[k, a, t][:, b * P : (b + 1) * P]
                nc.tensor.matmul(
                    sums[k, b, a][:, t * P : (t + 1) * P], square, ident[:],
                    start=(term == 0 and t == 0), stop=(term == 1 and t == PACK - 1), is_transpose=True,
                )

        def open_interaction(k):
            rooms_h[k] = (h_grouped(), h_words(), h_scales())

        def soften(k, b, a):
            soft = soft_room()
            nc.scalar.activation(soft[:], sums[k, b, a][:], ACT.Abs_reciprocal_sqrt, bias=1.0)
            softening[k, b, a] = soft[:].rearrange("p (t j) -> p t j", t=PACK)

        def add_squares(k, a):
            total = c_squares[k, a]
            nc.vector.tensor_tensor(total, total, d_squares[k, a], ALU.add)

        def add_squares_shared(k, a):
            totals[k, a] = shared_sum[:, 0:PACK, :]
            for engine, part in ((nc.vector, slice(0, PER_BANK)), (nc.gpsimd, slice(PER_BANK, PACK))):
                engine.tensor_tensor(totals[k, a][:, part, :], c_squares[k, a][:, part, :], d_squares[k, a][:, part, :], ALU.add)

        def add_squares_mostly(k, a):
            totals[k, a] = sum_rooms[:, PACK - 1 :, :]
            for engine, part in ((nc.vector, slice(1, PACK)), (nc.gpsimd, slice(0, 1))):
                engine.tensor_tensor(totals[k, a][:, part, :], c_squares[k, a][:, part, :], d_squares[k, a][:, part, :], ALU.add)

        def add_squares_in_room(engine, k, a, slices):
            totals[k, a] = sum_room[:]
            engine.tensor_tensor(sum_room[:, slices, :], c_squares[k, a][:, slices, :], d_squares[k, a][:, slices, :], ALU.add)

        def soften_in_place(k, a):
            total = totals.get((k, a), c_squares[k, a])
            nc.scalar.activation(total, total, ACT.Abs_reciprocal_sqrt, bias=1.0)
            softening[k, a] = total

        def turn_back(k, b, a):
            back = sums[k, b, a]
            for t in range(PACK):
                cols = slice(t * P, (t + 1) * P)
                nc.tensor.transpose(back[:, cols], softening[k, b, a][:, t, :], ident[:])
            softening[k, b, a] = back[:].rearrange("p (t j) -> p t j", t=PACK)

        def form_interaction(target, soft, scaled):
            nc.vector.tensor_tensor(
                target.rearrange("p (g i t) -> p g t i", i=RUN, t=PACK),
                soft.rearrange("p t (g i) -> p g t i", i=RUN),
                scaled.rearrange("p t (g i) -> p g t i", i=RUN),
                ALU.mult,
            )

        def form_pass(k, a):
            room = rooms_h[k][0][:, a * CHUNK * PACK : (a + 1) * CHUNK * PACK]
            form_interaction(room, softening[k, a], gained[k, a])

        def form_unit(k, b, a):
            first = (units(k).index((b, a))) * P
            room = rooms_h[k][0][:, first * PACK : (first + P) * PACK]
            form_interaction(room, softening[k, b, a], gained[k, a][:, :, b * P : (b + 1) * P])

        def quantise_chunk(k):
            grouped, words, scales = rooms_h[k]
            quantise(words[:], scales[:], grouped[:])
            for a in range(H_PASSES):
                cols = slice(a * CHUNK, (a + 1) * CHUNK)
                interactions[k, 0, a] = (words[:, cols], scales[:, cols])

        def quantise_block(b):
            grouped, words, scales = rooms_h[LAST]
            cols = slice(b * CHUNK, (b + 1) * CHUNK)
            quantise(words[:, cols], scales[:, cols], grouped[:, b * CHUNK * PACK : (b + 1) * CHUNK * PACK])
            for a in range(H_PASSES):
                cols = slice(b * CHUNK + a * P, b * CHUNK + (a + 1) * P)
                interactions[LAST, b * P, a] = (words[:, cols], scales[:, cols])

        def store_forces(k, first, width, parts, homes):
            tiles = N_TILES // 2 if k == LAST else BANK // width
            for part, home in zip(parts, homes):
                m0 = part * tiles
                y = banks[home][:, 0 : tiles * width].rearrange("p (u j) -> p u j", j=width)
                for a in range(H_PASSES):
                    h_w, h_s = interactions[k, first, a]
                    for u in range(tiles):
                        col = (m0 + u) * P
                        nc.tensor.matmul_mx(
                            out=y[:, u, :],
                            lhsT=wf_w[:, a, col : col + P].bitcast(FP8X4), lhsT_scale=wf_s[:, a, col : col + P],
                            rhs=h_w.bitcast(FP8X4), rhs_scale=h_s,
                            start=(a == 0 and u == 0), stop=(a == H_PASSES - 1 and u == tiles - 1),
                        )
                rows = forces(k, first, width)[:, m0 : m0 + tiles, :]
                nc.vector.tensor_tensor(rows, y, rows, ALU.add)
                col = k * CHUNK + first
                nc.sync.dma_start(out_rows[:, m0 : m0 + tiles, col : col + width], rows)

        every = range(PACK)
        both = range(H_PASSES)
        blocks = range(BLOCKS)
        whole = slice(0, PACK)
        gather_species_scales()
        for half in range(CHUNKS // PER_BANK):
            gather_species_words(half)
        for i in range(WS_PIECES):
            round_ws(0, i)
        quantise_ws(0)
        for room in ((0, 0), (0, 1), (1, 1)):
            open_c_room(*room)
        for a in both:
            species_response(0, a, every, every)
        for i, unit in enumerate(units(0)):
            turn_squares(0, *unit, 0, PACK + i)
        species_response(1, 1, [0, 1], [0, 1])
        for i in range(WS_PIECES):
            round_ws(1, i)
        open_c_room(1, 0)
        species_response(1, 0, every, [2, 3, 0, 1])
        gather([(0, half * BANK, second_room()[:]) for half in range(2)])
        for t in range(1, PACK):
            room = second_room()
            gather([(t, u * CHUNK, room[:, u * CHUNK : (u + 1) * CHUNK]) for u in range(PER_BANK)])
        for k in range(PER_BANK):
            interleave_separation(k, nc.vector.tensor_copy)
        for k in range(PER_BANK):
            quantise_separation(k)
        quantise_ws(1)
        late = {t: placed("late%d" % t, [P, BANK], F32, LATE_ROOM + 2048 * (t - 1)) for t in range(1, PACK)}
        for t in late:
            gather_second(t, BANK, late[t][:])
        for t in range(1, PACK - 1):
            gather_first(t, BANK, late[t][:])

        open_interaction(0)
        separation_response(0, 0, [2, 3])
        for b in blocks:
            turn_squares(0, b, 0, 1)
        species_response(1, 1, [2], [0])
        for b in blocks:
            soften(0, b, 0)
            turn_back(0, b, 0)
        separation_response(0, 1, [1, 0])
        for b in blocks:
            turn_squares(0, b, 1, 1)
        gather_first(PACK - 1, BANK, late[PACK - 1][:])
        separation_response(1, 0, [2, 3])
        add_squares_in_room(nc.gpsimd, 1, 0, whole)
        for b in blocks:
            soften(0, b, 1)
            turn_back(0, b, 1)
        for unit in units(0):
            form_unit(0, *unit)
        species_response(1, 1, [3], [2])
        interleave_separation(2, nc.scalar.copy)
        quantise_chunk(0)
        quantise_separation(2)
        separation_response(1, 1, [0, 1])
        add_squares(1, 1)
        interleave_separation(LAST, nc.scalar.copy)
        quantise_separation(LAST)
        open_interaction(1)
        soften_in_place(1, 0)
        form_pass(1, 0)
        separation_response(2, 0, [2, 3])
        add_squares_mostly(2, 0)
        soften_in_place(1, 1)
        form_pass(1, 1)
        store_forces(0, 0, CHUNK, [0], [2])
        separation_response(2, 1, [4, 5])
        add_squares_shared(2, 1)
        quantise_chunk(1)
        store_forces(0, 0, CHUNK, [1, 2], [3, 2])
        for a in both:
            turned_species_response(0, a, 6 + a)
            turn_squares(LAST, 0, a, 0, 6 + a)
        open_interaction(2)
        soften_in_place(2, 0)
        form_pass(2, 0)
        for a in both:
            turned_separation_response(0, a, a)
            turn_squares(LAST, 0, a, 1)
        store_forces(1, 0, CHUNK, [0, 1], [4, 5])
        soften_in_place(2, 1)
        form_pass(2, 1)
        store_forces(1, 0, CHUNK, [2], [0])
        quantise_chunk(2)
        for a in both:
            turned_species_response(1, a, (3, 2)[a])
            turn_squares(LAST, 1, a, 0, (4, 2)[a])
        open_interaction(LAST)
        for a in both:
            soften(LAST, 0, a)
            form_unit(LAST, 0, a)
            turned_separation_response(1, a, (1, 5)[a])
            turn_squares(LAST, 1, a, 1)
        store_forces(2, 0, CHUNK, [0], [1])
        quantise_block(0)
        for a in both:
            soften(LAST, 1, a)
            form_unit(LAST, 1, a)
        store_forces(2, 0, CHUNK, [1], [5])
        quantise_block(1)
        store_forces(2, 0, CHUNK, [2], [7])
        store_forces(LAST, 0, P, [0, 1], [6, 3])
        store_forces(LAST, P, P, [0, 1], [0, 1])
